import numpy as np, ml_dtypes
CORES = [16,18,20,22]
N = 4
import mx_ref
BF = ml_dtypes.bfloat16
def entries(a):
    return np.ascontiguousarray(a.T).reshape(-1)
def table(e):
    return np.ascontiguousarray(np.reshape(e, (-1, 16)).T).astype(np.int32)
def pick(q, e):
    c = np.concatenate([q[0].reshape(128, -1, 4), np.zeros((128, 1, 4), np.uint8)], axis=1); s = np.concatenate([q[1], np.ones((16, 1), np.uint8)], axis=1)
    return (np.ascontiguousarray(c[:, e].reshape(128, -1)), np.ascontiguousarray(s[:, e]))
def join(*qs):
    return (np.concatenate([q[0] for q in qs], axis=1), np.concatenate([q[1] for q in qs], axis=1))
def put(q, e, v):
    c, s = q[0].reshape(128, -1, 4).copy(), q[1].copy(); c[:, e] = v[0].reshape(128, -1, 4); s[:, e] = v[1]
    return (c.reshape(128, -1), s)
def pk(c, s):
    return (np.ascontiguousarray(c), mx_ref.live(s))
def emit(q):
    return q[0], q[1]
def cols(t, e):
    v = np.concatenate([t.reshape(128, -1, 4), np.zeros((128, 1, 4), BF)], axis=1)
    return np.ascontiguousarray(v[:, e]).reshape(128, -1)
def cut(t, i, w=512):
    return t[:, w * i:w * i + w]
def f(rng, *shape):
    return mx_ref.flush((rng.standard_normal(shape, dtype=np.float32) * np.exp2(rng.integers(-2, 3, shape[:-1] + (1,)))).astype(BF))
def wide(rng, *shape, cols=0):
    v = rng.standard_normal(shape, dtype=np.float32) * np.exp2(rng.integers(-12, 13, shape)).astype(np.float32)
    if cols: v *= np.repeat(np.exp2(rng.integers(-cols, cols + 1, shape[:-2] + (1, shape[-1] // 4))) * (rng.random(shape[:-2] + (1, shape[-1] // 4)) > 0.0625), 4, axis=-1).astype(np.float32)
    return mx_ref.flush(v.astype(BF))
P, CAPP, LC = 256, 64, 192
def choose(e, g, d):
    c = e[np.arange(P), np.argmax(g[e], axis=1)]
    for s in range(N):
        if s != d:
            late = np.flatnonzero(c // P == s)[CAPP:]
            c[late] = e[late, 0]
    return c
def play(e0, e1, e2, p1, p2, u, a):
    k = [mx_ref.quantize(u[d]) for d in range(N)]
    A = [[mx_ref.quantize(np.ascontiguousarray(cut(a[d], i))) for i in range(4)] for d in range(N)]
    H = [mx_ref.quantize(e0[d]) for d in range(N)]
    g = np.stack([mx_ref.matmul(k[d], H[d])[0] for d in range(N)]) + np.float32(0)
    chosen, tiles, scores = [], [], [g]
    for e, p in ((e1, p1), (e2, p2)):
        every, before = join(*H), g.reshape(-1)
        H, g = [], np.zeros((N, P), np.float32)
        for d in range(N):
            c = choose(entries(p[d]).reshape(P, 4), before, d)
            x = pick(every, c)
            R = np.stack([mx_ref.matmul(A[d][i], x) for i in range(4)], axis=2).reshape(128, 4 * P)
            h = (R * np.float32(0.05) + e[d].astype(np.float32)).astype(BF)
            q = mx_ref.quantize(h)
            g[d] = before[c] + mx_ref.matmul(k[d], q)[0]
            H.append(q)
            chosen.append(c)
            tiles.append(h)
        scores.append(g)
    return np.stack(chosen).reshape(2, N, P), tiles, scores, H
def large(v):
    v = v.astype(np.float32)
    v[np.abs(v) < np.float32(0.03125)] = 0
    return v.astype(BF)
def lean(v, u, s):
    t = np.abs(v.astype(np.float32)).reshape(128, -1, 4) * np.sign(u[:, None, :4].astype(np.float32)) * np.asarray(s, np.float32)[None, :, None]
    return t.reshape(128, -1).astype(BF)
def near(t, u, score):
    size = np.concatenate([[0.0], np.exp2(np.arange(-26, -7))])[:, None] * np.array([1, 1.25, 1.5, 1.75])
    v = np.repeat(t.astype(np.float32).reshape(128, 1, 4), 80, axis=1)
    v[:8] = np.sign(u[:8, None, :4].astype(np.float32)) * size.reshape(1, 80, 1)
    v = np.ascontiguousarray(v.reshape(128, 320).astype(BF))
    s = score(v)
    i = int(np.argmin(np.abs(s - s[0] - np.float32(2.5) * np.spacing(np.abs(s[0])))))
    return cols(v, [0, i])
def strong(u):
    return (u.astype(np.float32) * np.float32(2.0 ** 24)).astype(BF)
def lists(rng):
    out = []
    for d in range(N):
        others = np.delete(np.arange(N), d)
        rank = others[np.argsort(rng.random((P, N - 1)), axis=1)[:, :3]]
        pool = np.stack([rng.permutation(P)[:LC] for s in range(N)])
        e = np.zeros((P, 4), int)
        e[:, 0] = d * P + rng.integers(0, P, P)
        e[:, 1:] = rank * P + pool[rank, rng.integers(0, LC, (P, 3))]
        out.append(table(e.reshape(-1)))
    return np.stack(out)
def crowd(rng, s):
    out, half = [], LC // 2
    for d in range(N):
        x = rng.permutation(np.delete(np.arange(N), d))
        hi = np.stack([rng.permutation(np.flatnonzero(s[r]))[:half] for r in range(N)])
        lo = np.stack([rng.permutation(np.flatnonzero(~s[r]))[:half] for r in range(N)])
        j = rng.permutation(P)
        one, two, home = j[:P // 2], j[P // 2:P // 2 + CAPP], j[P // 2 + CAPP:]
        rank = np.stack([np.full(P, x[0]), np.full(P, x[1]), x[rng.integers(2, N - 1, P)]], axis=1)
        n = rng.integers(0, half, (P, 3))
        n[j, 0] = np.arange(P) % (P // 2) % half
        n[two, 1] = rng.permutation(half)[:CAPP]
        at = lo[rank, n]
        at[one, 0] = hi[x[0], n[one, 0]]
        at[two, 1] = hi[x[1], n[two, 1]]
        e = np.zeros((P, 4), int)
        e[:, 0] = d * P + np.flatnonzero(~s[d])[rng.integers(0, P // 2, P)]
        e[home, 0] = d * P + np.flatnonzero(s[d])[rng.integers(0, P // 2, home.size)]
        e[:, 1:] = rng.permuted(rank * P + at, axis=1)
        out.append(table(e.reshape(-1)))
    return np.stack(out)
def plain(rng):
    u = np.array(f(rng, 128, 512))
    u[:, 4:] = 0
    return {"e0": np.array(f(rng, N, 128, 4 * P)), "e1": large(f(rng, N, 128, 4 * P)), "e2": large(f(rng, N, 128, 4 * P)), "p1": lists(rng), "p2": lists(rng),
            "u": np.stack([u] * N), "a": f(rng, N, 128, 2048), "w": f(rng, N, 128, 512)}
def setup_inputs(rng):
    return plain(rng)
def setup_inputs_full(rng):
    d = plain(rng)
    for e, p, size in (("e0", "p1", 1), ("e1", "p2", 64)):
        s = np.stack([rng.permutation(P) < P // 2 for r in range(N)])
        for r in range(N): d[e][r] = lean(d[e][r], d["u"][r], size * np.where(s[r], 1, -1))
        d[p] = crowd(rng, s)
    return d
def setup_inputs_ties(rng):
    d = plain(rng)
    u, a = np.ascontiguousarray(d["u"][0]), np.array(d["a"][0])
    a.reshape(128, 4, 512)[:, :, :32] = 0
    k = mx_ref.quantize(u)
    def row(t): return mx_ref.matmul(k, mx_ref.quantize(t))[0]
    x = np.concatenate([f(rng, 128, 16), near(lean(f(rng, 128, 4), u, [1]), u, row)], axis=1)
    best = cols(x, [5] * 4)
    top, q = row(best)[0], mx_ref.quantize(best)
    R = np.stack([mx_ref.matmul(mx_ref.quantize(np.ascontiguousarray(cut(a, i))), q)[:, 0] for i in range(4)], axis=1)
    def later(t): return top + row((np.tile(R, 80) * np.float32(0.05) + t.astype(np.float32)).astype(BF))
    z = near(lean(large(f(rng, 128, 4)), u, [8]), u, later)
    d["e0"] = np.stack([cols(x, rng.integers(0, 6, P)) for r in range(N)])
    d["e1"] = np.stack([cols(z, rng.integers(0, 2, P)) for r in range(N)])
    d["a"] = np.stack([a] * N)
    return d
def setup_inputs_own(rng):
    d = plain(rng)
    d["u"] = strong(d["u"])
    best, worst = rng.permutation(N)[:2]
    for r, s in ((best, 1), (worst, -1)):
        d["e0"][r] = lean(d["e0"][r], d["u"][r], np.full(P, 8 * s))
        d["e1"][r] = lean(d["e1"][r], d["u"][r], np.full(P, 256 * s))
    return d
def setup_inputs_flip(rng):
    d = plain(rng)
    d["u"] = strong(d["u"])
    for r in range(N):
        s = rng.permutation(P) % 2 * 2 - 1
        d["e0"][r] = lean(d["e0"][r], d["u"][r], 1024 * s)
        d["e1"][r] = lean(d["e1"][r], d["u"][r], -16384 * s)
    return d
def setup_inputs_spread(rng):
    d = plain(rng)
    d["e0"] = wide(rng, N, 128, 4 * P, cols=4)
    d["e1"] = large(wide(rng, N, 128, 4 * P, cols=4))
    d["e2"] = large(wide(rng, N, 128, 4 * P, cols=4))
    return d
def check_inputs(d):
    b = []
    for k in ("e0", "e1", "e2", "u", "a", "w"):
        v = np.abs(d[k].astype(np.float32))
        if not (np.isfinite(v).all() and ((v == 0) | (v >= 2.0 ** -30) & (v <= 2.0 ** 30)).all()): b.append("a value of " + k)
    u = d["u"].astype(np.float32)
    if (u[:, :, 4:] != 0).any(): b.append("u has numbers behind its column 0")
    if (u != u[:1]).any(): b.append("u isn't the same on all ranks")
    for k in ("p1", "p2"):
        for r in range(N):
            e = entries(d[k][r]).reshape(P, 4)
            if e.min() < 0 or e.max() >= N * P:
                b.append(k + " out of range")
                continue
            o = np.sort(e[:, 1:] // P, axis=1)
            if (e[:, 0] // P != r).any(): b.append(k + ": predecessor 0")
            if (o == r).any() or (o[:, 1:] == o[:, :-1]).any(): b.append(k + ": predecessors 1 to 3")
            if np.bincount(np.unique(e[:, 1:]) // P, minlength=N).max() > LC: b.append(k + ": too many columns of one rank")
    if not b:
        chosen, tiles, scores, H = play(*[d[k] for k in ("e0", "e1", "e2", "p1", "p2", "u", "a")])
        v = np.abs(np.stack(tiles).astype(np.float32))
        if not (np.isfinite(v).all() and ((v == 0) | (v >= 2.0 ** -30) & (v <= 2.0 ** 30)).all()): b.append("a value of h_1 or h_2")
        if not np.isfinite(np.stack(scores)).all(): b.append("a score")
    return b
def reference(e0, e1, e2, p1, p2, u, a, w):
    chosen, tiles, scores, H = play(e0, e1, e2, p1, p2, u, a)
    ch, g = np.zeros((N, 2, P), np.float32), np.zeros((N, 1, P), np.float32)
    oc, osc, y = np.zeros((N, 128, 4 * P), np.uint8), np.zeros((N, 16, P), np.uint8), np.zeros((N, 128, P), np.float32)
    for r in range(N):
        ch[r] = chosen[:, r]
        g[r, 0] = scores[2][r]
        oc[r], osc[r] = emit(H[r])
        y[r] = mx_ref.matmul(mx_ref.quantize(w[r]), H[r])
    return {"ch": ch, "g": g, "oc": oc, "osc": osc, "y": y}

@@ -1,0 +1,631 @@
+from concourse.bass import DstId, RemoteDMATransfer
+from concourse.mybir import dt, AluOpType as A, ActivationFunctionType as AF
+
+P, CAPP = 256, 64
+TINY = 2.0 ** -100
+STEP = 2.0 ** -24 * (1 + 2.0 ** -10)
+BIG = 1.5 * 2.0 ** 25
+WAIT, LEAST, ISSUE, WAY, ONCE = 0.13, 0.09, 0.8, 2.9, 1.5
+LOCAL, FIRST, LONG = 2.3, 3.8, 5.5
+F, B, I, H, C, S8 = "float32", "bfloat16", "int32", "uint16", "float8_e4m3fn_x4", "uint8"
+SCRATCH = {"PS": ("psum", [128, 4096], F)}
+PLACE = {"PS": ("PS", 0, 4096)}
+
+
+def _buf(dtype, **names):
+    for k, n in names.items():
+        SCRATCH[k] = ("sbuf", [128, n], dtype)
+        PLACE[k] = (k, 0, n)
+
+
+def _area(dtype, **names):
+    k = "W" + dtype
+    for name, n in names.items():
+        at = SCRATCH[k][1][1] if k in SCRATCH else 0
+        PLACE[name] = (k, at, n)
+        SCRATCH[k] = ("sbuf", [128, at + (n + 15) // 16 * 16], dtype)
+
+
+def _each(**names):
+    return {n + str(t): w for t in (1, 2) for n, w in names.items()}
+
+
+_buf(B, UT=512, E0=1024, AT=2048, WT=512, E1=1024, E2=1024, HT1=1024, HT2=1024)
+_buf(C, UQ=128, AQ=512, WQ=128, QO0=256, QO1=256, QO2=256, QW0=192, QW1=192, SQ1=192, SQ2=192)
+_buf(S8, UP=128, AP=512, WP=128, QS0=256, QS1=256, QS2=256, QP0=192, QP1=192, SS1=192, SS2=192)
+_buf(H, MSG1=8, MSG2=2, LM1=24, LM2=6, LS2=8, ST2=6, LC2=6, LU1=8, LU2=8)
+_buf(F, U1=32, U2=32, Z1=1792, Z2=1792, YB=256, S0=256, S1=256, S2=256, PR1=256, PR2=256, PB1=256, PB2=256)
+_buf(I, RAW1=64, RAW2=64)
+_area(H, DUP=8, PERM=2, PV=2)
+_area(I, PI=1, PJ=8, DUPI=8, PERMI=2, KC=8, KD=64)
+_area(F, ZERO=64, BAR=64, SEGT=40, KCOL=4, SL=4, XEO=8, GD=4, BC=4, TR=8, ZB=416, PF32=8, J4=64, SEG4=64, J16=128, MASK=128,
+      SEG16=128, SUF=32, J32=32, IDT=256, PKC=16, KF=64)
+_area(F, **_each(RL=64, T2=64, SCL=64, EQN=64, KQN=64, TK=64, SK=64, PK=16, LCN=8, OL=8, OB=8, CD=8, CG=8,
+                 VR=128, KK=32, G=128, SG=128, V4=32, AB=32, AC=32, DE=32, VA=32, BT=40, NI=64, RT=40, TJ=40, TA1=1, SFX=32,
+                 AA=8, W=6208, WD=128, TW=128, PF=16, M16=16, MM=8, EQ=32, KEY=32, K16=16, KM=8, TB2=32, EC2=32, SV=8,
+                 NW=8, NP=8, BP=8, VAL=24, BK=72, SA=24, SB=8, KS=8, CA=8, CO=8, CH=8, XC=8, A2=32, TA=32, XT=16, KQ=32, PP=32,
+                 P16=16, PA=8))
+_area(H, **_each(OF=8, PO=12, XO=16))
+NDMA = 60
+SEMAPHORES = ["qv", "qa", "qt", "qg", "m1", "lm1", "m2", "lm2", "m3", "lm3"] + ["d%d" % i for i in range(NDMA)] + [
+    x + str(t) for t in (1, 2) for x in ("v", "lv", "c", "lc", "s", "ls")]
+
+
+def rank_program(g, core, T, topo):
+    me = T.rank_of(core)
+    if me is None:
+        return
+    others = [(me + 1 + i) % 4 for i in range(3)]
+    slot_at = [(me - d) % 4 - 1 for d in others]
+    qs = {"v": g.vector, "a": g.scalar, "t": g.tensor, "g": g, "s": g.sync}
+    hist, know, cnt, total = {}, {q: {} for q in qs}, {}, {}
+    nodes, past, last, hold = [], {}, {}, [()]
+
+    def V(name, c0=0, c1=None, st=1, p0=0, p1=128):
+        return (name, p0, p1, c0, PLACE[name][2] if c1 is None else c1, st)
+
+    def blk(k, name, c0=0, c1=None, st=1):
+        return V(name, c0, c1, st, 32 * k, 32 * k + 32)
+
+    def ap(v):
+        name, o, _ = PLACE[v[0]]
+        return T[name][v[1]:v[2], o + v[3]:o + v[4]] if v[5] == 1 else T[name][v[1]:v[2], o + v[3]:o + v[4]:v[5]]
+
+    def width(v):
+        return (v[4] - v[3] + v[5] - 1) // v[5]
+
+    def clash(a, b):
+        if a[2] <= b[1] or b[2] <= a[1] or a[4] <= b[3] or b[4] <= a[3]:
+            return False
+        return not (a[5] == b[5] and a[5] > 1 and (a[3] - b[3]) % a[5])
+
+    def bank(v):
+        return (v[0], 0, 128, v[3] // 512 * 512, v[3] // 512 * 512 + 512, 1) if v[0] == "PS" else v
+
+    def regions(reads, writes):
+        return [(bank(v), False) for v in reads] + [(bank(v), True) for v in writes]
+
+    def push(opts, reads, writes, cost, dur=None, after=()):
+        i, deps = len(nodes), set(after)
+        for r, w in regions(reads, writes):
+            deps |= {j for (o, ow, j) in past.get(r[0], []) if (w or ow) and clash(r, o)}
+        for r, w in regions(reads, writes):
+            past.setdefault(r[0], []).append((r, w, i))
+        prev = list(hold[0]) + ([last["g"]] if "g" in opts and "g" in last else [])
+        if "g" in opts:
+            last["g"] = i
+        nodes.append({"opts": opts, "rd": reads, "wr": writes, "cost": cost, "dur": cost if dur is None else dur,
+                      "deps": deps - {i}, "prev": prev, "gate": [j for j in after]})
+        return i
+
+    def wait(q, evs):
+        need = {}
+        for sem, val, clock in evs:
+            if know[q].get(sem, 0) < val and need.get(sem, (0, 0))[0] < val:
+                need[sem] = (val, clock)
+        for sem in sorted(need):
+            val, clock = need[sem]
+            if know[q].get(sem, 0) >= val or any(o != sem and need[o][1].get(sem, 0) >= val for o in need):
+                continue
+            qs[q].wait_ge(T.sem[sem], val)
+        for sem in need:
+            for k, n in list(need[sem][1].items()) + [(sem, need[sem][0])]:
+                know[q][k] = max(know[q].get(k, 0), n)
+
+    def issue(node, q):
+        if q == "x":
+            return
+        evs = [nodes[j]["ev"] for j in node["gate"]]
+        for r, w in regions(node["rd"], node["wr"]):
+            evs += [ev for (o, ow, ev) in hist.get(r[0], []) if (w or ow) and clash(r, o)]
+        wait(q, evs)
+        kind, call = node["opts"][q]
+        if kind == "op":
+            sem, val = "q" + q, cnt.get(q, 0) + 1
+            cnt[q] = val
+            call().then_inc(T.sem[sem], 1)
+        elif kind == "dma":
+            sem, val = "d%d" % cnt.get("dma", 0), 16
+            cnt["dma"] = cnt.get("dma", 0) + 1
+            call().then_inc(T.sem[sem], 16)
+        else:
+            sem, val = call()
+        clock = dict(know[q])
+        clock[sem] = val
+        total[sem] = max(total.get(sem, 0), val)
+        node["ev"] = (sem, val, clock)
+        for r, w in regions(node["rd"], node["wr"]):
+            hist.setdefault(r[0], []).append((r, w, node["ev"]))
+
+    def lay():
+        n = len(nodes)
+        succ = [[] for _ in range(n)]
+        for i, nd in enumerate(nodes):
+            for j in nd["deps"]:
+                succ[j].append(i)
+        high = [0.0] * n
+        for i in range(n - 1, -1, -1):
+            high[i] = nodes[i]["dur"] + max([WAIT + high[j] for j in succ[i]] + [high[i]])
+            for p in nodes[i]["prev"]:
+                high[p] = max(high[p], nodes[p]["cost"] + high[i] - nodes[p]["dur"])
+        left = [len(nd["deps"]) for nd in nodes]
+        ready = {i for i in range(n) if left[i] == 0}
+        free, fin, done = {}, [0.0] * n, set()
+        while ready:
+            cand = []
+            for i in ready:
+                nd = nodes[i]
+                if any(p not in done for p in nd["prev"]):
+                    continue
+                s = max([fin[j] + WAIT for j in nd["deps"]] + [0.0])
+                start, q = min((max(s, free.get(q, 0.0)) if q != "x" else s, "vatgsx".index(q)) for q in nd["opts"])
+                cand.append((start, -high[i], i, "vatgsx"[q]))
+            first = min(cand)[0]
+            start, _, i, q = min((c for c in cand if c[0] <= first + 0.05), key=lambda c: c[1:])
+            issue(nodes[i], q)
+            free[q] = start + nodes[i]["cost"]
+            fin[i] = start + nodes[i]["dur"]
+            ready.discard(i)
+            done.add(i)
+            for j in succ[i]:
+                left[j] -= 1
+                if left[j] == 0:
+                    ready.add(j)
+
+    def us(cycles):
+        return max(LEAST, 0.02 + 0.001 * cycles)
+
+    def op(q, call, reads, writes, cycles):
+        return push({q: ("op", call)}, reads, writes, us(cycles))
+
+    def sv(s):
+        return ap(s) if isinstance(s, tuple) else s
+
+    def cols_of(*ss):
+        return [s for s in ss if isinstance(s, tuple)]
+
+    def tc(o, a):
+        op("v", lambda: g.vector.tensor_copy(ap(o), ap(a)), [a], [o], width(a))
+
+    def tt(o, a, b, f):
+        op("v", lambda: g.vector.tensor_tensor(ap(o), ap(a), ap(b), f), [a, b], [o], width(a) * (1 if a[0] == "PS" else 2))
+
+    def tti(o, w, off, b, f):
+        op("v", lambda: g.vector.tensor_tensor(ap(o), ap(w).indirect(ap(off)), ap(b), f), [w, off, b], [o], 50 + 1.5 * width(b))
+
+    def ts(o, a, s1, f1, s2=None, f2=None):
+        if f2 is None:
+            op("v", lambda: g.vector.tensor_scalar(ap(o), ap(a), sv(s1), None, f1), [a] + cols_of(s1), [o], width(a))
+        else:
+            op("v", lambda: g.vector.tensor_scalar(ap(o), ap(a), sv(s1), sv(s2), f1, f2), [a] + cols_of(s1, s2), [o], width(a))
+
+    def lin(o, a, scale=1.0, bias=0.0):
+        def on_v():
+            if scale == 1.0 and bias == 0.0:
+                return g.vector.tensor_copy(ap(o), ap(a))
+            if bias == 0.0:
+                return g.vector.tensor_scalar(ap(o), ap(a), sv(scale), None, A.mult)
+            if scale == 1.0:
+                return g.vector.tensor_scalar(ap(o), ap(a), sv(bias), None, A.add)
+            return g.vector.tensor_scalar(ap(o), ap(a), sv(scale), sv(bias), A.mult, A.add)
+
+        def on_a():
+            if bias == 0.0:
+                return g.scalar.activation(ap(o), ap(a), AF.Copy, scale=sv(scale))
+            return g.scalar.activation(ap(o), ap(a), AF.Identity, scale=sv(scale), bias=sv(bias))
+        push({"v": ("op", on_v), "a": ("op", on_a)}, [a] + cols_of(scale, bias), [o], us(width(a)))
+
+    def scan(o, a, b, f0=A.add, f1=A.add):
+        op("v", lambda: g.vector.tensor_tensor_scan(ap(o), ap(a), ap(b), 0.0, f0, f1), [a, b], [o], width(a))
+
+    def tr(o, a):
+        op("v", lambda: g.vector.transpose(ap(o), ap(a)), [a], [o], width(a))
+
+    def ms(o, c):
+        op("v", lambda: g.vector.memset(ap(o), c), [], [o], width(o))
+
+    def fill(o, base, step=0, rise=0, pattern=None):
+        n = width(o)
+        op("g", lambda: g.iota(ap(o), pattern or [[step, n]], base, rise, allow_small_or_imprecise_dtypes=True), [], [o], 130 + 2 * n)
+
+    def gat(o, w, off):
+        op("v", lambda: g.vector.tensor_copy(ap(o), ap(w).indirect(ap(off))), [w, off], [o], 50 + 1.5 * width(o))
+
+    def gata(o, w, off):
+        op("a", lambda: g.scalar.activation(ap(o), ap(w).indirect(ap(off)), AF.Copy), [w, off], [o], 70 + 1.5 * width(o))
+
+    def pick(qo, so, qw, sw, off):
+        op("v", lambda: g.vector.tensor_copy(ap(qo).bitcast(dt.uint32), ap(qw).bitcast(dt.uint32).indirect(ap(off))), [qw, off], [qo],
+           50 + 1.5 * width(qo))
+        gata(so, sw, off)
+
+    def qz(q, s, a):
+        return op("v", lambda: g.vector.quantize_mx(ap(q), ap(s), ap(a)), [a], [q, s], 0.25 * width(a))
+
+    def act(o, a, scale=1.0):
+        op("a", lambda: g.scalar.activation(ap(o), ap(a), AF.Copy, scale=scale), [a], [o], width(a))
+
+    def mm(b, n, wq, ws, xq, xs):
+        o = V("PS", 512 * b, 512 * b + n)
+        op("t", lambda: g.tensor.matmul_mx(ap(o), ap(wq), ap(ws), ap(xq), ap(xs), True, True), [wq, ws, xq, xs], [o], n + 16)
+        return o
+
+    def dma(q, out, in_, reads, writes, after=(), dur=LOCAL):
+        return push({q: ("dma", lambda: qs[q].dma_start(out, in_))}, reads, writes, 0.08, dur, after)
+
+    def load(q, v, src, dur, after=()):
+        return dma(q, ap(v), src, [], [v], after, dur)
+
+    def mask_of(engines):
+        return sum(1 << e for e in engines)
+
+    def dst(d):
+        rid, pid, _ = topo.addr(T.cores[d])
+        return DstId(rid=rid, pnc=pid)
+
+    def remote(transfers, src, lsem, count, sem, arrivals, landing):
+        def call():
+            g.remote_dma_fused(transfers, local_sem=T.sem[lsem])
+            return lsem, count
+        more = 0.0 if cnt.get("remote") else ONCE
+        cnt["remote"] = 1
+        i = push({"g": ("remote", call)}, [src], [], ISSUE + more, ISSUE + 0.5 + more)
+        push({"x": None}, [], [landing], 0.0, WAY - ISSUE - 0.5, [i])
+        total[sem] = arrivals
+        hist.setdefault(landing[0], []).append((landing, True, (sem, arrivals, {sem: arrivals})))
+        return i
+
+    def spread(src, land, sem, lsem, landing):
+        e = topo.engines(core, T.cores[others[0]])[:16]
+        return remote([RemoteDMATransfer(
+            dst_ids=[dst(d) for d in others], dma_engine_mask=mask_of(e), remote_sem=T.sem[sem], srcs=[ap(src)],
+            dsts=[ap(land(s)) for s in slot_at])], src, lsem, len(e), sem, 3 * len(e), landing)
+
+    def each(src, w, land, sem, lsem, turn=0):
+        trs = []
+        for i, d in enumerate(others):
+            e = topo.engines(core, T.cores[d])
+            j = 4 * ((i + turn) % 4)
+            a, z = V(src, w * i, w * i + w), V(land, w * slot_at[i], w * slot_at[i] + w)
+            code = SCRATCH[src][2] == C
+            trs.append(RemoteDMATransfer(
+                dst_ids=[dst(d)], dma_engine_mask=mask_of(e[j:j + 4]), remote_sem=T.sem[sem],
+                srcs=[ap(a).bitcast(dt.uint8) if code else ap(a)], dsts=[ap(z).bitcast(dt.uint8) if code else ap(z)]))
+        return remote(trs, V(src), lsem, 12, sem, 12, V(land))
+
+    def zb(t, o, n):
+        o = o if t == 0 else 64 + 176 * (t - 1) + o
+        return V("ZB", o, o + n)
+
+    def sub(v, a, b, k=None, st=1):
+        return (v[0], v[1] if k is None else 32 * k, v[2] if k is None else 32 * k + 32, v[3] + a, v[3] + b, st)
+
+    def bufs(t):
+        return lambda name, *a: V(name + str(t), *a)
+
+    for i in range(8):
+        load("sa"[i % 2], V("RAW1", p0=16 * i, p1=16 * i + 16), T.p1[:], LOCAL)
+    load("s", V("E0", 0, 512), T.e0[:, 0:512], FIRST)
+    load("a", V("UT", 0, 4), T.u[:, 0:4], FIRST)
+    load("a", V("E0", 512, 1024), T.e0[:, 512:1024], FIRST)
+    for i in range(8):
+        load("s", V("RAW2", p0=16 * i, p1=16 * i + 16), T.p2[:], FIRST)
+    op("g", lambda: g.iota(ap(V("PI")), [[0, 1]], 0, 1), [], [V("PI")], 100)
+    fill(V("J4"), 0, pattern=[[0, 16], [1, 4]])
+    fill(V("J16"), 0, pattern=[[0, 8], [1, 16]])
+    for j, m in enumerate((15, 3, 1, 96, 31, 16)):
+        ts(V("PJ", j, j + 1), V("PI"), m, A.bitwise_and)
+    ts(V("PJ", 6, 7), V("PI"), 2, A.logical_shift_right, 3, A.bitwise_and)
+    tc(V("PF32", 0, 7), V("PJ", 0, 7))
+    p15, kcol, p31, p4 = V("PF32", 0, 1), V("PF32", 1, 2), V("PF32", 4, 5), V("PF32", 6, 7)
+    ts(V("SL", 0, 1), V("PF32", 3, 4), 8.0, A.mult, -0.5, A.add)
+    ts(V("SL", 1, 2), V("PF32", 3, 4), 8.0, A.mult, P - 0.5, A.add)
+    ts(V("SL", 2, 3), V("PF32", 3, 4), 24.0, A.mult, 3 * (P - 0.5), A.add)
+    ts(V("SEG4"), V("J4"), 1.0, A.min)
+    fill(V("PKC"), 4, pattern=[[0, 2], [-3, 2], [0, 4]])
+    op("g", lambda: g.iota(ap(V("DUPI")), [[64, 4], [0, 2]], 0, 0), [], [V("DUPI")], 100)
+    op("g", lambda: g.iota(ap(V("PERMI")), [[4, 2]], 0, 0), [], [V("PERMI")], 100)
+    fill(V("J32"), 0, 1)
+    fill(V("TR"), 1028, 4, 32)
+
+    def fills():
+        fill(V("IDT"), 0, 1)
+        for t in (1, 2):
+            fill(V("RT%d" % t, 32, 40), 4)
+
+    def constants():
+        for c in range(0, 416, 104):
+            ms(V("ZB", c, c + 104), 0.0)
+        ms(V("ZERO"), 0.0)
+        ms(V("W1", 0, 256), 0.0)
+        ms(V("BAR"), 0.0)
+        ms(V("BAR", 4, 33, 4), -BIG - 4.0)
+        ms(V("BAR", 1, 32, 4), 1.5)
+        ms(V("BAR", 3, 32, 4), BIG)
+        ts(V("SEGT"), V("J4", 0, 40), 1.5, A.is_gt)
+        lin(V("SEGT", 4, 33, 4), V("TR"))
+        ts(V("MASK"), V("J16"), p15, A.is_equal)
+        ts(V("SEG16"), V("J16"), 1.0, A.min)
+        ts(V("SUF"), V("J32"), p31, A.is_ge)
+        ts(V("KCOL", 1, 2), kcol, 8.0, A.mult, p4, A.add)
+        ts(V("KCOL", 2, 3), p15, 4.0, A.mult)
+        ts(V("DUP"), V("DUPI"), V("KCOL", 2, 3), A.add)
+        ts(V("PERM"), V("PERMI"), V("KCOL", 1, 2), A.add)
+        ts(V("PV"), V("PERMI"), p4, A.add)
+        ts(V("XEO", 4, 5), V("PF32", 2, 3), 1.0, A.mult)
+        lin(V("XEO", 0, 1), V("PF32", 2, 3), -1.0, 1.0)
+        ts(V("GD", 0, 1), V("PF32", 3, 4), 8.0, A.mult, float(-P * me), A.add)
+        for k in range(4):
+            ms(blk(k, "BC", 0, 1), float(255 + 64 * others.index(k)) if k != me else 0.0)
+
+    def prep_lists(t, out):
+        b = bufs(t)
+        for h in range(2):
+            ts(b("RL", 32 * h, 32 * h + 32), V("RAW%d" % t, h, 64, 2), V("SL", 0, 1), A.max, V("SL", 1, 2), A.min)
+        for h in range(2):
+            tr(b("T2", 32 * h, 32 * h + 32), b("RL", 32 * h, 32 * h + 32))
+        for h in range(2):
+            scan(b("SCL", 32 * h, 32 * h + 32), V("SEG4", 0, 32), b("T2", 32 * h, 32 * h + 32), A.mult, A.add)
+        for h in range(2):
+            ts(V(out, 4 * h, 4 * h + 4), b("SCL", 32 * h + 3, 32 * h + 16, 4), V("SL", 2, 3), A.subtract)
+
+    def prep_ties(t):
+        b = bufs(t)
+        for h in range(2):
+            tt(b("EQN", 32 * h, 32 * h + 32), b("RL", 32 * h, 32 * h + 32), V("RAW%d" % t, h, 64, 2), A.is_equal)
+        lin(b("KQN"), b("EQN"), scale=V("KCOL", 0, 1))
+        tr(b("TK"), b("KQN"))
+        scan(b("SK"), V("SEG4"), b("TK"), A.mult, A.add)
+        scan(b("PK"), V("PKC"), b("SK", 3, 64, 4), A.mult, A.add)
+        tc(V("MSG2", t - 1, t), b("PK", 15, 16))
+
+    def own_columns(t):
+        b = bufs(t)
+        tc(b("LCN"), V("MSG1") if t == 1 else V("LS2"))
+        for k in [me] + others:
+            act(blk(k, "OL%d" % t), blk(me, "LCN%d" % t))
+        lin(blk(me, "CO%d" % t), blk(me, "LCN%d" % t), bias=float(P * me))
+        lin(b("OB"), b("OL"), -1.0, V("BC", 0, 1))
+        tt(b("CD"), b("LCN"), b("OL"), A.subtract)
+        lin(b("CG"), b("CD"), bias=V("GD", 0, 1))
+
+    def decode_ties():
+        slot = {d: i for i, d in enumerate(others + [me])}
+        tc(V("KC", 0, 6), V("LM2"))
+        tc(V("KC", 6, 8), V("MSG2"))
+        for c in range(8):
+            ts(V("KD", c, 64, 8), V("KC"), 2 * (7 - c), A.logical_shift_right, 3, A.bitwise_and)
+        tc(V("KF"), V("KD"))
+        ka = zb(0, 0, 64)
+        for d in range(4):
+            for s in range(4):
+                if s != d:
+                    i = (s - me) % 4
+                    lin(sub(ka, 16 * i, 16 * i + 16, d), blk(s, "KF", 16 * slot[d], 16 * slot[d] + 16))
+
+    def tie_flags(t):
+        ka, o = zb(0, 0, 64), 8 * (t - 1)
+        for i in range(4):
+            if i:
+                tt(sub(zb(t, 80, 32), i, 32, None, 4), sub(ka, 16 * i + o, 16 * i + o + 8), sub(ka, o, o + 8), A.is_lt)
+            lin(V("KK%d" % t, 8 * i, 8 * i + 8), sub(ka, 16 * i + o, 16 * i + o + 8), -1.0, 4.0)
+
+    def value_rows(t):
+        b = bufs(t)
+        gata(b("V4"), b("U", 0, 8), V("PV"))
+        op("a", lambda: g.scalar.activation(ap(b("AB")), ap(b("V4")), AF.Abs, scale=STEP), [b("V4")], [b("AB")], 32)
+        gata(b("VR"), V("IDT"), b("LU"))
+
+    def thresholds(t):
+        b = bufs(t)
+        ts(b("AC"), b("AB"), TINY, A.add)
+        tt(b("DE"), b("AC"), zb(t, 80, 32), A.mult)
+        tt(b("VA"), b("V4"), b("DE"), A.subtract)
+
+    def scores_out(t):
+        b = bufs(t)
+        tti(b("G"), V("S%d" % (t - 1)), b("LU"), V("MASK"), A.mult)
+        scan(b("SG"), V("SEG16"), b("G"), A.mult, A.add)
+        lin(b("U", 0, 8), b("SG", 15, 128, 16))
+        return spread(b("U", 0, 8), lambda s: b("U", 8 + 8 * s, 16 + 8 * s), "v%d" % t, "lv%d" % t, b("U", 8, 32))
+
+    def prefix(x, add, ni, eb, tb, ec):
+        scan(sub(ni, 0, 8), x, add)
+        tr(tb, ni)
+        scan(sub(eb, 1, 33), tb, V("ZERO", 0, 32))
+        tr(ec, sub(eb, 0, 32))
+
+    def choose_and_send(t):
+        b = bufs(t)
+        worse = zb(t, 112, 64)
+        tti(sub(worse, 0, 32), b("U"), V("PERM"), b("VA"), A.is_gt)
+        scan(b("NI"), worse, V("BAR"))
+        scan(b("BT", 0, 33), V("SEGT", 0, 33), sub(worse, 0, 33), A.mult, A.max)
+        tr(b("RT", 0, 32), b("NI", 32, 64))
+        op("a", lambda: g.scalar.activation(ap(b("TJ", 0, 33)), ap(b("RT", 0, 33)), AF.Copy, accum_out=ap(b("TA1"))),
+           [b("RT", 0, 33)], [b("TJ", 0, 33), b("TA1")], 50)
+        tt(b("AA"), b("BT", 4, 33, 4), b("NI", 4, 33, 4), A.subtract)
+        scan(b("SFX"), b("RT", 0, 32), V("SUF"), A.add, A.mult)
+        ts(b("OF"), b("AA"), b("TA1"), A.subtract, b("SFX", 31, 32), A.add)
+        op("v", lambda: g.vector.tensor_copy(ap(b("W")).indirect(ap(b("OF"))), ap(b("VR"))), [b("VR"), b("OF")], [b("W")], 450)
+        gat(b("WD", 0, 64), b("W", 0, 256), V("DUP", 0, 4))
+        gata(b("WD", 64, 128), b("W", 0, 256), V("DUP", 4, 8))
+        tr(b("TW"), b("WD"))
+        cols = {d: (4 * i, 4 * i + 4) for i, d in enumerate(others)}
+        pf = "PF%d" % t
+        alone = me // 2 * 2 + 1 - me % 2
+        for d in [d for d in others if d != alone] + [alone]:
+            lo, hi = cols[d]
+            tt(blk(d, pf, lo, hi), blk(d, "TW%d" % t, 0, 128, 32), blk(d, "TW%d" % t, 16, 128, 32), A.add)
+            k = d // 2 * 2 + 1 - d % 2
+            if d == alone:
+                tt(blk(k, pf, lo, hi), blk(d, "TW%d" % t, 0, 128, 32), blk(d, "TW%d" % t, 16, 128, 32), A.add)
+            else:
+                act(blk(k, pf, lo, hi), blk(d, pf, lo, hi))
+        for half in (me // 2, 1 - me // 2):
+            own = [cols[d] for d in others if d // 2 == half]
+            lo, hi = min(own)[0], max(own)[1]
+            for h in (half, 1 - half):
+                tc(V("PO%d" % t, lo, hi, 1, 64 * h, 64 * h + 64), V(pf, lo, hi, 1, 64 * half, 64 * half + 64))
+        pick(b("SQ"), b("SS"), V("QO%d" % (t - 1)), V("QS%d" % (t - 1)), b("PO"))
+        each("SQ%d" % t, 64, "QW%d" % (t - 1), "c%d" % t, "lc%d" % t)
+        return each("SS%d" % t, 64, "QP%d" % (t - 1), "s%d" % t, "ls%d" % t, 3)
+
+    def own_list(t):
+        b = bufs(t)
+        mk = lambda name, *a: blk(me, name + str(t), *a)
+        tt(b("M16"), b("U", 0, 16), b("U", 16, 32), A.max)
+        tt(b("MM"), b("M16", 0, 8), b("M16", 8, 16), A.max)
+        for i in range(4):
+            tt(b("EQ", 8 * i, 8 * i + 8), b("U", 8 * i, 8 * i + 8), b("MM"), A.is_equal)
+        tt(b("KEY"), b("EQ"), b("KK"), A.mult)
+        tt(b("K16"), b("KEY", 0, 16), b("KEY", 16, 32), A.max)
+        tt(b("KM"), b("K16", 0, 8), b("K16", 8, 16), A.max)
+        wb, i2 = zb(t, 72, 8), zb(t, 0, 32)
+        for i, s in enumerate(others):
+            tt(sub(wb, 0, 8, s), mk("KEY", 8 * i + 8, 8 * i + 16), mk("KM"), A.is_equal)
+        prefix(wb, V("ZERO", 0, 8), i2, zb(t, 32, 40), b("TB2"), b("EC2"))
+        lin(b("NW"), wb, -1000.0, 1000.0)
+        tt(b("NP"), sub(i2, 0, 8), b("NW"), A.add)
+        tt(b("BP"), sub(i2, 0, 8), b("OB"), A.add)
+        keep = b("VAL", 16, 24)
+        ts(keep, b("NP"), b("EC2", 7, 8), A.add, float(CAPP), A.is_le)
+        ts(b("SV"), b("BP"), b("EC2", 7, 8), A.add)
+        tt(b("VAL", 8, 16), keep, b("CG"), A.mult)
+        tt(b("VAL", 0, 8), keep, b("SV"), A.mult)
+        for i, s in enumerate(others):
+            lin(mk("BK", 24 * i, 24 * i + 24), blk(s, "VAL%d" % t))
+            lin(mk("KQ", 8 * i + 8, 8 * i + 16), mk("BK", 24 * i + 16, 24 * i + 24))
+        tt(mk("SA"), mk("BK", 0, 24), mk("BK", 24, 48), A.add)
+        tt(mk("SB"), mk("BK", 48, 56), mk("LCN"), A.add)
+        tt(mk("KS"), mk("SA", 16, 24), mk("BK", 64, 72), A.add)
+        tt(mk("XC"), mk("SA", 0, 8), mk("SB"), A.add)
+        lin(mk("KQ", 0, 8), mk("KS"), -1.0, 1.0)
+        for j in range(4):
+            lin(mk("A2", 8 * j, 8 * j + 8), mk("XC"), scale=blk(me, "XEO", 4 * (j % 2), 4 * (j % 2) + 1))
+        tr(mk("TA"), mk("A2"))
+        tt(mk("XT"), mk("TA", 0, 32, 2), mk("TA", 1, 32, 2), A.add)
+        half = me // 2
+        for k in (2 * half, 2 * half + 1):
+            tc(blk(k, "XO%d" % t), mk("XT"))
+        tc(V("XO%d" % t, p0=64 - 64 * half, p1=128 - 64 * half), V("XO%d" % t, p0=64 * half, p1=64 * half + 64))
+        tt(mk("PP"), mk("KQ"), mk("U"), A.mult)
+        tt(mk("P16"), mk("PP", 0, 16), mk("PP", 16, 32), A.add)
+        tt(mk("PA"), mk("P16", 0, 8), mk("P16", 8, 16), A.add)
+        pr = V("PR%d" % t, 0, 256, 1, 0, 1)
+        dma("s", ap(pr), ap(mk("PA")), [mk("PA")], [pr])
+        op("g", lambda: g.partition_broadcast(ap(b("PB")), ap(pr), 128), [pr], [b("PB")], 1024)
+
+    def own_choice(t):
+        mk = lambda name, *a: blk(me, name + str(t), *a)
+        tt(mk("CA"), mk("BK", 56, 64), mk("CO"), A.add)
+        tt(mk("CH"), mk("SA", 8, 16), mk("CA"), A.add)
+        dma("s", T.ch[t - 1:t, :], ap(mk("CH")), [mk("CH")], [])
+
+    def products(t, i, arrived):
+        q, s, n, o = ("QW", "QP", 192, 256) if arrived else ("QO", "QS", 256, 0)
+        r = mm(i if arrived else 4 + i, n, V("AQ", 128 * i, 128 * i + 128), V("AP", 128 * i, 128 * i + 128), V(q + str(t - 1)), V(s + str(t - 1)))
+        act(V("Z%d" % t, 448 * i + o, 448 * i + o + n), r, 0.05)
+
+    def new_columns(t):
+        b = bufs(t)
+        for i in range(4):
+            products(t, i, True)
+        rs, first, wide = {}, None, 3
+
+        def choose(i, lo, hi):
+            tti(b("HT", 4 * lo + i, 4 * hi, 4), b("Z", 448 * i, 448 * i + 448), b("XO", lo // 16, hi // 16),
+                V("E%d" % t, 4 * lo + i, 4 * hi, 4), A.add)
+        for i in range(wide):
+            choose(i, 0, P)
+        for i in range(wide, 4):
+            choose(i, 0, 128)
+            choose(i, 128, P)
+        for f in range(2):
+            lo, hi = 128 * f, 128 * f + 128
+            first = qz(V("QO%d" % t, lo, hi), V("QS%d" % t, lo, hi), b("HT", 512 * f, 512 * f + 512))
+            rs[f] = mm(4 + f, 128, V("UQ"), V("UP"), V("QO%d" % t, lo, hi), V("QS%d" % t, lo, hi))
+            if t == 2:
+                yp = mm(6 + f, 128, V("WQ"), V("WP"), V("QO2", lo, hi), V("QS2", lo, hi))
+                dma("s", T.oc[:, 4 * lo:4 * hi], ap(V("QO2", lo, hi)).bitcast(dt.uint8), [V("QO2", lo, hi)], [])
+                for k in range(4):
+                    sc = V("QS2", lo, hi, 1, 32 * k, 32 * k + 4)
+                    dma("s", T.osc[4 * k:4 * k + 4, lo:hi], ap(sc), [sc], [])
+                lin(V("YB", lo, hi), yp)
+                dma("a", T.y[:, lo:hi], ap(V("YB", lo, hi)), [V("YB", lo, hi)], [], dur=LOCAL + 0.6)
+        hold[0] = (first,)
+        for f in range(2):
+            tt(V("S%d" % t, 128 * f, 128 * f + 128), rs[f], b("PB", 128 * f, 128 * f + 128), A.add)
+        hold[0] = ()
+        if t == 2:
+            row = V("S2", 0, 256, 1, 0, 1)
+            dma("s", T.g[:], ap(row), [row], [])
+
+    prep_lists(1, "MSG1")
+    sent = spread(V("MSG1"), lambda s: V("LM1", 8 * s, 8 * s + 8), "m1", "lm1", V("LM1"))
+    w = 4
+    while w < 512:
+        act(V("UT", w, 2 * w), V("UT", 0, w))
+        w *= 2
+    qz(V("UQ"), V("UP"), V("UT"))
+    qz(V("QO0"), V("QS0"), V("E0"))
+    act(V("S0"), mm(0, 256, V("UQ"), V("UP"), V("QO0"), V("QS0")))
+    prep_lists(2, "LS2")
+    hold[0] = (sent,)
+    ts(V("KCOL", 0, 1), V("PF32", 5, 6), 0.0, A.is_equal, kcol, A.mult)
+    prep_ties(1)
+    prep_ties(2)
+    ties = spread(V("MSG2"), lambda s: V("LM2", 2 * s, 2 * s + 2), "m2", "lm2", V("LM2"))
+    load("s", V("AT", 0, 1024), T.a[:, 0:1024], LONG, [ties])
+    fills()
+    constants()
+    hold[0] = ()
+    for d in [me] + others:
+        tc(blk(d, "LU1"), blk(me, "MSG1") if d == me else blk(me, "LM1", 8 * others.index(d), 8 * others.index(d) + 8))
+    tc(blk(me, "LU2"), blk(me, "LS2"))
+    scores = scores_out(1)
+    load("s", V("AT", 1024, 2048), T.a[:, 1024:2048], LONG, [scores])
+    load("s", V("E1"), T.e1[:], LONG, [scores])
+    own_columns(1)
+    for i, d in enumerate(others):
+        dma("s", ap(V("ST2", 2 * i, 2 * i + 2)), ap(blk(d, "LS2")), [blk(d, "LS2")], [V("ST2", 2 * i, 2 * i + 2)])
+    hold[0] = (scores - 1,)
+    value_rows(1)
+    hold[0] = ()
+    decode_ties()
+    tie_flags(1)
+    thresholds(1)
+    sent = choose_and_send(1)
+    each("ST2", 2, "LC2", "m3", "lm3")
+    for i, d in enumerate(others):
+        dma("s", ap(blk(d, "LU2")), ap(V("LC2", 2 * i, 2 * i + 2)), [V("LC2", 2 * i, 2 * i + 2)], [blk(d, "LU2")])
+    hold[0] = (sent,)
+    for i in range(4):
+        qz(V("AQ", 128 * i, 128 * i + 128), V("AP", 128 * i, 128 * i + 128), V("AT", 512 * i, 512 * i + 512))
+        products(1, i, False)
+    hold[0] = ()
+    own_list(1)
+    new_columns(1)
+    scores = scores_out(2)
+    load("s", V("WT"), T.w[:], LONG, [scores])
+    load("s", V("E2"), T.e2[:], LONG, [scores])
+    hold[0] = (scores - 1,)
+    tie_flags(2)
+    value_rows(2)
+    thresholds(2)
+    for i in range(4):
+        products(2, i, False)
+    ms(V("W2", 0, 256), 0.0)
+    own_columns(2)
+    own_choice(1)
+    hold[0] = ()
+    sent = choose_and_send(2)
+    hold[0] = (sent,)
+    qz(V("WQ"), V("WP"), V("WT"))
+    hold[0] = ()
+    own_list(2)
+    own_choice(2)
+    new_columns(2)
+    lay()
+    for sem in sorted(total):
+        wait("s", [(sem, total[sem], {})])

@@ -5,7 +5,7 @@ P, CAPP = 256, 64
 TINY = 2.0 ** -100
 STEP = 2.0 ** -24 * (1 + 2.0 ** -10)
 BIG = 1.5 * 2.0 ** 25
-WAIT, LEAST, ISSUE, WAY, ONCE = 0.13, 0.09, 0.8, 2.9, 1.5
+WAIT, LEAST, ISSUE, WAY, ONCE = 0.16, 0.09, 0.8, 2.8, 1.5
 LOCAL, FIRST, LONG = 2.3, 3.8, 5.5
 F, B, I, H, C, S8 = "float32", "bfloat16", "int32", "uint16", "float8_e4m3fn_x4", "uint8"
 SCRATCH = {"PS": ("psum", [128, 4096], F)}
@@ -30,21 +30,22 @@ def _each(**names):
     return {n + str(t): w for t in (1, 2) for n, w in names.items()}
 
 
-_buf(B, UT=512, E0=1024, AT=2048, WT=512, E1=1024, E2=1024, HT1=1024, HT2=1024)
+_buf(B, UC=4, UT=512, E0=1024, AT=2048, WT=512, E1=1024, E2=1024, HT1=1024, HT2=1024)
 _buf(C, UQ=128, AQ=512, WQ=128, QO0=256, QO1=256, QO2=256, QW0=192, QW1=192, SQ1=192, SQ2=192)
 _buf(S8, UP=128, AP=512, WP=128, QS0=256, QS1=256, QS2=256, QP0=192, QP1=192, SS1=192, SS2=192)
 _buf(H, MSG1=8, MSG2=2, LM1=24, LM2=6, LS2=8, ST2=6, LC2=6, LU1=8, LU2=8)
-_buf(F, U1=32, U2=32, Z1=1792, Z2=1792, YB=256, S0=256, S1=256, S2=256, PR1=256, PR2=256, PB1=256, PB2=256)
+_buf(F, ZERO=128, U1=32, U2=32, Z1=1792, Z2=1792, YB=256, S0=256, S1=256, S2=256, PR1=256, PR2=256, PB1=256)
 _buf(I, RAW1=64, RAW2=64)
 _area(H, DUP=8, PERM=2, PV=2)
 _area(I, PI=1, PJ=8, DUPI=8, PERMI=2, KC=8, KD=64)
-_area(F, ZERO=64, BAR=64, SEGT=40, KCOL=4, SL=4, XEO=8, GD=4, BC=4, TR=8, ZB=416, PF32=8, J4=64, SEG4=64, J16=128, MASK=128,
+_area(F, BAR=64, SEGT=40, KCOL=4, SL=4, XEO=8, GD=4, BC=4, TR=8, ZB=416, PF32=8, J4=64, SEG4=64, J16=128, MASK=128,
       SEG16=128, SUF=32, J32=32, IDT=256, PKC=16, KF=64)
 _area(F, **_each(RL=64, T2=64, SCL=64, EQN=64, KQN=64, TK=64, SK=64, PK=16, LCN=8, OL=8, OB=8, CD=8, CG=8,
                  VR=128, KK=32, G=128, SG=128, V4=32, AB=32, AC=32, DE=32, VA=32, BT=40, NI=64, RT=40, TJ=40, TA1=1, SFX=32,
-                 AA=8, W=6208, WD=128, TW=128, PF=16, M16=16, MM=8, EQ=32, KEY=32, K16=16, KM=8, TB2=32, EC2=32, SV=8,
-                 NW=8, NP=8, BP=8, VAL=24, BK=72, SA=24, SB=8, KS=8, CA=8, CO=8, CH=8, XC=8, A2=32, TA=32, XT=16, KQ=32, PP=32,
-                 P16=16, PA=8))
+                 AA=8, W=6208, WD=128, TW=128, PF=16, M16=16, MM=8, EQ=32, KEY=32, K16=16, KM=8,
+                 IC=40, RC=40, TJC=40, TAC=1, SFC=32, KP=8, CB=8, SV=8,
+                 NW=8, NP=8, BP=8, VAL=24, BK=24, SA=8, SB=8, CA=8, CO=8, CH=8, XC=8, A2=32, TA=32, XT=16, KQ=16, PP=16,
+                 PA=8))
 _area(H, **_each(OF=8, PO=12, XO=16))
 NDMA = 60
 SEMAPHORES = ["qv", "qa", "qt", "qg", "m1", "lm1", "m2", "lm2", "m3", "lm3"] + ["d%d" % i for i in range(NDMA)] + [
@@ -95,7 +96,7 @@ def rank_program(g, core, T, topo):
         if "g" in opts:
             last["g"] = i
         nodes.append({"opts": opts, "rd": reads, "wr": writes, "cost": cost, "dur": cost if dur is None else dur,
-                      "deps": deps - {i}, "prev": prev, "gate": [j for j in after]})
+                      "deps": deps - {i}, "prev": prev, "gate": [j for j in after], "more": 0.0})
         return i
 
     def wait(q, evs):
@@ -145,9 +146,9 @@ def rank_program(g, core, T, topo):
                 succ[j].append(i)
         high = [0.0] * n
         for i in range(n - 1, -1, -1):
-            high[i] = nodes[i]["dur"] + max([WAIT + high[j] for j in succ[i]] + [high[i]])
+            high[i] = nodes[i]["dur"] + nodes[i]["more"] + max([WAIT + high[j] for j in succ[i]] + [high[i]])
             for p in nodes[i]["prev"]:
-                high[p] = max(high[p], nodes[p]["cost"] + high[i] - nodes[p]["dur"])
+                high[p] = max(high[p], nodes[p]["cost"] + high[i] - nodes[i]["more"] - nodes[p]["dur"])
         left = [len(nd["deps"]) for nd in nodes]
         ready = {i for i in range(n) if left[i] == 0}
         free, fin, done = {}, [0.0] * n, set()
@@ -161,7 +162,7 @@ def rank_program(g, core, T, topo):
                 start, q = min((max(s, free.get(q, 0.0)) if q != "x" else s, "vatgsx".index(q)) for q in nd["opts"])
                 cand.append((start, -high[i], i, "vatgsx"[q]))
             first = min(cand)[0]
-            start, _, i, q = min((c for c in cand if c[0] <= first + 0.05), key=lambda c: c[1:])
+            start, _, i, q = min((c for c in cand if c[0] <= first + 0.07), key=lambda c: c[1:])
             issue(nodes[i], q)
             free[q] = start + nodes[i]["cost"]
             fin[i] = start + nodes[i]["dur"]
@@ -199,7 +200,7 @@ def rank_program(g, core, T, topo):
         else:
             op("v", lambda: g.vector.tensor_scalar(ap(o), ap(a), sv(s1), sv(s2), f1, f2), [a] + cols_of(s1, s2), [o], width(a))
 
-    def lin(o, a, scale=1.0, bias=0.0):
+    def lin(o, a, scale=1.0, bias=0.0, only=None):
         def on_v():
             if scale == 1.0 and bias == 0.0:
                 return g.vector.tensor_copy(ap(o), ap(a))
@@ -213,7 +214,8 @@ def rank_program(g, core, T, topo):
             if bias == 0.0:
                 return g.scalar.activation(ap(o), ap(a), AF.Copy, scale=sv(scale))
             return g.scalar.activation(ap(o), ap(a), AF.Identity, scale=sv(scale), bias=sv(bias))
-        push({"v": ("op", on_v), "a": ("op", on_a)}, [a] + cols_of(scale, bias), [o], us(width(a)))
+        opts = {"v": ("op", on_v), "a": ("op", on_a)}
+        push({only: opts[only]} if only else opts, [a] + cols_of(scale, bias), [o], us(width(a)))
 
     def scan(o, a, b, f0=A.add, f1=A.add):
         op("v", lambda: g.vector.tensor_tensor_scan(ap(o), ap(a), ap(b), 0.0, f0, f1), [a, b], [o], width(a))
@@ -281,17 +283,21 @@ def rank_program(g, core, T, topo):
             dst_ids=[dst(d) for d in others], dma_engine_mask=mask_of(e), remote_sem=T.sem[sem], srcs=[ap(src)],
             dsts=[ap(land(s)) for s in slot_at])], src, lsem, len(e), sem, 3 * len(e), landing)
 
+    def deal(s, turn):
+        order = sorted([d for d in range(4) if d != s], key=lambda d: (topo.die(T.cores[d]) != topo.die(T.cores[s]), (d - s) % 4 == 2))
+        e = topo.engines(T.cores[s], T.cores[order[0]])
+        a, z = (e[8:16], e[0:8]) if turn else (e[0:8], e[8:16])
+        return {order[0]: a[1::2], order[1]: a[0::2], order[2]: z}
+
     def each(src, w, land, sem, lsem, turn=0):
         trs = []
         for i, d in enumerate(others):
-            e = topo.engines(core, T.cores[d])
-            j = 4 * ((i + turn) % 4)
             a, z = V(src, w * i, w * i + w), V(land, w * slot_at[i], w * slot_at[i] + w)
             code = SCRATCH[src][2] == C
             trs.append(RemoteDMATransfer(
-                dst_ids=[dst(d)], dma_engine_mask=mask_of(e[j:j + 4]), remote_sem=T.sem[sem],
+                dst_ids=[dst(d)], dma_engine_mask=mask_of(deal(me, turn)[d]), remote_sem=T.sem[sem],
                 srcs=[ap(a).bitcast(dt.uint8) if code else ap(a)], dsts=[ap(z).bitcast(dt.uint8) if code else ap(z)]))
-        return remote(trs, V(src), lsem, 12, sem, 12, V(land))
+        return remote(trs, V(src), lsem, 16, sem, sum(len(deal(s, turn)[me]) for s in others), V(land))
 
     def zb(t, o, n):
         o = o if t == 0 else 64 + 176 * (t - 1) + o
@@ -306,10 +312,14 @@ def rank_program(g, core, T, topo):
     for i in range(8):
         load("sa"[i % 2], V("RAW1", p0=16 * i, p1=16 * i + 16), T.p1[:], LOCAL)
     load("s", V("E0", 0, 512), T.e0[:, 0:512], FIRST)
-    load("a", V("UT", 0, 4), T.u[:, 0:4], FIRST)
+    load("a", V("UC"), T.u[:, 0:4], FIRST)
     load("a", V("E0", 512, 1024), T.e0[:, 512:1024], FIRST)
-    for i in range(8):
-        load("s", V("RAW2", p0=16 * i, p1=16 * i + 16), T.p2[:], FIRST)
+    ms(V("RAW2"), 0)
+    for i in range(4):
+        raw = load("s", V("RAW2", p0=32 * i, p1=32 * i + 16), T.p2[:], FIRST)
+    hold[0] = (raw,)
+    load("s", V("AT", 0, 1024), T.a[:, 0:1024], LONG)
+    hold[0] = ()
     op("g", lambda: g.iota(ap(V("PI")), [[0, 1]], 0, 1), [], [V("PI")], 100)
     fill(V("J4"), 0, pattern=[[0, 16], [1, 4]])
     fill(V("J16"), 0, pattern=[[0, 8], [1, 16]])
@@ -318,30 +328,38 @@ def rank_program(g, core, T, topo):
     ts(V("PJ", 6, 7), V("PI"), 2, A.logical_shift_right, 3, A.bitwise_and)
     tc(V("PF32", 0, 7), V("PJ", 0, 7))
     p15, kcol, p31, p4 = V("PF32", 0, 1), V("PF32", 1, 2), V("PF32", 4, 5), V("PF32", 6, 7)
-    ts(V("SL", 0, 1), V("PF32", 3, 4), 8.0, A.mult, -0.5, A.add)
-    ts(V("SL", 1, 2), V("PF32", 3, 4), 8.0, A.mult, P - 0.5, A.add)
-    ts(V("SL", 2, 3), V("PF32", 3, 4), 24.0, A.mult, 3 * (P - 0.5), A.add)
+    ts(V("SL", 0, 1), V("PJ", 3, 4), 8.0, A.mult, -0.5, A.add)
+    ts(V("SL", 1, 2), V("PJ", 3, 4), 8.0, A.mult, P - 0.5, A.add)
+    ts(V("SL", 2, 3), V("PJ", 3, 4), 24.0, A.mult, 3 * (P - 0.5), A.add)
     ts(V("SEG4"), V("J4"), 1.0, A.min)
     fill(V("PKC"), 4, pattern=[[0, 2], [-3, 2], [0, 4]])
     op("g", lambda: g.iota(ap(V("DUPI")), [[64, 4], [0, 2]], 0, 0), [], [V("DUPI")], 100)
     op("g", lambda: g.iota(ap(V("PERMI")), [[4, 2]], 0, 0), [], [V("PERMI")], 100)
     fill(V("J32"), 0, 1)
     fill(V("TR"), 1028, 4, 32)
+    fill(V("ZERO"), 0)
+    for k in range(4):
+        ms(blk(k, "BC", 0, 1), float(255 + CAPP + 64 * others.index(k)) if k != me else 0.0)
+    ms(V("BAR"), 0.0)
+    ms(V("BAR", 4, 33, 4), -BIG - 4.0)
+    ms(V("BAR", 1, 32, 4), 1.5)
+    ms(V("BAR", 3, 32, 4), BIG)
+    act(V("XEO", 4, 5), V("PF32", 2, 3))
+    lin(V("XEO", 0, 1), V("PF32", 2, 3), -1.0, 1.0, "a")
+    lin(V("GD", 0, 1), V("PF32", 3, 4), 8.0, float(-P * me), "a")
 
-    def fills():
-        fill(V("IDT"), 0, 1)
+    def more_fills():
+        fill(V("RT1", 32, 40), 4)
+        fill(V("W1", 0, 256), 0)
         for t in (1, 2):
-            fill(V("RT%d" % t, 32, 40), 4)
+            fill(V("KK%d" % t, 0, 8), 4)
+            fill(V("RC%d" % t, 32, 40), -CAPP)
+        fill(V("RT2", 32, 40), 4)
+        fill(V("W2", 0, 256), 0)
 
     def constants():
         for c in range(0, 416, 104):
             ms(V("ZB", c, c + 104), 0.0)
-        ms(V("ZERO"), 0.0)
-        ms(V("W1", 0, 256), 0.0)
-        ms(V("BAR"), 0.0)
-        ms(V("BAR", 4, 33, 4), -BIG - 4.0)
-        ms(V("BAR", 1, 32, 4), 1.5)
-        ms(V("BAR", 3, 32, 4), BIG)
         ts(V("SEGT"), V("J4", 0, 40), 1.5, A.is_gt)
         lin(V("SEGT", 4, 33, 4), V("TR"))
         ts(V("MASK"), V("J16"), p15, A.is_equal)
@@ -352,11 +370,6 @@ def rank_program(g, core, T, topo):
         ts(V("DUP"), V("DUPI"), V("KCOL", 2, 3), A.add)
         ts(V("PERM"), V("PERMI"), V("KCOL", 1, 2), A.add)
         ts(V("PV"), V("PERMI"), p4, A.add)
-        ts(V("XEO", 4, 5), V("PF32", 2, 3), 1.0, A.mult)
-        lin(V("XEO", 0, 1), V("PF32", 2, 3), -1.0, 1.0)
-        ts(V("GD", 0, 1), V("PF32", 3, 4), 8.0, A.mult, float(-P * me), A.add)
-        for k in range(4):
-            ms(blk(k, "BC", 0, 1), float(255 + 64 * others.index(k)) if k != me else 0.0)
 
     def prep_lists(t, out):
         b = bufs(t)
@@ -390,25 +403,24 @@ def rank_program(g, core, T, topo):
         lin(b("CG"), b("CD"), bias=V("GD", 0, 1))
 
     def decode_ties():
-        slot = {d: i for i, d in enumerate(others + [me])}
         tc(V("KC", 0, 6), V("LM2"))
         tc(V("KC", 6, 8), V("MSG2"))
         for c in range(8):
             ts(V("KD", c, 64, 8), V("KC"), 2 * (7 - c), A.logical_shift_right, 3, A.bitwise_and)
         tc(V("KF"), V("KD"))
         ka = zb(0, 0, 64)
-        for d in range(4):
+        for j, d in enumerate(others):
             for s in range(4):
                 if s != d:
                     i = (s - me) % 4
-                    lin(sub(ka, 16 * i, 16 * i + 16, d), blk(s, "KF", 16 * slot[d], 16 * slot[d] + 16))
+                    lin(sub(ka, 16 * i, 16 * i + 16, d), blk(s, "KF", 16 * j, 16 * j + 16))
 
     def tie_flags(t):
         ka, o = zb(0, 0, 64), 8 * (t - 1)
-        for i in range(4):
-            if i:
-                tt(sub(zb(t, 80, 32), i, 32, None, 4), sub(ka, 16 * i + o, 16 * i + o + 8), sub(ka, o, o + 8), A.is_lt)
-            lin(V("KK%d" % t, 8 * i, 8 * i + 8), sub(ka, 16 * i + o, 16 * i + o + 8), -1.0, 4.0)
+        for i in range(1, 4):
+            tt(sub(zb(t, 80, 32), i, 32, None, 4), sub(ka, 16 * i + o, 16 * i + o + 8), sub(ka, o, o + 8), A.is_lt)
+        for i, s in enumerate(others):
+            lin(blk(me, "KK%d" % t, 8 * i + 8, 8 * i + 16), blk(s, "KF", 48 + o, 56 + o), -1.0, 4.0)
 
     def value_rows(t):
         b = bufs(t)
@@ -429,12 +441,6 @@ def rank_program(g, core, T, topo):
         lin(b("U", 0, 8), b("SG", 15, 128, 16))
         return spread(b("U", 0, 8), lambda s: b("U", 8 + 8 * s, 16 + 8 * s), "v%d" % t, "lv%d" % t, b("U", 8, 32))
 
-    def prefix(x, add, ni, eb, tb, ec):
-        scan(sub(ni, 0, 8), x, add)
-        tr(tb, ni)
-        scan(sub(eb, 1, 33), tb, V("ZERO", 0, 32))
-        tr(ec, sub(eb, 0, 32))
-
     def choose_and_send(t):
         b = bufs(t)
         worse = zb(t, 112, 64)
@@ -451,75 +457,68 @@ def rank_program(g, core, T, topo):
         gat(b("WD", 0, 64), b("W", 0, 256), V("DUP", 0, 4))
         gata(b("WD", 64, 128), b("W", 0, 256), V("DUP", 4, 8))
         tr(b("TW"), b("WD"))
-        cols = {d: (4 * i, 4 * i + 4) for i, d in enumerate(others)}
         pf = "PF%d" % t
-        alone = me // 2 * 2 + 1 - me % 2
-        for d in [d for d in others if d != alone] + [alone]:
-            lo, hi = cols[d]
-            tt(blk(d, pf, lo, hi), blk(d, "TW%d" % t, 0, 128, 32), blk(d, "TW%d" % t, 16, 128, 32), A.add)
-            k = d // 2 * 2 + 1 - d % 2
-            if d == alone:
-                tt(blk(k, pf, lo, hi), blk(d, "TW%d" % t, 0, 128, 32), blk(d, "TW%d" % t, 16, 128, 32), A.add)
-            else:
-                act(blk(k, pf, lo, hi), blk(d, pf, lo, hi))
-        for half in (me // 2, 1 - me // 2):
-            own = [cols[d] for d in others if d // 2 == half]
-            lo, hi = min(own)[0], max(own)[1]
-            for h in (half, 1 - half):
-                tc(V("PO%d" % t, lo, hi, 1, 64 * h, 64 * h + 64), V(pf, lo, hi, 1, 64 * half, 64 * half + 64))
+        for i, d in enumerate(others):
+            tt(blk(me, pf, 4 * i, 4 * i + 4), blk(d, "TW%d" % t, 0, 128, 32), blk(d, "TW%d" % t, 16, 128, 32), A.add)
+        for k in range(4):
+            tc(blk(k, "PO%d" % t), blk(me, pf, 0, 12))
         pick(b("SQ"), b("SS"), V("QO%d" % (t - 1)), V("QS%d" % (t - 1)), b("PO"))
         each("SQ%d" % t, 64, "QW%d" % (t - 1), "c%d" % t, "lc%d" % t)
-        return each("SS%d" % t, 64, "QP%d" % (t - 1), "s%d" % t, "ls%d" % t, 3)
+        return each("SS%d" % t, 64, "QP%d" % (t - 1), "s%d" % t, "ls%d" % t, 1)
 
     def own_list(t):
         b = bufs(t)
         mk = lambda name, *a: blk(me, name + str(t), *a)
-        tt(b("M16"), b("U", 0, 16), b("U", 16, 32), A.max)
-        tt(b("MM"), b("M16", 0, 8), b("M16", 8, 16), A.max)
+        tt(mk("M16"), mk("U", 0, 16), mk("U", 16, 32), A.max)
+        tt(mk("MM"), mk("M16", 0, 8), mk("M16", 8, 16), A.max)
         for i in range(4):
-            tt(b("EQ", 8 * i, 8 * i + 8), b("U", 8 * i, 8 * i + 8), b("MM"), A.is_equal)
-        tt(b("KEY"), b("EQ"), b("KK"), A.mult)
-        tt(b("K16"), b("KEY", 0, 16), b("KEY", 16, 32), A.max)
-        tt(b("KM"), b("K16", 0, 8), b("K16", 8, 16), A.max)
-        wb, i2 = zb(t, 72, 8), zb(t, 0, 32)
+            tt(mk("EQ", 8 * i, 8 * i + 8), mk("U", 8 * i, 8 * i + 8), mk("MM"), A.is_equal)
+        tt(mk("KEY"), mk("EQ"), mk("KK"), A.mult)
+        tt(mk("K16"), mk("KEY", 0, 16), mk("KEY", 16, 32), A.max)
+        tt(mk("KM"), mk("K16", 0, 8), mk("K16", 8, 16), A.max)
+        wb, ic = zb(t, 0, 40), b("IC")
         for i, s in enumerate(others):
             tt(sub(wb, 0, 8, s), mk("KEY", 8 * i + 8, 8 * i + 16), mk("KM"), A.is_equal)
-        prefix(wb, V("ZERO", 0, 8), i2, zb(t, 32, 40), b("TB2"), b("EC2"))
-        lin(b("NW"), wb, -1000.0, 1000.0)
-        tt(b("NP"), sub(i2, 0, 8), b("NW"), A.add)
-        tt(b("BP"), sub(i2, 0, 8), b("OB"), A.add)
-        keep = b("VAL", 16, 24)
-        ts(keep, b("NP"), b("EC2", 7, 8), A.add, float(CAPP), A.is_le)
-        ts(b("SV"), b("BP"), b("EC2", 7, 8), A.add)
-        tt(b("VAL", 8, 16), keep, b("CG"), A.mult)
-        tt(b("VAL", 0, 8), keep, b("SV"), A.mult)
+        scan(ic, wb, V("ZERO", 0, 40))
+        tr(b("RC", 0, 32), sub(ic, 8, 40))
+        op("a", lambda: g.scalar.activation(ap(b("TJC", 0, 33)), ap(b("RC", 0, 33)), AF.Copy, scale=-1.0, accum_out=ap(b("TAC"))),
+           [b("RC", 0, 33)], [b("TJC", 0, 33), b("TAC")], 50)
+        scan(b("SFC"), b("RC", 0, 32), V("SUF"), A.add, A.mult)
+        lin(b("NW"), sub(wb, 0, 8), -1000.0, 1000.0)
+        tt(b("NP"), sub(ic, 0, 8), b("NW"), A.add)
+        tt(b("BP"), sub(ic, 0, 8), b("OB"), A.add)
+        ts(b("KP"), b("NP"), b("SFC", 31, 32), A.subtract, b("TAC"), A.is_le)
+        ts(b("SV"), b("BP"), b("SFC", 31, 32), A.subtract, b("TAC"), A.subtract)
         for i, s in enumerate(others):
-            lin(mk("BK", 24 * i, 24 * i + 24), blk(s, "VAL%d" % t))
-            lin(mk("KQ", 8 * i + 8, 8 * i + 16), mk("BK", 24 * i + 16, 24 * i + 24))
-        tt(mk("SA"), mk("BK", 0, 24), mk("BK", 24, 48), A.add)
-        tt(mk("SB"), mk("BK", 48, 56), mk("LCN"), A.add)
-        tt(mk("KS"), mk("SA", 16, 24), mk("BK", 64, 72), A.add)
-        tt(mk("XC"), mk("SA", 0, 8), mk("SB"), A.add)
-        lin(mk("KQ", 0, 8), mk("KS"), -1.0, 1.0)
+            tt(mk("BK", 8 * i, 8 * i + 8), blk(s, "KP%d" % t), blk(s, "SV%d" % t), A.mult)
+        tt(mk("SB"), mk("BK", 0, 8), mk("LCN"), A.add)
+        tt(mk("SA"), mk("BK", 8, 16), mk("BK", 16, 24), A.add)
+        tt(mk("XC"), mk("SA"), mk("SB"), A.add)
         for j in range(4):
             lin(mk("A2", 8 * j, 8 * j + 8), mk("XC"), scale=blk(me, "XEO", 4 * (j % 2), 4 * (j % 2) + 1))
         tr(mk("TA"), mk("A2"))
-        tt(mk("XT"), mk("TA", 0, 32, 2), mk("TA", 1, 32, 2), A.add)
         half = me // 2
         for k in (2 * half, 2 * half + 1):
-            tc(blk(k, "XO%d" % t), mk("XT"))
-        tc(V("XO%d" % t, p0=64 - 64 * half, p1=128 - 64 * half), V("XO%d" % t, p0=64 * half, p1=64 * half + 64))
-        tt(mk("PP"), mk("KQ"), mk("U"), A.mult)
-        tt(mk("P16"), mk("PP", 0, 16), mk("PP", 16, 32), A.add)
-        tt(mk("PA"), mk("P16", 0, 8), mk("P16", 8, 16), A.add)
+            tt(blk(k, "XT%d" % t), mk("TA", 0, 32, 2), mk("TA", 1, 32, 2), A.add)
+        for h in range(2):
+            tc(V("XO%d" % t, p0=64 * h, p1=64 * h + 64), V("XT%d" % t, p0=64 * half, p1=64 * half + 64))
+        ts(mk("KQ", 0, 8), mk("XC"), P - 0.5, A.is_lt)
+        ts(mk("KQ", 8, 16), mk("XC"), P - 0.5, A.is_gt)
+        tt(mk("PP", 0, 8), mk("KQ", 0, 8), mk("U", 0, 8), A.mult)
+        tt(mk("PP", 8, 16), mk("KQ", 8, 16), mk("MM"), A.mult)
+        tt(mk("PA"), mk("PP", 0, 8), mk("PP", 8, 16), A.add)
         pr = V("PR%d" % t, 0, 256, 1, 0, 1)
         dma("s", ap(pr), ap(mk("PA")), [mk("PA")], [pr])
-        op("g", lambda: g.partition_broadcast(ap(b("PB")), ap(pr), 128), [pr], [b("PB")], 1024)
+        if t == 1:
+            op("g", lambda: g.partition_broadcast(ap(b("PB")), ap(pr), 128), [pr], [b("PB")], 1024)
 
     def own_choice(t):
         mk = lambda name, *a: blk(me, name + str(t), *a)
-        tt(mk("CA"), mk("BK", 56, 64), mk("CO"), A.add)
-        tt(mk("CH"), mk("SA", 8, 16), mk("CA"), A.add)
+        for i, s in enumerate(others):
+            tt(mk("VAL", 8 * i, 8 * i + 8), blk(s, "KP%d" % t), blk(s, "CG%d" % t), A.mult)
+        tt(mk("CA"), mk("VAL", 0, 8), mk("CO"), A.add)
+        tt(mk("CB"), mk("VAL", 8, 16), mk("VAL", 16, 24), A.add)
+        tt(mk("CH"), mk("CB"), mk("CA"), A.add)
         dma("s", T.ch[t - 1:t, :], ap(mk("CH")), [mk("CH")], [])
 
     def products(t, i, arrived):
@@ -548,14 +547,19 @@ def rank_program(g, core, T, topo):
             if t == 2:
                 yp = mm(6 + f, 128, V("WQ"), V("WP"), V("QO2", lo, hi), V("QS2", lo, hi))
                 dma("s", T.oc[:, 4 * lo:4 * hi], ap(V("QO2", lo, hi)).bitcast(dt.uint8), [V("QO2", lo, hi)], [])
-                for k in range(4):
-                    sc = V("QS2", lo, hi, 1, 32 * k, 32 * k + 4)
-                    dma("s", T.osc[4 * k:4 * k + 4, lo:hi], ap(sc), [sc], [])
                 lin(V("YB", lo, hi), yp)
                 dma("a", T.y[:, lo:hi], ap(V("YB", lo, hi)), [V("YB", lo, hi)], [], dur=LOCAL + 0.6)
+        if t == 2:
+            for k in range(4):
+                sc = V("QS2", 0, P, 1, 32 * k, 32 * k + 4)
+                dma("s", T.osc[4 * k:4 * k + 4, :], ap(sc), [sc], [])
         hold[0] = (first,)
         for f in range(2):
-            tt(V("S%d" % t, 128 * f, 128 * f + 128), rs[f], b("PB", 128 * f, 128 * f + 128), A.add)
+            lo, hi = 128 * f, 128 * f + 128
+            if t == 1:
+                tt(V("S1", lo, hi), rs[f], V("PB1", lo, hi), A.add)
+            else:
+                tt(V("S2", lo, hi, 1, 0, 1), rs[f][:2] + (1,) + rs[f][3:], V("PR2", lo, hi, 1, 0, 1), A.add)
         hold[0] = ()
         if t == 2:
             row = V("S2", 0, 256, 1, 0, 1)
@@ -563,10 +567,8 @@ def rank_program(g, core, T, topo):
 
     prep_lists(1, "MSG1")
     sent = spread(V("MSG1"), lambda s: V("LM1", 8 * s, 8 * s + 8), "m1", "lm1", V("LM1"))
-    w = 4
-    while w < 512:
-        act(V("UT", w, 2 * w), V("UT", 0, w))
-        w *= 2
+    for i in range(4):
+        lin(V("UT", i, 512, 4), V("ZERO"), 1.0, V("UC", i, i + 1), "a")
     qz(V("UQ"), V("UP"), V("UT"))
     qz(V("QO0"), V("QS0"), V("E0"))
     act(V("S0"), mm(0, 256, V("UQ"), V("UP"), V("QO0"), V("QS0")))
@@ -575,15 +577,15 @@ def rank_program(g, core, T, topo):
     ts(V("KCOL", 0, 1), V("PF32", 5, 6), 0.0, A.is_equal, kcol, A.mult)
     prep_ties(1)
     prep_ties(2)
-    ties = spread(V("MSG2"), lambda s: V("LM2", 2 * s, 2 * s + 2), "m2", "lm2", V("LM2"))
-    load("s", V("AT", 0, 1024), T.a[:, 0:1024], LONG, [ties])
-    fills()
+    spread(V("MSG2"), lambda s: V("LM2", 2 * s, 2 * s + 2), "m2", "lm2", V("LM2"))
+    fill(V("IDT"), 0, 1)
     constants()
     hold[0] = ()
     for d in [me] + others:
         tc(blk(d, "LU1"), blk(me, "MSG1") if d == me else blk(me, "LM1", 8 * others.index(d), 8 * others.index(d) + 8))
     tc(blk(me, "LU2"), blk(me, "LS2"))
     scores = scores_out(1)
+    more_fills()
     load("s", V("AT", 1024, 2048), T.a[:, 1024:2048], LONG, [scores])
     load("s", V("E1"), T.e1[:], LONG, [scores])
     own_columns(1)
@@ -599,9 +601,10 @@ def rank_program(g, core, T, topo):
     each("ST2", 2, "LC2", "m3", "lm3")
     for i, d in enumerate(others):
         dma("s", ap(blk(d, "LU2")), ap(V("LC2", 2 * i, 2 * i + 2)), [V("LC2", 2 * i, 2 * i + 2)], [blk(d, "LU2")])
-    hold[0] = (sent,)
+    hold[0] = (sent - 2,)
     for i in range(4):
-        qz(V("AQ", 128 * i, 128 * i + 128), V("AP", 128 * i, 128 * i + 128), V("AT", 512 * i, 512 * i + 512))
+        j = qz(V("AQ", 128 * i, 128 * i + 128), V("AP", 128 * i, 128 * i + 128), V("AT", 512 * i, 512 * i + 512))
+        nodes[j]["more"] = 2.5 - 0.4 * i
         products(1, i, False)
     hold[0] = ()
     own_list(1)
@@ -615,7 +618,6 @@ def rank_program(g, core, T, topo):
     thresholds(2)
     for i in range(4):
         products(2, i, False)
-    ms(V("W2", 0, 256), 0.0)
     own_columns(2)
     own_choice(1)
     hold[0] = ()

@@ -5,7 +5,7 @@ P, CAPP = 256, 64
 TINY = 2.0 ** -100
 STEP = 2.0 ** -24 * (1 + 2.0 ** -10)
 BIG = 1.5 * 2.0 ** 25
-WAIT, LEAST, ISSUE, WAY, ONCE = 0.16, 0.09, 0.8, 2.8, 1.5
+WAIT, LEAST, ISSUE, WAY, ONCE = 0.2, 0.09, 0.8, 2.8, 1.5
 LOCAL, FIRST, LONG = 2.3, 3.8, 5.5
 F, B, I, H, C, S8 = "float32", "bfloat16", "int32", "uint16", "float8_e4m3fn_x4", "uint8"
 SCRATCH = {"PS": ("psum", [128, 4096], F)}
@@ -309,12 +309,16 @@ def rank_program(g, core, T, topo):
     def bufs(t):
         return lambda name, *a: V(name + str(t), *a)
 
-    for i in range(8):
-        load("sa"[i % 2], V("RAW1", p0=16 * i, p1=16 * i + 16), T.p1[:], LOCAL)
+    ms(V("RAW1"), 0)
+    for i in range(4):
+        raw = load("sa"[i % 2], V("RAW1", p0=32 * i, p1=32 * i + 16), T.p1[:], LOCAL)
+    hold[0] = (raw - 1, raw)
     load("s", V("E0", 0, 512), T.e0[:, 0:512], FIRST)
     load("a", V("UC"), T.u[:, 0:4], FIRST)
     load("a", V("E0", 512, 1024), T.e0[:, 512:1024], FIRST)
+    hold[0] = ()
     ms(V("RAW2"), 0)
+    hold[0] = (raw - 1, raw)
     for i in range(4):
         raw = load("s", V("RAW2", p0=32 * i, p1=32 * i + 16), T.p2[:], FIRST)
     hold[0] = (raw,)
@@ -546,13 +550,13 @@ def rank_program(g, core, T, topo):
             rs[f] = mm(4 + f, 128, V("UQ"), V("UP"), V("QO%d" % t, lo, hi), V("QS%d" % t, lo, hi))
             if t == 2:
                 yp = mm(6 + f, 128, V("WQ"), V("WP"), V("QO2", lo, hi), V("QS2", lo, hi))
-                dma("s", T.oc[:, 4 * lo:4 * hi], ap(V("QO2", lo, hi)).bitcast(dt.uint8), [V("QO2", lo, hi)], [])
                 lin(V("YB", lo, hi), yp)
-                dma("a", T.y[:, lo:hi], ap(V("YB", lo, hi)), [V("YB", lo, hi)], [], dur=LOCAL + 0.6)
         if t == 2:
+            dma("s", T.oc[:], ap(V("QO2")).bitcast(dt.uint8), [V("QO2")], [], dur=LOCAL + 0.6)
+            dma("a", T.y[:], ap(V("YB")), [V("YB")], [], dur=LOCAL + 0.6)
             for k in range(4):
                 sc = V("QS2", 0, P, 1, 32 * k, 32 * k + 4)
-                dma("s", T.osc[4 * k:4 * k + 4, :], ap(sc), [sc], [])
+                dma("sa"[k == 3], T.osc[4 * k:4 * k + 4, :], ap(sc), [sc], [])
         hold[0] = (first,)
         for f in range(2):
             lo, hi = 128 * f, 128 * f + 128

@@ -34,13 +34,13 @@ _buf(B, UC=4, UT=512, E0=1024, AT=2048, WT=512, E1=1024, E2=1024, HT1=1024, HT2=
 _buf(C, UQ=128, AQ=512, WQ=128, QO0=256, QO1=256, QO2=256, QW0=192, QW1=192, SQ1=192, SQ2=192)
 _buf(S8, UP=128, AP=512, WP=128, QS0=256, QS1=256, QS2=256, QP0=192, QP1=192, SS1=192, SS2=192)
 _buf(H, MSG1=8, MSG2=2, LM1=24, LM2=6, LS2=8, ST2=6, LC2=6, LU1=8, LU2=8)
-_buf(F, ZERO=128, U1=32, U2=32, Z1=1792, Z2=1792, YB=256, S0=256, S1=256, S2=256, PR1=256, PR2=256, PB1=256)
-_buf(I, RAW1=64, RAW2=64)
+_buf(F, ZERO=128, U1=32, U2=32, Z1=1792, Z2=1792, YB=256, S0=448, S1=256, S2=256, PR2=256, PB1=256)
+_buf(I, RAW=64)
 _area(H, DUP=8, PERM=2, PV=2)
 _area(I, PI=1, PJ=8, DUPI=8, PERMI=2, KC=8, KD=64)
 _area(F, BAR=64, SEGT=40, KCOL=4, SL=4, XEO=8, GD=4, BC=4, TR=8, ZB=416, PF32=8, J4=64, SEG4=64, J16=128, MASK=128,
-      SEG16=128, SUF=32, J32=32, IDT=256, PKC=16, KF=64)
-_area(F, **_each(RL=64, T2=64, SCL=64, EQN=64, KQN=64, TK=64, SK=64, PK=16, LCN=8, OL=8, OB=8, CD=8, CG=8,
+      SEG16=128, SUF=32, J32=32, IDT=256, PKC=16, KF=64, RL=64, T2=64, SCL=64, EQN=64, KQN=64, TK=64, SK=64, PK=16)
+_area(F, **_each(LCN=8, OL=8, OB=8, CD=8, CG=8,
                  VR=128, KK=32, G=128, SG=128, V4=32, AB=32, AC=32, DE=32, VA=32, BT=40, NI=64, RT=40, TJ=40, TA1=1, SFX=32,
                  AA=8, W=6208, WD=128, TW=128, PF=16, M16=16, MM=8, EQ=32, KEY=32, K16=16, KM=8,
                  IC=40, RC=40, TJC=40, TAC=1, SFC=32, KP=8, CB=8, SV=8,
@@ -224,7 +224,7 @@ def rank_program(g, core, T, topo):
         op("v", lambda: g.vector.transpose(ap(o), ap(a)), [a], [o], width(a))
 
     def ms(o, c):
-        op("v", lambda: g.vector.memset(ap(o), c), [], [o], width(o))
+        lin(o, ("ZERO",) + o[1:3] + (0, width(o), 1), 1.0, c, "a")
 
     def fill(o, base, step=0, rise=0, pattern=None):
         n = width(o)
@@ -309,39 +309,32 @@ def rank_program(g, core, T, topo):
     def bufs(t):
         return lambda name, *a: V(name + str(t), *a)
 
-    ms(V("RAW1"), 0)
-    for i in range(4):
-        raw = load("sa"[i % 2], V("RAW1", p0=32 * i, p1=32 * i + 16), T.p1[:], LOCAL)
+    for i in range(8):
+        raw = load("sa"[i % 2], V("RAW", p0=16 * i, p1=16 * i + 16), (T.p1, T.p2)[i % 2][:], LOCAL)
     hold[0] = (raw - 1, raw)
     load("s", V("E0", 0, 512), T.e0[:, 0:512], FIRST)
     load("a", V("UC"), T.u[:, 0:4], FIRST)
     load("a", V("E0", 512, 1024), T.e0[:, 512:1024], FIRST)
-    hold[0] = ()
-    ms(V("RAW2"), 0)
-    hold[0] = (raw - 1, raw)
-    for i in range(4):
-        raw = load("s", V("RAW2", p0=32 * i, p1=32 * i + 16), T.p2[:], FIRST)
-    hold[0] = (raw,)
     load("s", V("AT", 0, 1024), T.a[:, 0:1024], LONG)
     hold[0] = ()
     op("g", lambda: g.iota(ap(V("PI")), [[0, 1]], 0, 1), [], [V("PI")], 100)
     fill(V("J4"), 0, pattern=[[0, 16], [1, 4]])
+    fill(V("ZERO"), 0)
     fill(V("J16"), 0, pattern=[[0, 8], [1, 16]])
-    for j, m in enumerate((15, 3, 1, 96, 31, 16)):
+    for j, m in enumerate((15, 3, 1, 96, 31)):
         ts(V("PJ", j, j + 1), V("PI"), m, A.bitwise_and)
-    ts(V("PJ", 6, 7), V("PI"), 2, A.logical_shift_right, 3, A.bitwise_and)
-    tc(V("PF32", 0, 7), V("PJ", 0, 7))
-    p15, kcol, p31, p4 = V("PF32", 0, 1), V("PF32", 1, 2), V("PF32", 4, 5), V("PF32", 6, 7)
+    ts(V("PJ", 5, 6), V("PI"), 2, A.logical_shift_right, 3, A.bitwise_and)
+    tc(V("PF32", 0, 6), V("PJ", 0, 6))
+    p15, kcol, p31, p4 = V("PF32", 0, 1), V("PF32", 1, 2), V("PF32", 4, 5), V("PF32", 5, 6)
     ts(V("SL", 0, 1), V("PJ", 3, 4), 8.0, A.mult, -0.5, A.add)
     ts(V("SL", 1, 2), V("PJ", 3, 4), 8.0, A.mult, P - 0.5, A.add)
     ts(V("SL", 2, 3), V("PJ", 3, 4), 24.0, A.mult, 3 * (P - 0.5), A.add)
     ts(V("SEG4"), V("J4"), 1.0, A.min)
-    fill(V("PKC"), 4, pattern=[[0, 2], [-3, 2], [0, 4]])
+    act(V("PKC"), V("SEG4", 0, 16), 4.0)
     op("g", lambda: g.iota(ap(V("DUPI")), [[64, 4], [0, 2]], 0, 0), [], [V("DUPI")], 100)
     op("g", lambda: g.iota(ap(V("PERMI")), [[4, 2]], 0, 0), [], [V("PERMI")], 100)
     fill(V("J32"), 0, 1)
     fill(V("TR"), 1028, 4, 32)
-    fill(V("ZERO"), 0)
     for k in range(4):
         ms(blk(k, "BC", 0, 1), float(255 + CAPP + 64 * others.index(k)) if k != me else 0.0)
     ms(V("BAR"), 0.0)
@@ -369,32 +362,34 @@ def rank_program(g, core, T, topo):
         ts(V("MASK"), V("J16"), p15, A.is_equal)
         ts(V("SEG16"), V("J16"), 1.0, A.min)
         ts(V("SUF"), V("J32"), p31, A.is_ge)
-        ts(V("KCOL", 1, 2), kcol, 8.0, A.mult, p4, A.add)
-        ts(V("KCOL", 2, 3), p15, 4.0, A.mult)
+        lin(V("KCOL", 1, 2), kcol, 8.0, p4, "a")
+        act(V("KCOL", 2, 3), p15, 4.0)
         ts(V("DUP"), V("DUPI"), V("KCOL", 2, 3), A.add)
         ts(V("PERM"), V("PERMI"), V("KCOL", 1, 2), A.add)
         ts(V("PV"), V("PERMI"), p4, A.add)
 
-    def prep_lists(t, out):
-        b = bufs(t)
+    def prep_lists():
         for h in range(2):
-            ts(b("RL", 32 * h, 32 * h + 32), V("RAW%d" % t, h, 64, 2), V("SL", 0, 1), A.max, V("SL", 1, 2), A.min)
+            ts(V("RL", 32 * h, 32 * h + 32), V("RAW", h, 64, 2), V("SL", 0, 1), A.max, V("SL", 1, 2), A.min)
         for h in range(2):
-            tr(b("T2", 32 * h, 32 * h + 32), b("RL", 32 * h, 32 * h + 32))
+            tr(V("T2", 32 * h, 32 * h + 32), V("RL", 32 * h, 32 * h + 32))
         for h in range(2):
-            scan(b("SCL", 32 * h, 32 * h + 32), V("SEG4", 0, 32), b("T2", 32 * h, 32 * h + 32), A.mult, A.add)
-        for h in range(2):
-            ts(V(out, 4 * h, 4 * h + 4), b("SCL", 32 * h + 3, 32 * h + 16, 4), V("SL", 2, 3), A.subtract)
+            scan(V("SCL", 32 * h, 32 * h + 32), V("SEG4", 0, 32), V("T2", 32 * h, 32 * h + 32), A.mult, A.add)
 
-    def prep_ties(t):
-        b = bufs(t)
+    def list_of(t, out):
         for h in range(2):
-            tt(b("EQN", 32 * h, 32 * h + 32), b("RL", 32 * h, 32 * h + 32), V("RAW%d" % t, h, 64, 2), A.is_equal)
-        lin(b("KQN"), b("EQN"), scale=V("KCOL", 0, 1))
-        tr(b("TK"), b("KQN"))
-        scan(b("SK"), V("SEG4"), b("TK"), A.mult, A.add)
-        scan(b("PK"), V("PKC"), b("SK", 3, 64, 4), A.mult, A.add)
-        tc(V("MSG2", t - 1, t), b("PK", 15, 16))
+            o = 32 * h + 16 * (t - 1)
+            ts(V(out, 4 * h, 4 * h + 4), V("SCL", o + 3, o + 16, 4), V("SL", 2, 3), A.subtract)
+
+    def prep_ties():
+        for h in range(2):
+            tt(V("EQN", 32 * h, 32 * h + 32), V("RL", 32 * h, 32 * h + 32), V("RAW", h, 64, 2), A.is_equal)
+        lin(V("KQN"), V("EQN"), scale=kcol)
+        tr(V("TK"), V("KQN"))
+        scan(V("SK"), V("SEG4"), V("TK"), A.mult, A.add)
+        scan(V("PK"), V("PKC"), V("SK", 3, 64, 4), A.mult, A.add)
+        for j in range(2):
+            ts(V("MSG2", j, j + 1), V("PK", 4 * j + 3, 4 * j + 4), 256.0, A.mult, V("PK", 4 * j + 11, 4 * j + 12), A.add)
 
     def own_columns(t):
         b = bufs(t)
@@ -440,7 +435,7 @@ def rank_program(g, core, T, topo):
 
     def scores_out(t):
         b = bufs(t)
-        tti(b("G"), V("S%d" % (t - 1)), b("LU"), V("MASK"), A.mult)
+        tti(b("G"), V("S%d" % (t - 1), 0, P), b("LU"), V("MASK"), A.mult)
         scan(b("SG"), V("SEG16"), b("G"), A.mult, A.add)
         lin(b("U", 0, 8), b("SG", 15, 128, 16))
         return spread(b("U", 0, 8), lambda s: b("U", 8 + 8 * s, 16 + 8 * s), "v%d" % t, "lv%d" % t, b("U", 8, 32))
@@ -506,15 +501,14 @@ def rank_program(g, core, T, topo):
             tt(blk(k, "XT%d" % t), mk("TA", 0, 32, 2), mk("TA", 1, 32, 2), A.add)
         for h in range(2):
             tc(V("XO%d" % t, p0=64 * h, p1=64 * h + 64), V("XT%d" % t, p0=64 * half, p1=64 * half + 64))
-        ts(mk("KQ", 0, 8), mk("XC"), P - 0.5, A.is_lt)
-        ts(mk("KQ", 8, 16), mk("XC"), P - 0.5, A.is_gt)
-        tt(mk("PP", 0, 8), mk("KQ", 0, 8), mk("U", 0, 8), A.mult)
-        tt(mk("PP", 8, 16), mk("KQ", 8, 16), mk("MM"), A.mult)
-        tt(mk("PA"), mk("PP", 0, 8), mk("PP", 8, 16), A.add)
-        pr = V("PR%d" % t, 0, 256, 1, 0, 1)
-        dma("s", ap(pr), ap(mk("PA")), [mk("PA")], [pr])
-        if t == 1:
-            op("g", lambda: g.partition_broadcast(ap(b("PB")), ap(pr), 128), [pr], [b("PB")], 1024)
+        if t == 2:
+            ts(mk("KQ", 0, 8), mk("XC"), P - 0.5, A.is_lt)
+            ts(mk("KQ", 8, 16), mk("XC"), P - 0.5, A.is_gt)
+            tt(mk("PP", 0, 8), mk("KQ", 0, 8), mk("U", 0, 8), A.mult)
+            tt(mk("PP", 8, 16), mk("KQ", 8, 16), mk("MM"), A.mult)
+            tt(mk("PA"), mk("PP", 0, 8), mk("PP", 8, 16), A.add)
+            pr = V("PR2", 0, 256, 1, 0, 1)
+            dma("s", ap(pr), ap(mk("PA")), [mk("PA")], [pr])
 
     def own_choice(t):
         mk = lambda name, *a: blk(me, name + str(t), *a)
@@ -534,6 +528,9 @@ def rank_program(g, core, T, topo):
         b = bufs(t)
         for i in range(4):
             products(t, i, True)
+        if t == 1:
+            act(V("S0", P, 448), mm(6, 192, V("UQ"), V("UP"), V("QW0"), V("QP0")))
+            gata(V("PB1"), V("S0"), b("XO"))
         rs, first, wide = {}, None, 3
 
         def choose(i, lo, hi):
@@ -547,10 +544,11 @@ def rank_program(g, core, T, topo):
         for f in range(2):
             lo, hi = 128 * f, 128 * f + 128
             first = qz(V("QO%d" % t, lo, hi), V("QS%d" % t, lo, hi), b("HT", 512 * f, 512 * f + 512))
-            rs[f] = mm(4 + f, 128, V("UQ"), V("UP"), V("QO%d" % t, lo, hi), V("QS%d" % t, lo, hi))
             if t == 2:
                 yp = mm(6 + f, 128, V("WQ"), V("WP"), V("QO2", lo, hi), V("QS2", lo, hi))
                 lin(V("YB", lo, hi), yp)
+                nodes[-1]["more"] = 0.3
+            rs[f] = mm(4 + f, 128, V("UQ"), V("UP"), V("QO%d" % t, lo, hi), V("QS%d" % t, lo, hi))
         if t == 2:
             dma("s", T.oc[:], ap(V("QO2")).bitcast(dt.uint8), [V("QO2")], [], dur=LOCAL + 0.6)
             dma("a", T.y[:], ap(V("YB")), [V("YB")], [], dur=LOCAL + 0.6)
@@ -569,18 +567,17 @@ def rank_program(g, core, T, topo):
             row = V("S2", 0, 256, 1, 0, 1)
             dma("s", T.g[:], ap(row), [row], [])
 
-    prep_lists(1, "MSG1")
+    prep_lists()
+    list_of(1, "MSG1")
     sent = spread(V("MSG1"), lambda s: V("LM1", 8 * s, 8 * s + 8), "m1", "lm1", V("LM1"))
     for i in range(4):
         lin(V("UT", i, 512, 4), V("ZERO"), 1.0, V("UC", i, i + 1), "a")
     qz(V("UQ"), V("UP"), V("UT"))
     qz(V("QO0"), V("QS0"), V("E0"))
-    act(V("S0"), mm(0, 256, V("UQ"), V("UP"), V("QO0"), V("QS0")))
-    prep_lists(2, "LS2")
+    act(V("S0", 0, P), mm(0, 256, V("UQ"), V("UP"), V("QO0"), V("QS0")))
     hold[0] = (sent,)
-    ts(V("KCOL", 0, 1), V("PF32", 5, 6), 0.0, A.is_equal, kcol, A.mult)
-    prep_ties(1)
-    prep_ties(2)
+    list_of(2, "LS2")
+    prep_ties()
     spread(V("MSG2"), lambda s: V("LM2", 2 * s, 2 * s + 2), "m2", "lm2", V("LM2"))
     fill(V("IDT"), 0, 1)
     constants()

@@ -36,16 +36,15 @@ _buf(S8, UP=128, AP=512, WP=128, QS0=256, QS1=256, QS2=256, QP0=192, QP1=192, SS
 _buf(H, MSG1=8, MSG2=2, LM1=24, LM2=6, LS2=8, ST2=6, LC2=6, LU1=8, LU2=8)
 _buf(F, ZERO=128, U1=32, U2=32, Z1=1792, Z2=1792, YB=256, S0=448, S1=256, S2=256, PR2=256, PB1=256)
 _buf(I, RAW=64)
-_area(H, DUP=8, PERM=2, PV=2)
+_area(H, DUP=8, PERM=2, PV=2, P8=2, XA=2, DO=2, KO=2)
 _area(I, PI=1, PJ=8, DUPI=8, PERMI=2, KC=8, KD=64)
-_area(F, BAR=64, SEGT=40, KCOL=4, SL=4, XEO=8, GD=4, BC=4, TR=8, ZB=416, PF32=8, J4=64, SEG4=64, J16=128, MASK=128,
-      SEG16=128, SUF=32, J32=32, IDT=256, PKC=16, KF=64, RL=64, T2=64, SCL=64, EQN=64, KQN=64, TK=64, SK=64, PK=16)
+_area(F, BAR=64, SEGT=40, KCOL=8, SL=4, XM=32, XI=32, GD=4, BC=4, TR=8, ZB=416, PF32=8, J4=64, SEG4=64, J16=128, MASK=128,
+      SEG16=128, SUF=32, J32=32, IDT=256, PKC=16, KW=8, FL=64, RL=64, T2=64, SCL=64, EQN=64, KQN=64, TK=64, SK=64, PK=16)
 _area(F, **_each(LCN=8, OL=8, OB=8, CD=8, CG=8,
                  VR=128, KK=32, G=128, SG=128, V4=32, AB=32, AC=32, DE=32, VA=32, BT=40, NI=64, RT=40, TJ=40, TA1=1, SFX=32,
                  AA=8, W=6208, WD=128, TW=128, PF=16, M16=16, MM=8, EQ=32, KEY=32, K16=16, KM=8,
-                 IC=40, RC=40, TJC=40, TAC=1, SFC=32, KP=8, CB=8, SV=8,
-                 NW=8, NP=8, BP=8, VAL=24, BK=24, SA=8, SB=8, CA=8, CO=8, CH=8, XC=8, A2=32, TA=32, XT=16, KQ=16, PP=16,
-                 PA=8))
+                 IC=40, RC=40, TJC=40, TAC=1, SFC=32, KP=8, SV=8,
+                 NW=8, NP=8, BP=8, VAL=32, CS=32, CH=8, XS=32, A2=32, TA=32, XT=16, KQ=16, PP=16, PA=8))
 _area(H, **_each(OF=8, PO=12, XO=16))
 NDMA = 60
 SEMAPHORES = ["qv", "qa", "qt", "qg", "m1", "lm1", "m2", "lm2", "m3", "lm3"] + ["d%d" % i for i in range(NDMA)] + [
@@ -321,11 +320,12 @@ def rank_program(g, core, T, topo):
     fill(V("J4"), 0, pattern=[[0, 16], [1, 4]])
     fill(V("ZERO"), 0)
     fill(V("J16"), 0, pattern=[[0, 8], [1, 16]])
-    for j, m in enumerate((15, 3, 1, 96, 31)):
+    for j, m in enumerate((15, 3, 1, 96, 31, 7)):
         ts(V("PJ", j, j + 1), V("PI"), m, A.bitwise_and)
-    ts(V("PJ", 5, 6), V("PI"), 2, A.logical_shift_right, 3, A.bitwise_and)
-    tc(V("PF32", 0, 6), V("PJ", 0, 6))
-    p15, kcol, p31, p4 = V("PF32", 0, 1), V("PF32", 1, 2), V("PF32", 4, 5), V("PF32", 5, 6)
+    ts(V("PJ", 6, 7), V("PI"), 2, A.logical_shift_right, 3, A.bitwise_and)
+    ts(V("PJ", 7, 8), V("PI"), 3, A.logical_shift_right, 1, A.bitwise_and)
+    tc(V("PF32"), V("PJ"))
+    p15, kcol, odd, p96, p31, p7, p4, p8 = [V("PF32", j, j + 1) for j in range(8)]
     ts(V("SL", 0, 1), V("PJ", 3, 4), 8.0, A.mult, -0.5, A.add)
     ts(V("SL", 1, 2), V("PJ", 3, 4), 8.0, A.mult, P - 0.5, A.add)
     ts(V("SL", 2, 3), V("PJ", 3, 4), 24.0, A.mult, 3 * (P - 0.5), A.add)
@@ -341,15 +341,14 @@ def rank_program(g, core, T, topo):
     ms(V("BAR", 4, 33, 4), -BIG - 4.0)
     ms(V("BAR", 1, 32, 4), 1.5)
     ms(V("BAR", 3, 32, 4), BIG)
-    act(V("XEO", 4, 5), V("PF32", 2, 3))
-    lin(V("XEO", 0, 1), V("PF32", 2, 3), -1.0, 1.0, "a")
-    lin(V("GD", 0, 1), V("PF32", 3, 4), 8.0, float(-P * me), "a")
+    lin(V("GD", 0, 1), p96, 8.0, float(-P * me), "a")
 
     def more_fills():
         fill(V("RT1", 32, 40), 4)
         fill(V("W1", 0, 256), 0)
+        fill(V("XI"), 0, pattern=[[0, 2], [1, 2], [0, 8]])
+        ts(V("XM"), V("XI"), odd, A.is_equal)
         for t in (1, 2):
-            fill(V("KK%d" % t, 0, 8), 4)
             fill(V("RC%d" % t, 32, 40), -CAPP)
         fill(V("RT2", 32, 40), 4)
         fill(V("W2", 0, 256), 0)
@@ -357,16 +356,26 @@ def rank_program(g, core, T, topo):
     def constants():
         for c in range(0, 416, 104):
             ms(V("ZB", c, c + 104), 0.0)
+        ms(V("FL", 0, 64, 4), 0.0)
         ts(V("SEGT"), V("J4", 0, 40), 1.5, A.is_gt)
         lin(V("SEGT", 4, 33, 4), V("TR"))
         ts(V("MASK"), V("J16"), p15, A.is_equal)
         ts(V("SEG16"), V("J16"), 1.0, A.min)
         ts(V("SUF"), V("J32"), p31, A.is_ge)
-        lin(V("KCOL", 1, 2), kcol, 8.0, p4, "a")
-        act(V("KCOL", 2, 3), p15, 4.0)
-        ts(V("DUP"), V("DUPI"), V("KCOL", 2, 3), A.add)
-        ts(V("PERM"), V("PERMI"), V("KCOL", 1, 2), A.add)
+        kc = [V("KCOL", j, j + 1) for j in range(8)]
+        lin(kc[1], kcol, 8.0, p4, "a")
+        act(kc[2], p15, 4.0)
+        lin(kc[3], p4, 8.0, kcol, "a")
+        lin(kc[4], p4, 3.0, kc[1], "a")
+        lin(kc[5], p8, -7.0, kc[4], "a")
+        lin(kc[6], p7, 4.0, 3.0, "a")
+        ts(V("DUP"), V("DUPI"), kc[2], A.add)
+        ts(V("PERM"), V("PERMI"), kc[1], A.add)
         ts(V("PV"), V("PERMI"), p4, A.add)
+        ts(V("P8"), V("ZERO", 0, 2), p7, A.add)
+        ts(V("XA"), V("ZERO", 0, 2), kc[6], A.add)
+        ts(V("DO"), V("J32", 0, 2), 4.0, A.mult, kc[3], A.add)
+        ts(V("KO"), V("J32", 0, 2), 2.0, A.mult, kc[5], A.add)
 
     def prep_lists():
         for h in range(2):
@@ -388,49 +397,51 @@ def rank_program(g, core, T, topo):
         tr(V("TK"), V("KQN"))
         scan(V("SK"), V("SEG4"), V("TK"), A.mult, A.add)
         scan(V("PK"), V("PKC"), V("SK", 3, 64, 4), A.mult, A.add)
-        for j in range(2):
-            ts(V("MSG2", j, j + 1), V("PK", 4 * j + 3, 4 * j + 4), 256.0, A.mult, V("PK", 4 * j + 11, 4 * j + 12), A.add)
+        for h in range(2):
+            ts(V("MSG2", h, h + 1), V("PK", 8 * h + 3, 8 * h + 4), 256.0, A.mult, V("PK", 8 * h + 7, 8 * h + 8), A.add)
 
     def own_columns(t):
         b = bufs(t)
         tc(b("LCN"), V("MSG1") if t == 1 else V("LS2"))
         for k in [me] + others:
             act(blk(k, "OL%d" % t), blk(me, "LCN%d" % t))
-        lin(blk(me, "CO%d" % t), blk(me, "LCN%d" % t), bias=float(P * me))
-        lin(b("OB"), b("OL"), -1.0, V("BC", 0, 1))
-        tt(b("CD"), b("LCN"), b("OL"), A.subtract)
-        lin(b("CG"), b("CD"), bias=V("GD", 0, 1))
+        act(sub(zb(t, 80, 32), 3, 32, me, 4), blk(me, "LCN%d" % t))
+        lin(blk(me, "VAL%d" % t, 3, 32, 4), blk(me, "LCN%d" % t), 1.0, float(P * me), "a")
+        lin(b("OB"), b("OL"), -1.0, V("BC", 0, 1), "a")
 
     def decode_ties():
-        tc(V("KC", 0, 6), V("LM2"))
-        tc(V("KC", 6, 8), V("MSG2"))
-        for c in range(8):
-            ts(V("KD", c, 64, 8), V("KC"), 2 * (7 - c), A.logical_shift_right, 3, A.bitwise_and)
-        tc(V("KF"), V("KD"))
-        ka = zb(0, 0, 64)
+        ka = zb(0, 0, 8)
+        tc(V("KW", 6, 8), V("MSG2"))
+        for s in others:
+            act(sub(ka, (s - me) % 4, 8, me, 4), blk(s, "KW", 6, 8))
+        tc(V("KW", 0, 6), V("LM2"))
         for j, d in enumerate(others):
             for s in range(4):
                 if s != d:
-                    i = (s - me) % 4
-                    lin(sub(ka, 16 * i, 16 * i + 16, d), blk(s, "KF", 16 * j, 16 * j + 16))
+                    act(sub(ka, (s - me) % 4, 8, d, 4), blk(s, "KW", 2 * j, 2 * j + 2))
+        tc(V("KC"), ka)
 
-    def tie_flags(t):
-        ka, o = zb(0, 0, 64), 8 * (t - 1)
+    def digits(t):
+        o = 32 * t - 32
+        for c in range(4 * t - 4, 4 * t):
+            ts(V("KD", 8 * c, 8 * c + 8), V("KC"), 2 * (7 - c), A.logical_shift_right, 3, A.bitwise_and)
         for i in range(1, 4):
-            tt(sub(zb(t, 80, 32), i, 32, None, 4), sub(ka, 16 * i + o, 16 * i + o + 8), sub(ka, o, o + 8), A.is_lt)
-        for i, s in enumerate(others):
-            lin(blk(me, "KK%d" % t, 8 * i + 8, 8 * i + 16), blk(s, "KF", 48 + o, 56 + o), -1.0, 4.0)
+            tt(V("FL", o + i, o + 32, 4), V("KD", o + i, o + 32, 4), V("KD", o, o + 32, 4), A.is_lt)
+
+    def own_keys(t):
+        o, w, off = V("KK%d" % t), V("KD", 32 * t - 32, 32 * t), V("KO")
+        op("v", lambda: g.vector.tensor_scalar(ap(o), ap(w).indirect(ap(off)), -1.0, 4.0, A.mult, A.add), [w, off], [o], 100)
 
     def value_rows(t):
         b = bufs(t)
         gata(b("V4"), b("U", 0, 8), V("PV"))
         op("a", lambda: g.scalar.activation(ap(b("AB")), ap(b("V4")), AF.Abs, scale=STEP), [b("V4")], [b("AB")], 32)
+        ts(b("AC"), b("AB"), TINY, A.add)
         gata(b("VR"), V("IDT"), b("LU"))
 
     def thresholds(t):
         b = bufs(t)
-        ts(b("AC"), b("AB"), TINY, A.add)
-        tt(b("DE"), b("AC"), zb(t, 80, 32), A.mult)
+        tti(b("DE"), V("FL", 32 * t - 32, 32 * t), V("DO"), b("AC"), A.mult)
         tt(b("VA"), b("V4"), b("DE"), A.subtract)
 
     def scores_out(t):
@@ -468,14 +479,13 @@ def rank_program(g, core, T, topo):
     def own_list(t):
         b = bufs(t)
         mk = lambda name, *a: blk(me, name + str(t), *a)
-        tt(mk("M16"), mk("U", 0, 16), mk("U", 16, 32), A.max)
-        tt(mk("MM"), mk("M16", 0, 8), mk("M16", 8, 16), A.max)
-        for i in range(4):
-            tt(mk("EQ", 8 * i, 8 * i + 8), mk("U", 8 * i, 8 * i + 8), mk("MM"), A.is_equal)
+        tt(b("M16"), b("U", 0, 16), b("U", 16, 32), A.max)
+        tt(b("MM"), b("M16", 0, 8), b("M16", 8, 16), A.max)
+        tti(b("EQ"), b("MM"), V("P8"), b("U"), A.is_equal)
         tt(mk("KEY"), mk("EQ"), mk("KK"), A.mult)
         tt(mk("K16"), mk("KEY", 0, 16), mk("KEY", 16, 32), A.max)
         tt(mk("KM"), mk("K16", 0, 8), mk("K16", 8, 16), A.max)
-        wb, ic = zb(t, 0, 40), b("IC")
+        wb, ic, bk = zb(t, 0, 40), b("IC"), zb(t, 80, 32)
         for i, s in enumerate(others):
             tt(sub(wb, 0, 8, s), mk("KEY", 8 * i + 8, 8 * i + 16), mk("KM"), A.is_equal)
         scan(ic, wb, V("ZERO", 0, 40))
@@ -489,12 +499,9 @@ def rank_program(g, core, T, topo):
         ts(b("KP"), b("NP"), b("SFC", 31, 32), A.subtract, b("TAC"), A.is_le)
         ts(b("SV"), b("BP"), b("SFC", 31, 32), A.subtract, b("TAC"), A.subtract)
         for i, s in enumerate(others):
-            tt(mk("BK", 8 * i, 8 * i + 8), blk(s, "KP%d" % t), blk(s, "SV%d" % t), A.mult)
-        tt(mk("SB"), mk("BK", 0, 8), mk("LCN"), A.add)
-        tt(mk("SA"), mk("BK", 8, 16), mk("BK", 16, 24), A.add)
-        tt(mk("XC"), mk("SA"), mk("SB"), A.add)
-        for j in range(4):
-            lin(mk("A2", 8 * j, 8 * j + 8), mk("XC"), scale=blk(me, "XEO", 4 * (j % 2), 4 * (j % 2) + 1))
+            tt(sub(bk, i, 32, me, 4), blk(s, "KP%d" % t), blk(s, "SV%d" % t), A.mult)
+        scan(b("XS"), V("SEG4", 0, 32), bk, A.mult, A.add)
+        tti(b("A2"), b("XS"), V("XA"), V("XM"), A.mult)
         tr(mk("TA"), mk("A2"))
         half = me // 2
         for k in (2 * half, 2 * half + 1):
@@ -502,8 +509,8 @@ def rank_program(g, core, T, topo):
         for h in range(2):
             tc(V("XO%d" % t, p0=64 * h, p1=64 * h + 64), V("XT%d" % t, p0=64 * half, p1=64 * half + 64))
         if t == 2:
-            ts(mk("KQ", 0, 8), mk("XC"), P - 0.5, A.is_lt)
-            ts(mk("KQ", 8, 16), mk("XC"), P - 0.5, A.is_gt)
+            ts(mk("KQ", 0, 8), mk("XS", 3, 32, 4), P - 0.5, A.is_lt)
+            ts(mk("KQ", 8, 16), mk("XS", 3, 32, 4), P - 0.5, A.is_gt)
             tt(mk("PP", 0, 8), mk("KQ", 0, 8), mk("U", 0, 8), A.mult)
             tt(mk("PP", 8, 16), mk("KQ", 8, 16), mk("MM"), A.mult)
             tt(mk("PA"), mk("PP", 0, 8), mk("PP", 8, 16), A.add)
@@ -511,12 +518,14 @@ def rank_program(g, core, T, topo):
             dma("s", ap(pr), ap(mk("PA")), [mk("PA")], [pr])
 
     def own_choice(t):
+        b = bufs(t)
         mk = lambda name, *a: blk(me, name + str(t), *a)
+        tt(b("CD"), b("LCN"), b("OL"), A.subtract)
+        lin(b("CG"), b("CD"), 1.0, V("GD", 0, 1), "a")
         for i, s in enumerate(others):
-            tt(mk("VAL", 8 * i, 8 * i + 8), blk(s, "KP%d" % t), blk(s, "CG%d" % t), A.mult)
-        tt(mk("CA"), mk("VAL", 0, 8), mk("CO"), A.add)
-        tt(mk("CB"), mk("VAL", 8, 16), mk("VAL", 16, 24), A.add)
-        tt(mk("CH"), mk("CB"), mk("CA"), A.add)
+            tt(mk("VAL", i, 32, 4), blk(s, "KP%d" % t), blk(s, "CG%d" % t), A.mult)
+        scan(mk("CS"), blk(me, "SEG4", 0, 32), mk("VAL"), A.mult, A.add)
+        act(mk("CH"), mk("CS", 3, 32, 4))
         dma("s", T.ch[t - 1:t, :], ap(mk("CH")), [mk("CH")], [])
 
     def products(t, i, arrived):
@@ -567,6 +576,11 @@ def rank_program(g, core, T, topo):
             row = V("S2", 0, 256, 1, 0, 1)
             dma("s", T.g[:], ap(row), [row], [])
 
+    def quantise_a(i, more):
+        j = qz(V("AQ", 128 * i, 128 * i + 128), V("AP", 128 * i, 128 * i + 128), V("AT", 512 * i, 512 * i + 512))
+        nodes[j]["more"] = more
+        products(1, i, False)
+
     prep_lists()
     list_of(1, "MSG1")
     sent = spread(V("MSG1"), lambda s: V("LM1", 8 * s, 8 * s + 8), "m1", "lm1", V("LM1"))
@@ -582,6 +596,8 @@ def rank_program(g, core, T, topo):
     fill(V("IDT"), 0, 1)
     constants()
     hold[0] = ()
+    for i in range(2):
+        quantise_a(i, 0.0)
     for d in [me] + others:
         tc(blk(d, "LU1"), blk(me, "MSG1") if d == me else blk(me, "LM1", 8 * others.index(d), 8 * others.index(d) + 8))
     tc(blk(me, "LU2"), blk(me, "LS2"))
@@ -596,17 +612,16 @@ def rank_program(g, core, T, topo):
     value_rows(1)
     hold[0] = ()
     decode_ties()
-    tie_flags(1)
+    digits(1)
     thresholds(1)
+    own_keys(1)
     sent = choose_and_send(1)
     each("ST2", 2, "LC2", "m3", "lm3")
     for i, d in enumerate(others):
         dma("s", ap(blk(d, "LU2")), ap(V("LC2", 2 * i, 2 * i + 2)), [V("LC2", 2 * i, 2 * i + 2)], [blk(d, "LU2")])
     hold[0] = (sent - 2,)
-    for i in range(4):
-        j = qz(V("AQ", 128 * i, 128 * i + 128), V("AP", 128 * i, 128 * i + 128), V("AT", 512 * i, 512 * i + 512))
-        nodes[j]["more"] = 2.5 - 0.4 * i
-        products(1, i, False)
+    for i in range(2, 4):
+        quantise_a(i, 2.5 - 0.4 * i)
     hold[0] = ()
     own_list(1)
     new_columns(1)
@@ -614,9 +629,10 @@ def rank_program(g, core, T, topo):
     load("s", V("WT"), T.w[:], LONG, [scores])
     load("s", V("E2"), T.e2[:], LONG, [scores])
     hold[0] = (scores - 1,)
-    tie_flags(2)
     value_rows(2)
+    digits(2)
     thresholds(2)
+    own_keys(2)
     for i in range(4):
         products(2, i, False)
     own_columns(2)

@@ -5,8 +5,7 @@ P, CAPP = 256, 64
 TINY = 2.0 ** -100
 STEP = 2.0 ** -24 * (1 + 2.0 ** -10)
 BIG = 1.5 * 2.0 ** 25
-WAIT, LEAST, ISSUE, WAY, ONCE = 0.2, 0.09, 0.8, 2.8, 1.5
-LOCAL, FIRST, LONG = 2.3, 3.8, 5.5
+HUGE = 1e29
 F, B, I, H, C, S8 = "float32", "bfloat16", "int32", "uint16", "float8_e4m3fn_x4", "uint8"
 SCRATCH = {"PS": ("psum", [128, 4096], F)}
 PLACE = {"PS": ("PS", 0, 4096)}
@@ -36,19 +35,23 @@ _buf(S8, UP=128, AP=512, WP=128, QS0=256, QS1=256, QS2=256, QP0=192, QP1=192, SS
 _buf(H, MSG1=8, MSG2=2, LM1=24, LM2=6, LS2=8, ST2=6, LC2=6, LU1=8, LU2=8)
 _buf(F, ZERO=128, U1=32, U2=32, Z1=1792, Z2=1792, YB=256, S0=448, S1=256, S2=256, PR2=256, PB1=256)
 _buf(I, RAW=64)
-_area(H, DUP=8, PERM=2, PV=2, P8=2, XA=2, DO=2, KO=2)
-_area(I, PI=1, PJ=8, DUPI=8, PERMI=2, KC=8, KD=64)
-_area(F, BAR=64, SEGT=40, KCOL=8, SL=4, XM=32, XI=32, GD=4, BC=4, TR=8, ZB=416, PF32=8, J4=64, SEG4=64, J16=128, MASK=128,
-      SEG16=128, SUF=32, J32=32, IDT=256, PKC=16, KW=8, FL=64, RL=64, T2=64, SCL=64, EQN=64, KQN=64, TK=64, SK=64, PK=16)
-_area(F, **_each(LCN=8, OL=8, OB=8, CD=8, CG=8,
-                 VR=128, KK=32, G=128, SG=128, V4=32, AB=32, AC=32, DE=32, VA=32, BT=40, NI=64, RT=40, TJ=40, TA1=1, SFX=32,
-                 AA=8, W=6208, WD=128, TW=128, PF=16, M16=16, MM=8, EQ=32, KEY=32, K16=16, KM=8,
-                 IC=40, RC=40, TJC=40, TAC=1, SFC=32, KP=8, SV=8,
-                 NW=8, NP=8, BP=8, VAL=32, CS=32, CH=8, XS=32, A2=32, TA=32, XT=16, KQ=16, PP=16, PA=8))
+_area(H, TU=30)
+_area(I, PI=1, PJ=8, TI=64, KI=64, KD=64, KE=64)
+_area(F, BAR=96, SEGT=40, KCOL=8, SL=8, XM=32, XI=32, GD=4, BC=4, TR=8, ZB=544, PF32=8, J4=64, SEG4=64, J16=128, MASK=128,
+      SEG16=128, SUF=64, FOUR=8, J32=32, IDT=256, PKC=64, KW=8, FL=192, RL=64, T2=64, SCL=64, TK=64, SK=64, PK=64,
+      TB=30, DUPF=8, POW=8, MULT=64)
+_area(F, **_each(LCN=8, OL=8, OB=16, KK=32, G=128, SG=128, D1=96, VA=96, BT=40, NI=96, RT=64,
+                 SFX=64, AA=8, PF=16, M16=16, MM=8, EQ=32, KEY=32, K16=16, KM=8,
+                 IC=80, RC=64, SFC=64, KP=16, SV=16,
+                 NW=8, NP=8, CH=8, XS=64, A2=32, TA=32, XT=16, KQ=8, PP=8, PA=8))
+_area(B, **_each(VR=128, W=6208, WD=128, TW=384))
 _area(H, **_each(OF=8, PO=12, XO=16))
+TAB = dict(DUP=(0, 8), PERM=(8, 10), PV=(10, 12), P8=(12, 14), XA=(14, 16), KO=(16, 18), KX=(18, 22), MX=(22, 26), FX=(26, 30))
+WIDE = (3, 2)
 NDMA = 60
 SEMAPHORES = ["qv", "qa", "qt", "qg", "m1", "lm1", "m2", "lm2", "m3", "lm3"] + ["d%d" % i for i in range(NDMA)] + [
     x + str(t) for t in (1, 2) for x in ("v", "lv", "c", "lc", "s", "ls")]
+ORDER = """2s 1a 8g 9g 0s 3a 15v 19v 13v 10g 17v 5s 6a 16v 24v 22v 23v 21v 4s 7s 14v 11g 18v 12v 76a 78a 79a 30g 35a 36a 32g 33a 71a 31g 44v 29g 43v 26v 20v 46v 45v 27a 25v 34a 48v 47v 63v 28a 50v 98a 49v 81v 92a 64v 82a 51g 52x 56v 101a 53a 65v 61v 129v 91a 95v 54a 99a 96v 66v 93a 97v 62v 102a 67v 55a 103a 58v 75a 89a 133a 41v 145v 131a 57v 37a 88v 94a 59t 39v 269v 100a 68g 69x 87v 38a 105v 148a 86v 42a 107v 74a 110v 124g 83a 146v 278a 104v 272v 72a 70g 111t 116v 60a 130a 108t 77a 147a 114v 106a 115v 113v 271v 274a 80v 270a 118v 140s 141s 149v 154v 156v 158v 139s 151a 119v 150a 157v 155v 152a 153v 120v 134a 125v 109a 159v 121g 122x 143v 73a 160v 161v 138a 40a 162v 142a 84v 132a 90v 135a 163v 136a 164v 137a 144a 188g 189x 85a 128s 123g 127s 165v 199v 166v 167v 200v 168v 126g 169v 201v 170v 202v 171v 203v 172v 192s 204v 191s 117v 173v 174a 207v 190s 206v 205v 176v 177v 175v 211a 208v 178v 179v 209v 213v 181v 180v 212v 210v 182v 216a 214v 183a 215v 193v 184g 185x 218v 112a 217v 219v 194t 196v 220v 186g 187x 221v 197t 222v 223v 224v 198a 226v 225v 195a 227t 229t 228v 231t 230a 238v 233t 232a 239v 235t 234a 240v 279a 236a 241v 245v 237a 242v 246v 243t 247t 244v 267t 248v 265t 249v 260v 250v 261t 251v 257v 263t 256a 252g 253x 258a 259v 273v 264v 277a 262a 275v 276a 268a 255s 280s 281v 305v 254s 282v 283v 306v 284v 285v 307v 286v 308v 287v 309v 288v 310v 289v 290a 312v 311v 313v 292v 293v 291v 317a 314v 266a 294v 295v 315v 318v 296v 297v 316v 319v 298v 299a 321v 322a 320v 300g 301x 325v 324v 323v 304v 326v 302g 303x 327v 337a 333v 328v 334v 329v 330v 332v 331v 345t 341t 346v 339t 335v 342a 350v 336s 343t 359v 340a 338s 348v 344a 347v 358v 349v 360v 351v 361s 362t 368a 353t 352s 363v 369a 356t 367s 354a 365t 370a 357v 364s 366v 355s 371a"""
 
 
 def rank_program(g, core, T, topo):
@@ -59,10 +62,14 @@ def rank_program(g, core, T, topo):
     slot_at = [(me - d) % 4 - 1 for d in others]
     qs = {"v": g.vector, "a": g.scalar, "t": g.tensor, "g": g, "s": g.sync}
     hist, know, cnt, total = {}, {q: {} for q in qs}, {}, {}
-    nodes, past, last, hold = [], {}, {}, [()]
+    nodes, past = [], {}
 
     def V(name, c0=0, c1=None, st=1, p0=0, p1=128):
         return (name, p0, p1, c0, PLACE[name][2] if c1 is None else c1, st)
+
+    def tab(name, c0=0, c1=None, buf="TU"):
+        a, z = TAB[name]
+        return V(buf, a + c0, z if c1 is None else a + c1)
 
     def blk(k, name, c0=0, c1=None, st=1):
         return V(name, c0, c1, st, 32 * k, 32 * k + 32)
@@ -85,17 +92,13 @@ def rank_program(g, core, T, topo):
     def regions(reads, writes):
         return [(bank(v), False) for v in reads] + [(bank(v), True) for v in writes]
 
-    def push(opts, reads, writes, cost, dur=None, after=()):
+    def push(opts, reads, writes, after=()):
         i, deps = len(nodes), set(after)
         for r, w in regions(reads, writes):
             deps |= {j for (o, ow, j) in past.get(r[0], []) if (w or ow) and clash(r, o)}
         for r, w in regions(reads, writes):
             past.setdefault(r[0], []).append((r, w, i))
-        prev = list(hold[0]) + ([last["g"]] if "g" in opts and "g" in last else [])
-        if "g" in opts:
-            last["g"] = i
-        nodes.append({"opts": opts, "rd": reads, "wr": writes, "cost": cost, "dur": cost if dur is None else dur,
-                      "deps": deps - {i}, "prev": prev, "gate": [j for j in after], "more": 0.0})
+        nodes.append({"opts": opts, "rd": reads, "wr": writes, "deps": deps - {i}, "gate": list(after)})
         return i
 
     def wait(q, evs):
@@ -113,8 +116,10 @@ def rank_program(g, core, T, topo):
                 know[q][k] = max(know[q].get(k, 0), n)
 
     def issue(node, q):
+        node["done"] = True
         if q == "x":
             return
+        assert all("done" in nodes[j] for j in node["deps"])
         evs = [nodes[j]["ev"] for j in node["gate"]]
         for r, w in regions(node["rd"], node["wr"]):
             evs += [ev for (o, ow, ev) in hist.get(r[0], []) if (w or ow) and clash(r, o)]
@@ -138,45 +143,12 @@ def rank_program(g, core, T, topo):
             hist.setdefault(r[0], []).append((r, w, node["ev"]))
 
     def lay():
-        n = len(nodes)
-        succ = [[] for _ in range(n)]
-        for i, nd in enumerate(nodes):
-            for j in nd["deps"]:
-                succ[j].append(i)
-        high = [0.0] * n
-        for i in range(n - 1, -1, -1):
-            high[i] = nodes[i]["dur"] + nodes[i]["more"] + max([WAIT + high[j] for j in succ[i]] + [high[i]])
-            for p in nodes[i]["prev"]:
-                high[p] = max(high[p], nodes[p]["cost"] + high[i] - nodes[i]["more"] - nodes[p]["dur"])
-        left = [len(nd["deps"]) for nd in nodes]
-        ready = {i for i in range(n) if left[i] == 0}
-        free, fin, done = {}, [0.0] * n, set()
-        while ready:
-            cand = []
-            for i in ready:
-                nd = nodes[i]
-                if any(p not in done for p in nd["prev"]):
-                    continue
-                s = max([fin[j] + WAIT for j in nd["deps"]] + [0.0])
-                start, q = min((max(s, free.get(q, 0.0)) if q != "x" else s, "vatgsx".index(q)) for q in nd["opts"])
-                cand.append((start, -high[i], i, "vatgsx"[q]))
-            first = min(cand)[0]
-            start, _, i, q = min((c for c in cand if c[0] <= first + 0.07), key=lambda c: c[1:])
-            issue(nodes[i], q)
-            free[q] = start + nodes[i]["cost"]
-            fin[i] = start + nodes[i]["dur"]
-            ready.discard(i)
-            done.add(i)
-            for j in succ[i]:
-                left[j] -= 1
-                if left[j] == 0:
-                    ready.add(j)
+        for w in ORDER.split():
+            issue(nodes[int(w[:-1])], w[-1])
+        assert all("done" in nd for nd in nodes)
 
-    def us(cycles):
-        return max(LEAST, 0.02 + 0.001 * cycles)
-
-    def op(q, call, reads, writes, cycles):
-        return push({q: ("op", call)}, reads, writes, us(cycles))
+    def op(q, call, reads, writes):
+        return push({q: ("op", call)}, reads, writes)
 
     def sv(s):
         return ap(s) if isinstance(s, tuple) else s
@@ -185,21 +157,21 @@ def rank_program(g, core, T, topo):
         return [s for s in ss if isinstance(s, tuple)]
 
     def tc(o, a):
-        op("v", lambda: g.vector.tensor_copy(ap(o), ap(a)), [a], [o], width(a))
+        op("v", lambda: g.vector.tensor_copy(ap(o), ap(a)), [a], [o])
 
     def tt(o, a, b, f):
-        op("v", lambda: g.vector.tensor_tensor(ap(o), ap(a), ap(b), f), [a, b], [o], width(a) * (1 if a[0] == "PS" else 2))
+        op("v", lambda: g.vector.tensor_tensor(ap(o), ap(a), ap(b), f), [a, b], [o])
 
     def tti(o, w, off, b, f):
-        op("v", lambda: g.vector.tensor_tensor(ap(o), ap(w).indirect(ap(off)), ap(b), f), [w, off, b], [o], 50 + 1.5 * width(b))
+        op("v", lambda: g.vector.tensor_tensor(ap(o), ap(w).indirect(ap(off)), ap(b), f), [w, off, b], [o])
 
     def ts(o, a, s1, f1, s2=None, f2=None):
         if f2 is None:
-            op("v", lambda: g.vector.tensor_scalar(ap(o), ap(a), sv(s1), None, f1), [a] + cols_of(s1), [o], width(a))
+            op("v", lambda: g.vector.tensor_scalar(ap(o), ap(a), sv(s1), None, f1), [a] + cols_of(s1), [o])
         else:
-            op("v", lambda: g.vector.tensor_scalar(ap(o), ap(a), sv(s1), sv(s2), f1, f2), [a] + cols_of(s1, s2), [o], width(a))
+            op("v", lambda: g.vector.tensor_scalar(ap(o), ap(a), sv(s1), sv(s2), f1, f2), [a] + cols_of(s1, s2), [o])
 
-    def lin(o, a, scale=1.0, bias=0.0, only=None):
+    def lin(o, a, scale=1.0, bias=0.0):
         def on_v():
             if scale == 1.0 and bias == 0.0:
                 return g.vector.tensor_copy(ap(o), ap(a))
@@ -213,49 +185,47 @@ def rank_program(g, core, T, topo):
             if bias == 0.0:
                 return g.scalar.activation(ap(o), ap(a), AF.Copy, scale=sv(scale))
             return g.scalar.activation(ap(o), ap(a), AF.Identity, scale=sv(scale), bias=sv(bias))
-        opts = {"v": ("op", on_v), "a": ("op", on_a)}
-        push({only: opts[only]} if only else opts, [a] + cols_of(scale, bias), [o], us(width(a)))
+        push({"v": ("op", on_v), "a": ("op", on_a)}, [a] + cols_of(scale, bias), [o])
 
-    def scan(o, a, b, f0=A.add, f1=A.add):
-        op("v", lambda: g.vector.tensor_tensor_scan(ap(o), ap(a), ap(b), 0.0, f0, f1), [a, b], [o], width(a))
+    def scan(o, a, b, f0=A.add, f1=A.add, first=0.0):
+        op("v", lambda: g.vector.tensor_tensor_scan(ap(o), ap(a), ap(b), first, f0, f1), [a, b], [o])
 
     def tr(o, a):
-        op("v", lambda: g.vector.transpose(ap(o), ap(a)), [a], [o], width(a))
+        op("v", lambda: g.vector.transpose(ap(o), ap(a)), [a], [o])
 
     def ms(o, c):
-        lin(o, ("ZERO",) + o[1:3] + (0, width(o), 1), 1.0, c, "a")
+        lin(o, ("ZERO",) + o[1:3] + (0, width(o), 1), 1.0, c)
 
     def fill(o, base, step=0, rise=0, pattern=None):
-        n = width(o)
-        op("g", lambda: g.iota(ap(o), pattern or [[step, n]], base, rise, allow_small_or_imprecise_dtypes=True), [], [o], 130 + 2 * n)
+        op("g", lambda: g.iota(ap(o), pattern or [[step, width(o)]], base, rise, allow_small_or_imprecise_dtypes=True), [], [o])
 
     def gat(o, w, off):
-        op("v", lambda: g.vector.tensor_copy(ap(o), ap(w).indirect(ap(off))), [w, off], [o], 50 + 1.5 * width(o))
+        op("v", lambda: g.vector.tensor_copy(ap(o), ap(w).indirect(ap(off))), [w, off], [o])
 
-    def gata(o, w, off):
-        op("a", lambda: g.scalar.activation(ap(o), ap(w).indirect(ap(off)), AF.Copy), [w, off], [o], 70 + 1.5 * width(o))
+    def gata(o, w, off, func=AF.Copy, **k):
+        op("a", lambda: g.scalar.activation(ap(o), ap(w).indirect(ap(off)), func, **k), [w, off], [o])
+
+    def gatx(o, w, off):
+        push({"v": ("op", lambda: g.vector.tensor_copy(ap(o), ap(w).indirect(ap(off)))),
+              "a": ("op", lambda: g.scalar.activation(ap(o), ap(w).indirect(ap(off)), AF.Copy))}, [w, off], [o])
 
     def pick(qo, so, qw, sw, off):
-        op("v", lambda: g.vector.tensor_copy(ap(qo).bitcast(dt.uint32), ap(qw).bitcast(dt.uint32).indirect(ap(off))), [qw, off], [qo],
-           50 + 1.5 * width(qo))
+        op("v", lambda: g.vector.tensor_copy(ap(qo).bitcast(dt.uint32), ap(qw).bitcast(dt.uint32).indirect(ap(off))), [qw, off], [qo])
         gata(so, sw, off)
 
     def qz(q, s, a):
-        return op("v", lambda: g.vector.quantize_mx(ap(q), ap(s), ap(a)), [a], [q, s], 0.25 * width(a))
-
-    def act(o, a, scale=1.0):
-        op("a", lambda: g.scalar.activation(ap(o), ap(a), AF.Copy, scale=scale), [a], [o], width(a))
+        return op("v", lambda: g.vector.quantize_mx(ap(q), ap(s), ap(a)), [a], [q, s])
 
     def mm(b, n, wq, ws, xq, xs):
         o = V("PS", 512 * b, 512 * b + n)
-        op("t", lambda: g.tensor.matmul_mx(ap(o), ap(wq), ap(ws), ap(xq), ap(xs), True, True), [wq, ws, xq, xs], [o], n + 16)
+        op("t", lambda: g.tensor.matmul_mx(ap(o), ap(wq), ap(ws), ap(xq), ap(xs), True, True), [wq, ws, xq, xs], [o])
         return o
 
-    def dma(q, out, in_, reads, writes, after=(), dur=LOCAL):
-        return push({q: ("dma", lambda: qs[q].dma_start(out, in_))}, reads, writes, 0.08, dur, after)
+    def dma(q, out, in_, reads, writes, after=()):
+        return push({k: ("dma", lambda k=k: qs[k].dma_start(out, in_)) for k in q}, reads, writes, after)
 
-    def load(q, v, src, dur, after=()):
-        return dma(q, ap(v), src, [], [v], after, dur)
+    def load(q, v, src, after=()):
+        return dma(q, ap(v), src, [], [v], after)
 
     def mask_of(engines):
         return sum(1 << e for e in engines)
@@ -268,10 +238,8 @@ def rank_program(g, core, T, topo):
         def call():
             g.remote_dma_fused(transfers, local_sem=T.sem[lsem])
             return lsem, count
-        more = 0.0 if cnt.get("remote") else ONCE
-        cnt["remote"] = 1
-        i = push({"g": ("remote", call)}, [src], [], ISSUE + more, ISSUE + 0.5 + more)
-        push({"x": None}, [], [landing], 0.0, WAY - ISSUE - 0.5, [i])
+        i = push({"g": ("remote", call)}, [src], [])
+        push({"x": None}, [], [landing], [i])
         total[sem] = arrivals
         hist.setdefault(landing[0], []).append((landing, True, (sem, arrivals, {sem: arrivals})))
         return i
@@ -299,7 +267,7 @@ def rank_program(g, core, T, topo):
         return remote(trs, V(src), lsem, 16, sem, sum(len(deal(s, turn)[me]) for s in others), V(land))
 
     def zb(t, o, n):
-        o = o if t == 0 else 64 + 176 * (t - 1) + o
+        o = o if t == 0 else 16 + 264 * (t - 1) + o
         return V("ZB", o, o + n)
 
     def sub(v, a, b, k=None, st=1):
@@ -308,15 +276,13 @@ def rank_program(g, core, T, topo):
     def bufs(t):
         return lambda name, *a: V(name + str(t), *a)
 
-    for i in range(8):
-        raw = load("sa"[i % 2], V("RAW", p0=16 * i, p1=16 * i + 16), (T.p1, T.p2)[i % 2][:], LOCAL)
-    hold[0] = (raw - 1, raw)
-    load("s", V("E0", 0, 512), T.e0[:, 0:512], FIRST)
-    load("a", V("UC"), T.u[:, 0:4], FIRST)
-    load("a", V("E0", 512, 1024), T.e0[:, 512:1024], FIRST)
-    load("s", V("AT", 0, 1024), T.a[:, 0:1024], LONG)
-    hold[0] = ()
-    op("g", lambda: g.iota(ap(V("PI")), [[0, 1]], 0, 1), [], [V("PI")], 100)
+    for i in range(4):
+        load("sa", V("RAW", p0=16 * i, p1=16 * i + 16), (T.p1, T.p2)[i % 2][:])
+    load("sa", V("E0", 0, 512), T.e0[:, 0:512])
+    load("sa", V("UC"), T.u[:, 0:4])
+    load("sa", V("E0", 512, 1024), T.e0[:, 512:1024])
+    load("sa", V("AT", 0, 1024), T.a[:, 0:1024])
+    op("g", lambda: g.iota(ap(V("PI")), [[0, 1]], 0, 1), [], [V("PI")])
     fill(V("J4"), 0, pattern=[[0, 16], [1, 4]])
     fill(V("ZERO"), 0)
     fill(V("J16"), 0, pattern=[[0, 8], [1, 16]])
@@ -328,60 +294,72 @@ def rank_program(g, core, T, topo):
     p15, kcol, odd, p96, p31, p7, p4, p8 = [V("PF32", j, j + 1) for j in range(8)]
     ts(V("SL", 0, 1), V("PJ", 3, 4), 8.0, A.mult, -0.5, A.add)
     ts(V("SL", 1, 2), V("PJ", 3, 4), 8.0, A.mult, P - 0.5, A.add)
+    ts(V("SL", 4, 5), V("PJ", 3, 4), 8.0, A.mult, 2 * P - 0.5, A.add)
+    ts(V("SL", 5, 6), V("PJ", 3, 4), 8.0, A.mult, 3 * P - 0.5, A.add)
     ts(V("SL", 2, 3), V("PJ", 3, 4), 24.0, A.mult, 3 * (P - 0.5), A.add)
     ts(V("SEG4"), V("J4"), 1.0, A.min)
-    act(V("PKC"), V("SEG4", 0, 16), 4.0)
-    op("g", lambda: g.iota(ap(V("DUPI")), [[64, 4], [0, 2]], 0, 0), [], [V("DUPI")], 100)
-    op("g", lambda: g.iota(ap(V("PERMI")), [[4, 2]], 0, 0), [], [V("PERMI")], 100)
+    lin(V("PKC"), V("SEG4"), -3.0, 4.0)
+    lin(V("PKC", 0, 64, 32), V("ZERO", 0, 2))
+    fill(V("DUPF"), 0, pattern=[[64, 4], [0, 2]])
+    fill(V("FOUR"), 4)
     fill(V("J32"), 0, 1)
     fill(V("TR"), 1028, 4, 32)
     for k in range(4):
-        ms(blk(k, "BC", 0, 1), float(255 + CAPP + 64 * others.index(k)) if k != me else 0.0)
+        ms(blk(k, "BC", 0, 1), float(255 + 64 * others.index(k)) if k != me else 0.0)
     ms(V("BAR"), 0.0)
     ms(V("BAR", 4, 33, 4), -BIG - 4.0)
     ms(V("BAR", 1, 32, 4), 1.5)
     ms(V("BAR", 3, 32, 4), BIG)
-    lin(V("GD", 0, 1), p96, 8.0, float(-P * me), "a")
+    lin(V("GD", 0, 1), p96, 8.0, float(-P * me))
+    lin(V("GD", 1, 2), V("BC", 0, 1), -1.0, V("GD", 0, 1))
 
     def more_fills():
-        fill(V("RT1", 32, 40), 4)
         fill(V("W1", 0, 256), 0)
         fill(V("XI"), 0, pattern=[[0, 2], [1, 2], [0, 8]])
         ts(V("XM"), V("XI"), odd, A.is_equal)
-        for t in (1, 2):
-            fill(V("RC%d" % t, 32, 40), -CAPP)
-        fill(V("RT2", 32, 40), 4)
         fill(V("W2", 0, 256), 0)
 
     def constants():
-        for c in range(0, 416, 104):
-            ms(V("ZB", c, c + 104), 0.0)
-        ms(V("FL", 0, 64, 4), 0.0)
+        for c in range(0, 544, 109):
+            ms(V("ZB", c, min(544, c + 109)), 0.0)
+        ms(V("FL", 0, 192, 3), 0.0)
+        ms(V("FL", 1, 192, 3), -1.0)
+        for t in (1, 2):
+            ms(V("D1%d" % t, 1, 96, 3), -TINY)
+        for d in range(4):
+            ms(sub(zb(0, 0, 8), (d - me) % 4, 8, d, 4), 65535.0)
         ts(V("SEGT"), V("J4", 0, 40), 1.5, A.is_gt)
         lin(V("SEGT", 4, 33, 4), V("TR"))
         ts(V("MASK"), V("J16"), p15, A.is_equal)
         ts(V("SEG16"), V("J16"), 1.0, A.min)
-        ts(V("SUF"), V("J32"), p31, A.is_ge)
-        kc = [V("KCOL", j, j + 1) for j in range(8)]
-        lin(kc[1], kcol, 8.0, p4, "a")
-        act(kc[2], p15, 4.0)
-        lin(kc[3], p4, 8.0, kcol, "a")
-        lin(kc[4], p4, 3.0, kc[1], "a")
-        lin(kc[5], p8, -7.0, kc[4], "a")
-        lin(kc[6], p7, 4.0, 3.0, "a")
-        ts(V("DUP"), V("DUPI"), kc[2], A.add)
-        ts(V("PERM"), V("PERMI"), kc[1], A.add)
-        ts(V("PV"), V("PERMI"), p4, A.add)
-        ts(V("P8"), V("ZERO", 0, 2), p7, A.add)
-        ts(V("XA"), V("ZERO", 0, 2), kc[6], A.add)
-        ts(V("DO"), V("J32", 0, 2), 4.0, A.mult, kc[3], A.add)
-        ts(V("KO"), V("J32", 0, 2), 2.0, A.mult, kc[5], A.add)
+        ts(V("SUF", 0, 31), V("J32", 0, 31), p31, A.is_ge)
+        ms(V("SUF", 31, 32), -1.0)
+        ms(V("SUF", 32, 64), 1.0)
+        kc = [V("KCOL", j, j + 1) for j in range(4)]
+        lin(kc[0], kcol, 8.0, p4)
+        lin(kc[1], p15, 4.0)
+        lin(kc[2], p4, 4.0)
+        lin(kc[3], p7, 4.0, p8)
+        tb = lambda name: tab(name, buf="TB")
+        lin(tb("DUP"), V("DUPF"), 1.0, kc[1])
+        lin(tb("PERM"), V("J32", 0, 2), 4.0, kc[0])
+        lin(tb("PV"), V("J32", 0, 2), 4.0, p4)
+        lin(tb("P8"), V("ZERO", 0, 2), 1.0, p7)
+        lin(tb("XA"), tb("P8"), 4.0, 3.0)
+        lin(tb("KO"), V("J32", 0, 2), 2.0, kc[3])
+        lin(tb("KX"), V("J4", 0, 8, 2), 2.0, kcol)
+        lin(tb("MX"), V("DUPF", 0, 4), 1.0 / 16, p4)
+        lin(tb("FX"), V("J32", 0, 4), 16.0, kc[2])
+        tc(V("TU"), V("TB"))
+        scan(V("POW"), V("FOUR"), V("ZERO", 0, 8), A.mult, A.add, 0.25)
+        gata(V("MULT"), V("POW"), tab("MX"))
 
     def prep_lists():
+        for z in (0, 64):
+            ts(V("RL", 0, 64, 1, z, z + 64), V("RAW", 0, 64, 1, 0, 64), V("SL", z // 16, z // 16 + 1, 1, 0, 64), A.max,
+               V("SL", z // 16 + 1, z // 16 + 2, 1, 0, 64), A.min)
         for h in range(2):
-            ts(V("RL", 32 * h, 32 * h + 32), V("RAW", h, 64, 2), V("SL", 0, 1), A.max, V("SL", 1, 2), A.min)
-        for h in range(2):
-            tr(V("T2", 32 * h, 32 * h + 32), V("RL", 32 * h, 32 * h + 32))
+            tr(V("T2", 32 * h, 32 * h + 32), V("RL", h, 64, 2))
         for h in range(2):
             scan(V("SCL", 32 * h, 32 * h + 32), V("SEG4", 0, 32), V("T2", 32 * h, 32 * h + 32), A.mult, A.add)
 
@@ -391,58 +369,51 @@ def rank_program(g, core, T, topo):
             ts(V(out, 4 * h, 4 * h + 4), V("SCL", o + 3, o + 16, 4), V("SL", 2, 3), A.subtract)
 
     def prep_ties():
-        for h in range(2):
-            tt(V("EQN", 32 * h, 32 * h + 32), V("RL", 32 * h, 32 * h + 32), V("RAW", h, 64, 2), A.is_equal)
-        lin(V("KQN"), V("EQN"), scale=kcol)
-        tr(V("TK"), V("KQN"))
+        tc(V("TI"), V("T2"))
+        tt(V("TK"), V("TI"), V("T2"), A.is_equal)
         scan(V("SK"), V("SEG4"), V("TK"), A.mult, A.add)
-        scan(V("PK"), V("PKC"), V("SK", 3, 64, 4), A.mult, A.add)
-        for h in range(2):
-            ts(V("MSG2", h, h + 1), V("PK", 8 * h + 3, 8 * h + 4), 256.0, A.mult, V("PK", 8 * h + 7, 8 * h + 8), A.add)
+        scan(V("PK"), V("PKC"), V("SK"), A.mult, A.add)
+        ts(V("MSG2"), V("PK", 31, 64, 32), float(0x5555), A.subtract)
 
     def own_columns(t):
         b = bufs(t)
         tc(b("LCN"), V("MSG1") if t == 1 else V("LS2"))
         for k in [me] + others:
-            act(blk(k, "OL%d" % t), blk(me, "LCN%d" % t))
-        act(sub(zb(t, 80, 32), 3, 32, me, 4), blk(me, "LCN%d" % t))
-        lin(blk(me, "VAL%d" % t, 3, 32, 4), blk(me, "LCN%d" % t), 1.0, float(P * me), "a")
-        lin(b("OB"), b("OL"), -1.0, V("BC", 0, 1), "a")
+            lin(blk(k, "OL%d" % t), blk(me, "LCN%d" % t))
+        lin(sub(zb(t, 104, 32), 3, 32, me, 4), blk(me, "LCN%d" % t))
+        lin(sub(zb(t, 72, 32), 3, 32, me, 4), blk(me, "LCN%d" % t), 1.0, float(P * me))
+        for h in range(2):
+            lin(b("OB", 8 * h, 8 * h + 8), b("OL"), -1.0, V("BC", 0, 1))
+        lin(b("IC", 0, 8), b("LCN"), 1.0, V("GD", 1, 2))
 
     def decode_ties():
         ka = zb(0, 0, 8)
         tc(V("KW", 6, 8), V("MSG2"))
         for s in others:
-            act(sub(ka, (s - me) % 4, 8, me, 4), blk(s, "KW", 6, 8))
-        tc(V("KW", 0, 6), V("LM2"))
+            lin(sub(ka, (s - me) % 4, 8, me, 4), blk(s, "KW", 6, 8))
+        tc(V("KW", 0, 2), V("LM2", 0, 2))
         for j, d in enumerate(others):
             for s in range(4):
                 if s != d:
-                    act(sub(ka, (s - me) % 4, 8, d, 4), blk(s, "KW", 2 * j, 2 * j + 2))
-        tc(V("KC"), ka)
-
-    def digits(t):
-        o = 32 * t - 32
-        for c in range(4 * t - 4, 4 * t):
-            ts(V("KD", 8 * c, 8 * c + 8), V("KC"), 2 * (7 - c), A.logical_shift_right, 3, A.bitwise_and)
-        for i in range(1, 4):
-            tt(V("FL", o + i, o + 32, 4), V("KD", o + i, o + 32, 4), V("KD", o, o + 32, 4), A.is_lt)
+                    (tc if j else lin)(sub(ka, (s - me) % 4, 8, d, 4), blk(s, "LM2" if j else "KW", 2 * j, 2 * j + 2))
+        tti(V("KI"), ka, tab("KX"), V("MULT"), A.mult)
+        for name in ("KD", "KE"):
+            ts(V(name), V("KI"), 0xC000, A.bitwise_and)
+        tti(V("FL", 2, 192, 3), V("KD"), tab("FX"), V("KE"), A.is_lt)
 
     def own_keys(t):
-        o, w, off = V("KK%d" % t), V("KD", 32 * t - 32, 32 * t), V("KO")
-        op("v", lambda: g.vector.tensor_scalar(ap(o), ap(w).indirect(ap(off)), -1.0, 4.0, A.mult, A.add), [w, off], [o], 100)
+        o, w, off = V("KK%d" % t), V("KD", 32 * t - 32, 32 * t), tab("KO")
+        op("v", lambda: g.vector.tensor_scalar(ap(o), ap(w).indirect(ap(off)), 2.0 ** -14, 1.0, A.mult, A.add), [w, off], [o])
 
     def value_rows(t):
         b = bufs(t)
-        gata(b("V4"), b("U", 0, 8), V("PV"))
-        op("a", lambda: g.scalar.activation(ap(b("AB")), ap(b("V4")), AF.Abs, scale=STEP), [b("V4")], [b("AB")], 32)
-        ts(b("AC"), b("AB"), TINY, A.add)
+        gata(b("D1", 0, 96, 3), b("U", 0, 8), tab("PV"), AF.Abs, scale=STEP)
+        gatx(b("D1", 2, 96, 3), b("U", 0, 8), tab("PV"))
         gata(b("VR"), V("IDT"), b("LU"))
 
     def thresholds(t):
         b = bufs(t)
-        tti(b("DE"), V("FL", 32 * t - 32, 32 * t), V("DO"), b("AC"), A.mult)
-        tt(b("VA"), b("V4"), b("DE"), A.subtract)
+        scan(b("VA"), V("FL", 96 * t - 96, 96 * t), b("D1"), A.mult, A.add)
 
     def scores_out(t):
         b = bufs(t)
@@ -453,25 +424,23 @@ def rank_program(g, core, T, topo):
 
     def choose_and_send(t):
         b = bufs(t)
-        worse = zb(t, 112, 64)
-        tti(sub(worse, 0, 32), b("U"), V("PERM"), b("VA"), A.is_gt)
+        worse = zb(t, 136, 96)
+        tti(sub(worse, 0, 32), b("U"), tab("PERM"), b("VA", 2, 96, 3), A.is_gt)
         scan(b("NI"), worse, V("BAR"))
         scan(b("BT", 0, 33), V("SEGT", 0, 33), sub(worse, 0, 33), A.mult, A.max)
-        tr(b("RT", 0, 32), b("NI", 32, 64))
-        op("a", lambda: g.scalar.activation(ap(b("TJ", 0, 33)), ap(b("RT", 0, 33)), AF.Copy, accum_out=ap(b("TA1"))),
-           [b("RT", 0, 33)], [b("TJ", 0, 33), b("TA1")], 50)
+        tr(b("RT"), b("NI", 32, 96))
         tt(b("AA"), b("BT", 4, 33, 4), b("NI", 4, 33, 4), A.subtract)
-        scan(b("SFX"), b("RT", 0, 32), V("SUF"), A.add, A.mult)
-        ts(b("OF"), b("AA"), b("TA1"), A.subtract, b("SFX", 31, 32), A.add)
-        op("v", lambda: g.vector.tensor_copy(ap(b("W")).indirect(ap(b("OF"))), ap(b("VR"))), [b("VR"), b("OF")], [b("W")], 450)
-        gat(b("WD", 0, 64), b("W", 0, 256), V("DUP", 0, 4))
-        gata(b("WD", 64, 128), b("W", 0, 256), V("DUP", 4, 8))
-        tr(b("TW"), b("WD"))
-        pf = "PF%d" % t
+        scan(b("SFX"), b("RT"), V("SUF"), A.add, A.mult)
+        ts(b("OF"), b("AA"), b("SFX", 63, 64), A.subtract, 4.0, A.subtract)
+        op("v", lambda: g.vector.tensor_copy(ap(b("W")).indirect(ap(b("OF"))), ap(b("VR"))), [b("VR"), b("OF")], [b("W")])
+        gat(b("WD", 0, 96), b("W", 0, 256), tab("DUP", 0, 6))
+        gata(b("WD", 96, 128), b("W", 0, 256), tab("DUP", 6, 8))
         for i, d in enumerate(others):
-            tt(blk(me, pf, 4 * i, 4 * i + 4), blk(d, "TW%d" % t, 0, 128, 32), blk(d, "TW%d" % t, 16, 128, 32), A.add)
-        for k in range(4):
-            tc(blk(k, "PO%d" % t), blk(me, pf, 0, 12))
+            tr(blk(me, "TW%d" % t, 128 * i, 128 * i + 128), blk(d, "WD%d" % t))
+        for k in range(2):
+            tt(blk(k, "PF%d" % t, 0, 12), blk(me, "TW%d" % t, 0, 384, 32), blk(me, "TW%d" % t, 16, 384, 32), A.add)
+        for h in range(2):
+            tc(b("PO", 0, 12, 1, 64 * h, 64 * h + 64), b("PF", 0, 12, 1, 0, 64))
         pick(b("SQ"), b("SS"), V("QO%d" % (t - 1)), V("QS%d" % (t - 1)), b("PO"))
         each("SQ%d" % t, 64, "QW%d" % (t - 1), "c%d" % t, "lc%d" % t)
         return each("SS%d" % t, 64, "QP%d" % (t - 1), "s%d" % t, "ls%d" % t, 1)
@@ -481,27 +450,26 @@ def rank_program(g, core, T, topo):
         mk = lambda name, *a: blk(me, name + str(t), *a)
         tt(b("M16"), b("U", 0, 16), b("U", 16, 32), A.max)
         tt(b("MM"), b("M16", 0, 8), b("M16", 8, 16), A.max)
-        tti(b("EQ"), b("MM"), V("P8"), b("U"), A.is_equal)
+        tti(b("EQ"), b("MM"), tab("P8"), b("U"), A.is_equal)
         tt(mk("KEY"), mk("EQ"), mk("KK"), A.mult)
         tt(mk("K16"), mk("KEY", 0, 16), mk("KEY", 16, 32), A.max)
         tt(mk("KM"), mk("K16", 0, 8), mk("K16", 8, 16), A.max)
-        wb, ic, bk = zb(t, 0, 40), b("IC"), zb(t, 80, 32)
+        wb, ic, bk = zb(t, 0, 72), b("IC", 8, 80), zb(t, 72, 64)
         for i, s in enumerate(others):
             tt(sub(wb, 0, 8, s), mk("KEY", 8 * i + 8, 8 * i + 16), mk("KM"), A.is_equal)
-        scan(ic, wb, V("ZERO", 0, 40))
-        tr(b("RC", 0, 32), sub(ic, 8, 40))
-        op("a", lambda: g.scalar.activation(ap(b("TJC", 0, 33)), ap(b("RC", 0, 33)), AF.Copy, scale=-1.0, accum_out=ap(b("TAC"))),
-           [b("RC", 0, 33)], [b("TJC", 0, 33), b("TAC")], 50)
-        scan(b("SFC"), b("RC", 0, 32), V("SUF"), A.add, A.mult)
+        scan(ic, wb, V("ZERO", 0, 72))
+        tr(b("RC"), sub(ic, 8, 72))
+        scan(b("SFC"), b("RC"), V("SUF"), A.add, A.mult)
         lin(b("NW"), sub(wb, 0, 8), -1000.0, 1000.0)
         tt(b("NP"), sub(ic, 0, 8), b("NW"), A.add)
-        tt(b("BP"), sub(ic, 0, 8), b("OB"), A.add)
-        ts(b("KP"), b("NP"), b("SFC", 31, 32), A.subtract, b("TAC"), A.is_le)
-        ts(b("SV"), b("BP"), b("SFC", 31, 32), A.subtract, b("TAC"), A.subtract)
+        tt(b("SV"), b("IC", 0, 16), b("OB"), A.add)
+        for h in range(2):
+            ts(b("KP", 8 * h, 8 * h + 8), b("NP"), b("SFC", 63, 64), A.add, float(CAPP), A.is_le)
+        lin(b("SV", 8, 16), b("SV", 8, 16), 1.0, b("SFC", 63, 64))
         for i, s in enumerate(others):
-            tt(sub(bk, i, 32, me, 4), blk(s, "KP%d" % t), blk(s, "SV%d" % t), A.mult)
-        scan(b("XS"), V("SEG4", 0, 32), bk, A.mult, A.add)
-        tti(b("A2"), b("XS"), V("XA"), V("XM"), A.mult)
+            tt(sub(bk, i, 64, me, 4), blk(s, "KP%d" % t), blk(s, "SV%d" % t), A.mult)
+        scan(b("XS"), V("SEG4"), bk, A.mult, A.add)
+        tti(b("A2"), b("XS", 32, 64), tab("XA"), V("XM"), A.mult)
         tr(mk("TA"), mk("A2"))
         half = me // 2
         for k in (2 * half, 2 * half + 1):
@@ -509,139 +477,112 @@ def rank_program(g, core, T, topo):
         for h in range(2):
             tc(V("XO%d" % t, p0=64 * h, p1=64 * h + 64), V("XT%d" % t, p0=64 * half, p1=64 * half + 64))
         if t == 2:
-            ts(mk("KQ", 0, 8), mk("XS", 3, 32, 4), P - 0.5, A.is_lt)
-            ts(mk("KQ", 8, 16), mk("XS", 3, 32, 4), P - 0.5, A.is_gt)
-            tt(mk("PP", 0, 8), mk("KQ", 0, 8), mk("U", 0, 8), A.mult)
-            tt(mk("PP", 8, 16), mk("KQ", 8, 16), mk("MM"), A.mult)
-            tt(mk("PA"), mk("PP", 0, 8), mk("PP", 8, 16), A.add)
+            ts(mk("KQ"), mk("XS", 35, 64, 4), P - 0.5, A.is_lt, HUGE, A.mult)
+            tt(mk("PP"), mk("MM"), mk("KQ"), A.subtract)
+            tt(mk("PA"), mk("PP"), mk("U", 0, 8), A.max)
             pr = V("PR2", 0, 256, 1, 0, 1)
-            dma("s", ap(pr), ap(mk("PA")), [mk("PA")], [pr])
+            dma("sa", ap(pr), ap(mk("PA")), [mk("PA")], [pr])
 
     def own_choice(t):
-        b = bufs(t)
         mk = lambda name, *a: blk(me, name + str(t), *a)
-        tt(b("CD"), b("LCN"), b("OL"), A.subtract)
-        lin(b("CG"), b("CD"), 1.0, V("GD", 0, 1), "a")
-        for i, s in enumerate(others):
-            tt(mk("VAL", i, 32, 4), blk(s, "KP%d" % t), blk(s, "CG%d" % t), A.mult)
-        scan(mk("CS"), blk(me, "SEG4", 0, 32), mk("VAL"), A.mult, A.add)
-        act(mk("CH"), mk("CS", 3, 32, 4))
-        dma("s", T.ch[t - 1:t, :], ap(mk("CH")), [mk("CH")], [])
+        lin(mk("CH"), mk("XS", 3, 32, 4))
+        dma("sa", T.ch[t - 1:t, :], ap(mk("CH")), [mk("CH")], [])
 
     def products(t, i, arrived):
         q, s, n, o = ("QW", "QP", 192, 256) if arrived else ("QO", "QS", 256, 0)
-        r = mm(i if arrived else 4 + i, n, V("AQ", 128 * i, 128 * i + 128), V("AP", 128 * i, 128 * i + 128), V(q + str(t - 1)), V(s + str(t - 1)))
-        act(V("Z%d" % t, 448 * i + o, 448 * i + o + n), r, 0.05)
+        q, s, z = q + str(t - 1), s + str(t - 1), "Z%d" % t
+        a = (V("AQ", 128 * i, 128 * i + 128), V("AP", 128 * i, 128 * i + 128))
+        lin(V(z, 448 * i + o, 448 * i + o + n), mm(i if arrived else 4 + i, n, *a, V(q), V(s)), 0.05)
 
     def new_columns(t):
         b = bufs(t)
         for i in range(4):
             products(t, i, True)
         if t == 1:
-            act(V("S0", P, 448), mm(6, 192, V("UQ"), V("UP"), V("QW0"), V("QP0")))
+            lin(V("S0", P, 448), mm(6, 192, V("UQ"), V("UP"), V("QW0"), V("QP0")))
             gata(V("PB1"), V("S0"), b("XO"))
-        rs, first, wide = {}, None, 3
 
         def choose(i, lo, hi):
             tti(b("HT", 4 * lo + i, 4 * hi, 4), b("Z", 448 * i, 448 * i + 448), b("XO", lo // 16, hi // 16),
                 V("E%d" % t, 4 * lo + i, 4 * hi, 4), A.add)
+        wide = WIDE[t - 1]
         for i in range(wide):
             choose(i, 0, P)
-        for i in range(wide, 4):
-            choose(i, 0, 128)
-            choose(i, 128, P)
         for f in range(2):
             lo, hi = 128 * f, 128 * f + 128
-            first = qz(V("QO%d" % t, lo, hi), V("QS%d" % t, lo, hi), b("HT", 512 * f, 512 * f + 512))
+            for i in range(wide, 4):
+                choose(i, lo, hi)
+            q, s = V("QO%d" % t, lo, hi), V("QS%d" % t, lo, hi)
+            qz(q, s, b("HT", 512 * f, 512 * f + 512))
             if t == 2:
-                yp = mm(6 + f, 128, V("WQ"), V("WP"), V("QO2", lo, hi), V("QS2", lo, hi))
-                lin(V("YB", lo, hi), yp)
-                nodes[-1]["more"] = 0.3
-            rs[f] = mm(4 + f, 128, V("UQ"), V("UP"), V("QO%d" % t, lo, hi), V("QS%d" % t, lo, hi))
+                dma("sa", T.oc[:, 4 * lo:4 * hi], ap(q).bitcast(dt.uint8), [q], [])
+                lin(V("YB", lo, hi), mm(6 + f, 128, V("WQ"), V("WP"), q, s))
+                dma("sa", T.y[:, lo:hi], ap(V("YB", lo, hi)), [V("YB", lo, hi)], [])
+            r = mm(4 + f, 128, V("UQ"), V("UP"), q, s)
+            if t == 1:
+                tt(V("S1", lo, hi), r, V("PB1", lo, hi), A.add)
+            else:
+                tt(V("S2", lo, hi, 1, 0, 1), r[:2] + (1,) + r[3:], V("PR2", lo, hi, 1, 0, 1), A.add)
         if t == 2:
-            dma("s", T.oc[:], ap(V("QO2")).bitcast(dt.uint8), [V("QO2")], [], dur=LOCAL + 0.6)
-            dma("a", T.y[:], ap(V("YB")), [V("YB")], [], dur=LOCAL + 0.6)
             for k in range(4):
                 sc = V("QS2", 0, P, 1, 32 * k, 32 * k + 4)
-                dma("sa"[k == 3], T.osc[4 * k:4 * k + 4, :], ap(sc), [sc], [])
-        hold[0] = (first,)
-        for f in range(2):
-            lo, hi = 128 * f, 128 * f + 128
-            if t == 1:
-                tt(V("S1", lo, hi), rs[f], V("PB1", lo, hi), A.add)
-            else:
-                tt(V("S2", lo, hi, 1, 0, 1), rs[f][:2] + (1,) + rs[f][3:], V("PR2", lo, hi, 1, 0, 1), A.add)
-        hold[0] = ()
-        if t == 2:
+                dma("sa", T.osc[4 * k:4 * k + 4, :], ap(sc), [sc], [])
             row = V("S2", 0, 256, 1, 0, 1)
-            dma("s", T.g[:], ap(row), [row], [])
+            dma("sa", T.g[:], ap(row), [row], [])
 
-    def quantise_a(i, more):
-        j = qz(V("AQ", 128 * i, 128 * i + 128), V("AP", 128 * i, 128 * i + 128), V("AT", 512 * i, 512 * i + 512))
-        nodes[j]["more"] = more
+    def quantise_a(i):
+        qz(V("AQ", 128 * i, 128 * i + 128), V("AP", 128 * i, 128 * i + 128), V("AT", 512 * i, 512 * i + 512))
         products(1, i, False)
 
     prep_lists()
     list_of(1, "MSG1")
-    sent = spread(V("MSG1"), lambda s: V("LM1", 8 * s, 8 * s + 8), "m1", "lm1", V("LM1"))
+    spread(V("MSG1"), lambda s: V("LM1", 8 * s, 8 * s + 8), "m1", "lm1", V("LM1"))
     for i in range(4):
-        lin(V("UT", i, 512, 4), V("ZERO"), 1.0, V("UC", i, i + 1), "a")
+        lin(V("UT", i, 512, 4), V("ZERO"), 1.0, V("UC", i, i + 1))
     qz(V("UQ"), V("UP"), V("UT"))
     qz(V("QO0"), V("QS0"), V("E0"))
-    act(V("S0", 0, P), mm(0, 256, V("UQ"), V("UP"), V("QO0"), V("QS0")))
-    hold[0] = (sent,)
+    lin(V("S0", 0, P), mm(0, 256, V("UQ"), V("UP"), V("QO0"), V("QS0")))
     list_of(2, "LS2")
     prep_ties()
-    spread(V("MSG2"), lambda s: V("LM2", 2 * s, 2 * s + 2), "m2", "lm2", V("LM2"))
+    ties = spread(V("MSG2"), lambda s: V("LM2", 2 * s, 2 * s + 2), "m2", "lm2", V("LM2"))
     fill(V("IDT"), 0, 1)
     constants()
-    hold[0] = ()
     for i in range(2):
-        quantise_a(i, 0.0)
-    for d in [me] + others:
+        quantise_a(i)
+    for d in others + [me]:
         tc(blk(d, "LU1"), blk(me, "MSG1") if d == me else blk(me, "LM1", 8 * others.index(d), 8 * others.index(d) + 8))
     tc(blk(me, "LU2"), blk(me, "LS2"))
     scores = scores_out(1)
     more_fills()
-    load("s", V("AT", 1024, 2048), T.a[:, 1024:2048], LONG, [scores])
-    load("s", V("E1"), T.e1[:], LONG, [scores])
+    load("sa", V("AT", 1024, 2048), T.a[:, 1024:2048], [scores])
+    load("sa", V("E1"), T.e1[:], [scores])
     own_columns(1)
     for i, d in enumerate(others):
-        dma("s", ap(V("ST2", 2 * i, 2 * i + 2)), ap(blk(d, "LS2")), [blk(d, "LS2")], [V("ST2", 2 * i, 2 * i + 2)])
-    hold[0] = (scores - 1,)
+        dma("sa", ap(V("ST2", 2 * i, 2 * i + 2)), ap(blk(d, "LS2")), [blk(d, "LS2")], [V("ST2", 2 * i, 2 * i + 2)], [ties])
     value_rows(1)
-    hold[0] = ()
     decode_ties()
-    digits(1)
     thresholds(1)
     own_keys(1)
-    sent = choose_and_send(1)
+    choose_and_send(1)
     each("ST2", 2, "LC2", "m3", "lm3")
     for i, d in enumerate(others):
-        dma("s", ap(blk(d, "LU2")), ap(V("LC2", 2 * i, 2 * i + 2)), [V("LC2", 2 * i, 2 * i + 2)], [blk(d, "LU2")])
-    hold[0] = (sent - 2,)
+        dma("sa", ap(blk(d, "LU2")), ap(V("LC2", 2 * i, 2 * i + 2)), [V("LC2", 2 * i, 2 * i + 2)], [blk(d, "LU2")])
     for i in range(2, 4):
-        quantise_a(i, 2.5 - 0.4 * i)
-    hold[0] = ()
+        quantise_a(i)
     own_list(1)
     new_columns(1)
     scores = scores_out(2)
-    load("s", V("WT"), T.w[:], LONG, [scores])
-    load("s", V("E2"), T.e2[:], LONG, [scores])
-    hold[0] = (scores - 1,)
+    load("sa", V("WT"), T.w[:], [scores])
+    load("sa", V("E2"), T.e2[:], [scores])
     value_rows(2)
-    digits(2)
     thresholds(2)
     own_keys(2)
     for i in range(4):
         products(2, i, False)
     own_columns(2)
     own_choice(1)
-    hold[0] = ()
-    sent = choose_and_send(2)
-    hold[0] = (sent,)
+    choose_and_send(2)
     qz(V("WQ"), V("WP"), V("WT"))
-    hold[0] = ()
     own_list(2)
     own_choice(2)
     new_columns(2)

@@ -5,6 +5,7 @@ P, CAPP = 256, 64
 TINY = 2.0 ** -100
 STEP = 2.0 ** -24 * (1 + 2.0 ** -10)
 BIG = 1.5 * 2.0 ** 25
+FAINT = 2.0 ** -13
 HUGE = 1e29
 F, B, I, H, C, S8 = "float32", "bfloat16", "int32", "uint16", "float8_e4m3fn_x4", "uint8"
 SCRATCH = {"PS": ("psum", [128, 4096], F)}
@@ -34,24 +35,219 @@ _buf(C, UQ=128, AQ=512, WQ=128, QO0=256, QO1=256, QO2=256, QW0=192, QW1=192, SQ1
 _buf(S8, UP=128, AP=512, WP=128, QS0=256, QS1=256, QS2=256, QP0=192, QP1=192, SS1=192, SS2=192)
 _buf(H, MSG1=8, MSG2=2, LM1=24, LM2=6, LS2=8, ST2=6, LC2=6, LU1=8, LU2=8)
 _buf(F, ZERO=128, U1=32, U2=32, Z1=1792, Z2=1792, YB=256, S0=448, S1=256, S2=256, PR2=256, PB1=256)
-_buf(I, RAW=64)
-_area(H, TU=30)
-_area(I, PI=1, PJ=8, TI=64, KI=64, KD=64, KE=64)
-_area(F, BAR=96, SEGT=40, KCOL=8, SL=8, XM=32, XI=32, GD=4, BC=4, TR=8, ZB=544, PF32=8, J4=64, SEG4=64, J16=128, MASK=128,
-      SEG16=128, SUF=64, FOUR=8, J32=32, IDT=256, PKC=64, KW=8, FL=192, RL=64, T2=64, SCL=64, TK=64, SK=64, PK=64,
-      TB=30, DUPF=8, POW=8, MULT=64)
-_area(F, **_each(LCN=8, OL=8, OB=16, KK=32, G=128, SG=128, D1=96, VA=96, BT=40, NI=96, RT=64,
-                 SFX=64, AA=8, PF=16, M16=16, MM=8, EQ=32, KEY=32, K16=16, KM=8,
-                 IC=80, RC=64, SFC=64, KP=16, SV=16,
-                 NW=8, NP=8, CH=8, XS=64, A2=32, TA=32, XT=16, KQ=8, PP=8, PA=8))
+_buf(I, RAW=64, RA=32)
+_area(H, TU=22, LS1=8, LA1=8, LA2=8, LB=8)
+_area(I, PI=1, PJ=7, TI=64, KI1=32, KI2=32, KD1=32, KE1=32, KD2=32, KE2=32)
+_area(F, BAR=64, SEGT=40, KCOL=8, SL=8, XM=32, XI=32, GD=4, BC=4, TR=8, ZB=272, PF32=7, J4=64, SEG4=64,
+      SUF=32, FOUR=8, J32=32, IDT=256, PKC=64, KW=8, FL=192, RL=64, T2=64, SCL=64, TK=64, SK=64, PK=64,
+      TB=22, DUPF=8, POW=8, MULT=64, KB=8, XB=32, SEG8=128, RB=32, RC=32, RD=32)
+_area(F, **_each(GI=128, GT=128, LCN=8, OL=8, OG=8, AO=32, KK=32, G=128, SG=132, D1=96, VA=96, BT=40, NI=64, RT=32,
+                 SFX=32, AA=8, PF=16, M16=16, MM=8, EQ=32, KEY=32, KM=32,
+                 IC=48, RC=32, SFC=32, KP=8, SV=8, NQ=32, KR=32, SR=32,
+                 NW=8, NP=8, CH=8, XS=32, A2=32, TA=128, XT=128, KQ=8, PP=8, PA=8))
 _area(B, **_each(VR=128, W=6208, WD=128, TW=384))
 _area(H, **_each(OF=8, PO=12, XO=16))
-TAB = dict(DUP=(0, 8), PERM=(8, 10), PV=(10, 12), P8=(12, 14), XA=(14, 16), KO=(16, 18), KX=(18, 22), MX=(22, 26), FX=(26, 30))
-WIDE = (3, 2)
+TAB = dict(DUP=(0, 8), PERM=(8, 10), PV=(10, 12), P8=(12, 14), KX=(14, 16), MX=(16, 20), FX=(20, 22))
+WIDE = (3, 3)
 NDMA = 60
-SEMAPHORES = ["qv", "qa", "qt", "qg", "m1", "lm1", "m2", "lm2", "m3", "lm3"] + ["d%d" % i for i in range(NDMA)] + [
+SEMAPHORES = ["out", "qv", "qa", "qt", "qg", "m1", "lm1", "m2", "lm2", "m3", "lm3"] + ["d%d" % i for i in range(NDMA)] + [
     x + str(t) for t in (1, 2) for x in ("v", "lv", "c", "lc", "s", "ls")]
-ORDER = """2s 1a 8g 9g 0s 3a 15v 19v 13v 10g 17v 5s 6a 16v 24v 22v 23v 21v 4s 7s 14v 11g 18v 12v 76a 78a 79a 30g 35a 36a 32g 33a 71a 31g 44v 29g 43v 26v 20v 46v 45v 27a 25v 34a 48v 47v 63v 28a 50v 98a 49v 81v 92a 64v 82a 51g 52x 56v 101a 53a 65v 61v 129v 91a 95v 54a 99a 96v 66v 93a 97v 62v 102a 67v 55a 103a 58v 75a 89a 133a 41v 145v 131a 57v 37a 88v 94a 59t 39v 269v 100a 68g 69x 87v 38a 105v 148a 86v 42a 107v 74a 110v 124g 83a 146v 278a 104v 272v 72a 70g 111t 116v 60a 130a 108t 77a 147a 114v 106a 115v 113v 271v 274a 80v 270a 118v 140s 141s 149v 154v 156v 158v 139s 151a 119v 150a 157v 155v 152a 153v 120v 134a 125v 109a 159v 121g 122x 143v 73a 160v 161v 138a 40a 162v 142a 84v 132a 90v 135a 163v 136a 164v 137a 144a 188g 189x 85a 128s 123g 127s 165v 199v 166v 167v 200v 168v 126g 169v 201v 170v 202v 171v 203v 172v 192s 204v 191s 117v 173v 174a 207v 190s 206v 205v 176v 177v 175v 211a 208v 178v 179v 209v 213v 181v 180v 212v 210v 182v 216a 214v 183a 215v 193v 184g 185x 218v 112a 217v 219v 194t 196v 220v 186g 187x 221v 197t 222v 223v 224v 198a 226v 225v 195a 227t 229t 228v 231t 230a 238v 233t 232a 239v 235t 234a 240v 279a 236a 241v 245v 237a 242v 246v 243t 247t 244v 267t 248v 265t 249v 260v 250v 261t 251v 257v 263t 256a 252g 253x 258a 259v 273v 264v 277a 262a 275v 276a 268a 255s 280s 281v 305v 254s 282v 283v 306v 284v 285v 307v 286v 308v 287v 309v 288v 310v 289v 290a 312v 311v 313v 292v 293v 291v 317a 314v 266a 294v 295v 315v 318v 296v 297v 316v 319v 298v 299a 321v 322a 320v 300g 301x 325v 324v 323v 304v 326v 302g 303x 327v 337a 333v 328v 334v 329v 330v 332v 331v 345t 341t 346v 339t 335v 342a 350v 336s 343t 359v 340a 338s 348v 344a 347v 358v 349v 360v 351v 361s 362t 368a 353t 352s 363v 369a 356t 367s 354a 365t 370a 357v 364s 366v 355s 371a"""
+ORDER = """
+RAW.2s RAW.1a PI.0g J4.0g RAW.0s RAW.3a PJ.3v PJ.7v PJ.1v ZERO.0g PJ.5v UC.0s E0.1a PJ.4v SL.3v SL.1v SL.2v SL.0v E0.0s AT.0s
+PJ.2v J16.0g PJ.6v PJ.0v FL.0a D11.0a D12.0a FOUR.0g BC.2a BC.3a TR.0g BC.0a ZB.0a J32.0g RL.1v DUPF.0g RL.0v SEG4.0v PF32.0v
+T2.1v T2.0v PKC.0a SL.4v BC.1a SCL.1v SCL.0v TI.0v PKC.1a MSG1.1v TB.3a MSG1.0v ZB.6v KCOL.1a TK.0v ZB.7a oMSG1.0g _LM1.0x
+UT.3v TB.6a UT.0a SK.0v LS2.0v LCN1.0v KCOL.0a TB.0v UT.1a TB.4a TB.1v PK.0v KCOL.2a TB.2v LS2.1v TB.7a MSG2.0v UT.2a TB.8a
+QO0.0v ZB.4a SUF.1a OL1.3a GD.0v KW.0v OL1.1a UQ.0v BAR.0a SUF.0v KCOL.3a PS0.0t BAR.2v LCN2.0v TB.5a oMSG2.0g _LM2.0x
+SEG16.0v BAR.1a POW.0v ZB.13a MASK.0v GD.1a AQ.0v ZB.3a AQ.1v XI.0g ZB.8a ZB.11v IC2.0a TU.0v OL2.2v ZB.1a IDT.0g PS5.0t
+LU1.3v S0.0a OL1.0a PS4.0t FL.1a ZB.12a LU1.1v MULT.0a LU1.2v LU1.0v OL2.1v ZB.30a ZB.5v OL2.0a G1.0v ST2.1s ST2.2s KW.1v
+ZB.18v ZB.20v ZB.22v ST2.0s ZB.15a SG1.0v ZB.14a ZB.21v ZB.19v ZB.16a ZB.17v U1.0v ZB.9a XM.0v Z1.0a KI.0v oU1.0g _U1.0x
+D11.2v ZB.2a KD.0v KE.0v IC1.0a BAR.3a FL.2v D11.1a SEGT.0v OL1.2a SUF.2v ZB.10a VA1.0v OB1.0a KK1.0v OB1.1a VR1.0a
+oST2.0g _LC2.0x SEGT.1a E1.0s W1.0g AT.1s
+ZB.23v M161.0v NI1.0v BT1.0v MM1.0v RT1.0v W2.0g AA1.0v EQ1.0v SFX1.0v KEY1.0v OF1.0v K161.0v W1.1v LU2.3s KM1.0v LU2.2s
+LU2.0v WD1.0v WD1.1a ZB.26v LU2.1s ZB.25v ZB.24v TW1.1v TW1.2v TW1.0v NW1.0a IC1.1v PF1.0v PF1.1v RC1.0v SV1.0v PO1.1v
+PO1.0v NP1.0v SFC1.0v SQ1.0v SV1.1a KP1.0v SS1.0a KP1.1v AQ.2v oSQ1.0g _QW0.0x ZB.28v Z1.1a ZB.27v ZB.29v PS6.0t AQ.3v
+XS1.0v oSS1.0g _QP0.0x A21.0v PS7.0t TA1.0v XT1.0v XT1.1v Z1.3a XO1.1v XO1.0v Z1.2a
+PS0.1t PS1.0t Z1.4v PS2.0t Z1.5a HT1.0v PS3.0t Z1.6a HT1.1v PS6.1t Z1.7a HT1.2v CH1.0a S0.1a HT1.3v HT1.4v PB1.0a
+QO1.0v QO1.1v PS4.1t PS5.1t S1.0v PS7.1t S1.1v PS6.2t G2.0v KK2.0v SG2.0v PS4.2t U2.0v D12.2v PS5.2t D12.1a oU2.0g _U2.0x
+VR2.0a VA2.0v OL2.3v Z2.1v OB2.1a Z2.0a ZB.31v OB2.0a Z2.3a E2.0s oCH1.0s
+ZB.32v M162.0v WT.0s NI2.0v BT2.0v MM2.0v RT2.0v AA2.0v EQ2.0v SFX2.0v KEY2.0v OF2.0v K162.0v W2.1v KM2.0v WD2.0v WD2.1a
+ZB.34v ZB.33v ZB.35v TW2.1v TW2.2v TW2.0v NW2.0a IC2.1v Z2.2a PF2.0v PF2.1v RC2.0v NP2.0v PO2.0v PO2.1v SFC2.0v SV2.0v
+SQ2.0v SS2.0a KP2.1v SV2.1a KP2.0v oSQ2.0g _QW1.0x ZB.38v ZB.37v ZB.36v WQ.0v XS2.0v oSS2.0g _QP1.0x A22.0v CH2.0a KQ2.0v
+TA2.0v PP2.0v XT2.0v XT2.1v XO2.1v XO2.0v
+PS3.1t PS1.1t Z2.7v PS0.2t PA2.0v Z2.5a HT2.3v PR2.0s PS2.1t HT2.5v Z2.4a oCH2.0s HT2.1v Z2.6a HT2.0v HT2.4v HT2.2v
+QO2.1v QO2.0v oQO2.1s PS7.2t oQS2.1a PS6.3t oQO2.0s YB.1v oQS2.2a PS4.3t oQS2.0s YB.0a PS5.3t oQS2.3a S2.0v oYB.1s S2.1v
+oYB.0s oS2.0a
+"""
+
+
+ORDER = """
+PI.0g RAW.2s PV.0v RAW.1a RAW.0s ZERO.0g RAW.3a UC.0s PJ.1v J4.0g PJ.2v PJ.0v SL.3v E0.1a SL.2v SL.1v SL.0v BC.2a KA.2a E0.0s
+BC.1a BC.0a KA.0a PJ.5v PJ.3v RL.1v RL.0v AT.0s SEG4.0v FL.0a BAR.0a TR.0g SL.4v UT.3a J32.0g UT.0a PJ.4v UT.1a PKC.0a T2.1v
+DUPF.0g T2.0v FOUR.0g ZB.0a PJ.6v SCL.1v SCL.0v TI.0v J16.0g PF32.0v UT.2a MSG1.1v MSG1.0v oMSG1.0g _LM1.0x KA.3a TK.0v QO0.0v
+SK.0v PKC.1a IDT.0g D11.0a UQ.0v TB.4a KCOL.2a LU1.3v KV.0v KA.1a TB.3a TB.2a FL.1a TB.5a PS0.0t PK.0v LS2.0v LS1.0v KCOL.0a
+XI.0g KCOL.1a KA.14a KA.13a SUF.1a GD.0a SEG16.0v W1.0g MASK.0v LS2.1v S0.0a ST2.2v TB.6a ST2.1v ST2.0v KB.3a LU1.2v LU1.1v
+LU1.0v KV.1v W2.0g KA.15a ST2.4s TB.0a TB.1a KA.6a ST2.5s LCN1.0v G1.0v KA.7a KA.4a KA.11a KA.12a KA.5v KA.10v KA.8a ST2.3s
+KA.9v BC.3a KB.0a BAR.1a SG1.0v KB.2a U1.0a oST2.0g _LC2.0x oU1.0g _U1.0x SEGT.0v KR.0v SUF.2v BAR.2v TU.0v SUF.0v KE1.0v
+KD1.0v AQ.1v BAR.3a D11.2v FL.2v AQ.0v E1.0s OL1.3a SEGT.1a KB.1a D11.1a OL1.1a XM.0v VA1.0v AT.1s KK1.0v KW.0v ZB.1a OL1.2v
+ZB.4v KB.4v M161.0v PS5.0t PS4.0t SEG8.0a NI1.0v BT1.0v SEG8.1a MM1.0v KW.1v RT1.0v VR1.0a OG1.0a AA1.0v EQ1.0v SFX1.0v AO1.0v
+LU2.3s KEY1.0v KB.6a LU2.2s KB.9a Z1.0a OF1.0v XB.0a KM1.0v W1.1v ZB.6v KB.7a ZB.5v KB.12a WD1.1a ZB.7v WD1.0v TA1.0v IC1.1v
+TW1.2v KB.13a TW1.0v TW1.1v LU2.1s RC1.0v NW1.0a KB.15a NP1.0v PF1.1v PF1.0v IC1.0a SFC1.0v NQ1.0v D12.0a PO1.0v PO1.1v SR1.0v
+OL1.0a KR1.0v KB.11a SQ1.0v A21.0v AQ.2v ZB.3a PS6.0t Z1.1a KB.5a AQ.3v TA1.2v SV1.0v KP1.0v TA1.1v KB.8a TA1.3v ZB.8v ZB.9v
+ZB.2a oSQ1.0g _QW0.0x SS1.0a ZB.10v oSS1.0g _QP0.0x PS7.0t Z1.3a POW.0v XT1.1v PS0.1t LCN2.0v PS3.0t XT1.0v KB.10v OL2.0v
+MULT.0a XO1.0v XO1.1v KB.14a PS2.0t Z1.4a Z1.2a Z1.7a LU2.0v XS1.0v KI.0v PS1.0t Z1.6a CH1.0v HT1.0v HT1.3v Z1.5a PS6.1t
+HT1.2v HT1.1v HT1.4v S0.1a QO1.0v QO1.1v AO2.0v PS4.1t KD2.0v PB1.0a PS5.1t VR2.0a KE2.0v S1.0v S1.1v OG2.0v G2.0v SG2.0v
+OL2.3a oSG2.0g U2.0v _U2.0x D12.1a KK2.0v D12.2v FL.3v E2.0s VA2.0v OL2.2a ZB.11v M162.0v IC2.0a PS4.2t NI2.0v PS6.2t oCH1.0s
+WT.0s BT2.0v MM2.0v RT2.0v Z2.0a AA2.0v EQ2.0v PS5.2t PS7.1t SFX2.0v TA2.0v KEY2.0v OF2.0v KM2.0v W2.1v WD2.1a ZB.12v ZB.13v
+ZB.14v WD2.0v IC2.1v NW2.0v TW2.0v Z2.2a TW2.1v TW2.2v NP2.0v RC2.0v Z2.3a Z2.1a PF2.1v OL2.1a PF2.0v SFC2.0v NQ2.0v PO2.0v
+PO2.1v SR2.0v KR2.0v SQ2.0v SS2.0a SV2.0v A22.0v oSQ2.0g _QW1.0x KP2.0v TA2.2v ZB.17v ZB.16v TA2.1v WQ.0v ZB.15v oSS2.0g
+_QP1.0x TA2.3v XS2.0v XT2.0v PS3.1t XT2.1v PS0.2t KQ2.0v CH2.0v PP2.0v XO2.0v XO2.1v Z2.7a PS1.1t PA2.0v Z2.5a PR2.0s
+oCH2.0s PS2.1t HT2.3v Z2.6a HT2.4v HT2.1v Z2.4a HT2.0v HT2.2v QO2.1v QO2.0v oQO2.1s oQS2.1a PS7.2t PS5.3t oQO2.0s PS6.3t
+oQS2.2a YB.1v PS4.3t S2.1v S2.0v YB.0a oQS2.0s oQS2.3a oYB.1s oYB.0s oS2.0a
+"""
+
+
+def _moved(order, moves):
+    o = order.split()
+    for line in moves.strip().split("\n"):
+        after, *ws = line.split()
+        o = [w for w in o if w[:-1] not in [x[:-1] for x in ws]]
+        i = [w[:-1] for w in o].index(after) + 1
+        o[i:i] = ws
+    return " ".join(o)
+
+
+ORDER = _moved(ORDER, """
+ST2.3 AT.0s
+A21.0 AQ.0v PS4.0t AQ.1v PS5.0t
+SS1.0 Z1.0a Z1.1a
+KK1.0 AO1.0v
+Z1.1 Z1.2a
+IC1.1 LU2.0v
+A21.0 LB.0v LB.1v
+Z1.0 GI.0a
+XT1.0 GT.0v GT.1v GT.2v GT.3v
+XO1.1 LA.0v LA.1v
+S1.1 G2.1a G2.0v OG2.0v SG2.0v SG2.1v SG2.2v SG2.3v
+W1.1 KM1.0v
+W2.1 KM2.0v
+PA2.0 PS0.2t PS1.1t PS2.1t PS3.1t Z2.4v Z2.5a Z2.6a Z2.7a PR2.0s oCH2.0s HT2.0v HT2.1v HT2.2v HT2.4v HT2.3v QO2.1v QO2.0v
+""")
+
+
+ORDER = """
+PI.0g RAW.2s PV.0v PJ.2v PJ.1v ZERO.0g RAW.1a PJ.0v SL.0v RAW.0s SL.2v SL.3v RAW.3a SL.1v PJ.5v UC.0s KB.3a E0.1a PJ.6v PJ.3v
+RL.1v RL.0v KA.2a BC.1a BAR.0a PJ.4v DUPF.0g E0.0s FOUR.0g J4.0g SEG4.0v T2.1v T2.0v PF32.0v SL.4v FL.1a BC.0a SUF.1a SCL.1v
+D11.0a AT.0s UT.2a UT.3a SCL.0v KCOL.1v TI.0v MSG1.1v J32.0g MSG1.0v BAR.1a PKC.0a J16.0g UT.0a FL.0a KCOL.0a TR.0g KCOL.2a
+XI.0g oMSG1.0g _LM1.0x SEG16.0v TB.2a LS2.0v UT.1a TK.0v IDT.0g PKC.1a KA.0a BC.2a BC.3a BAR.2a TB.1a TB.4a TB.3a LS2.1v ZB.0a
+GD.0a KV.0v QO0.0v SK.0v LS1.0v UQ.0v TB.5a KA.3a AQ.0v TB.0a KA.14a PK.0v KB.0v MASK.0v KA.15a KB.1a LU1.3v ST2.1v ST2.2v
+PS0.0t PS4.0t ST2.0v AQ.1v TB.6a ST2.4s W2.0g ST2.5s KA.1a KA.13a S0.0a Z1.0a W1.0g KV.1v LU1.0v LU1.2v LU1.1v KA.8a KA.4a
+KA.6a LCN1.0v KA.11v KA.7v ST2.3s G1.0v KA.9a KA.12a SEGT.0v AT.1s oST2.0g _LC2.0x KA.5a KW.0v KA.10a OL1.3a XM.0v SG1.0v
+ZB.2a TU.0v KR.0v SEGT.1v PS5.0t U1.0v SEG8.0a AO1.0v KE1.0v KD1.0v BAR.3v Z1.1a oU1.0g _U1.0x KB.6a OL1.2a KB.4a E1.0s
+SEG8.1a ZB.1a AQ.2v D11.2v FL.2v KK1.0v SUF.0v D11.1a AQ.3v KW.1v VA1.0v ZB.4v M161.0v PS6.0t NI1.0v OL1.0a MM1.0v BT1.0v
+KB.2a RT1.0v SUF.2a OG1.0a PS7.0t EQ1.0v AA1.0v XB.0a OL1.1a VR1.0a Z1.2a SFX1.0v KB.12a KEY1.0v OF1.0v LU2.3s LU2.0v KM1.0v
+KB.13a KB.11a KB.15a LU2.2s W1.1v ZB.5v ZB.7v ZB.6v IC1.0a WD1.0v IC1.1v KB.14a KB.5a KB.7a KB.8a KB.9a KB.10a D12.0a ZB.3a
+Z1.3a WD1.1a TW1.2v TW1.0v NW1.0a TW1.1v RC1.0v NP1.0v TA1.0v PF1.1v LU2.1s PF1.0v SFC1.0v NQ1.0v PO1.1v PO1.0v SR1.0v KR1.0v
+SQ1.0v KP1.0v SV1.0v POW.0v A21.0v oSQ1.0g _QW0.0x LCN2.0v ZB.8v ZB.10v TA1.2v TA1.1v TA1.3v LB.1v SS1.0a MULT.0a LB.0v ZB.9v
+XT1.0v oSS1.0g _QP0.0x PS0.1t OL2.0a OL2.3a OG2.0a OL2.2a AO2.0v PS1.0t PS2.0t PS3.0t KI.0v XS1.0v XT1.1v IC2.0a GI.0a GT.1v
+CH1.0v GT.0v GT.3v GT.2v KE2.0v XO1.0v XO1.1v PS6.1t LA.0v OL2.1a Z1.4a Z1.6a LA.1v Z1.5v HT1.0v Z1.7a HT1.2v HT1.3v HT1.1v
+HT1.4v QO1.0v S0.1a QO1.1v PS4.1t KD2.0v VR2.0a PB1.0a TA2.0v S1.0v PS5.1t PS7.1t PS6.2t PS4.2t S1.1v G2.0v SG2.1v SG2.0v
+PS5.2t G2.1a SG2.3v SG2.2v oSG2.0g FL.3v U2.0v _U2.0x D12.2v E2.0s KK2.0v oCH1.0s WT.0s Z2.0a D12.1a Z2.1a Z2.2a VA2.0v ZB.11v
+M162.0v NI2.0v MM2.0v BT2.0v RT2.0v EQ2.0v AA2.0v SFX2.0v KEY2.0v OF2.0v KM2.0v W2.1v ZB.12v ZB.14v ZB.13v WD2.0v IC2.1v Z2.3a
+WD2.1a TW2.0v TW2.2v NW2.0a TW2.1v RC2.0v NP2.0v PF2.1v PF2.0v SFC2.0v NQ2.0v PO2.0v PO2.1v SR2.0v KR2.0v SQ2.0v KP2.0v SV2.0v
+A22.0v oSQ2.0g _QW1.0x ZB.16v ZB.15v ZB.17v TA2.3v TA2.1v TA2.2v XS2.0v WQ.0v XT2.0v KQ2.0v XT2.1v PP2.0v CH2.0v SS2.0a
+oSS2.0g _QP1.0x PS0.2t PS3.1t PS2.1t PS1.1t XO2.0v XO2.1v PA2.0v Z2.7a Z2.4v Z2.6a PR2.0s oCH2.0s HT2.0v Z2.5a HT2.4v HT2.1v
+HT2.2v HT2.3v QO2.1v PS7.2t oQO2.1s QO2.0v YB.1a PS5.3t oQS2.1a PS6.3t YB.0a S2.1v oQO2.0s PS4.3t oQS2.2a oQS2.0s S2.0v
+oQS2.3a oYB.1s oYB.0s oS2.0a
+"""
+
+
+ORDER = """
+PI.0g RAW.2s PV.0v PJ.2v PJ.1v ZERO.0g RAW.1a PJ.0v SL.0v RAW.0s SL.2v SL.3v RAW.3a SL.1v PJ.5v UC.0s KB.3a E0.1a PJ.6v PJ.3v
+RL.1v RL.0v KA.2a BC.1a BAR.0a PJ.4v DUPF.0g E0.0s FOUR.0g J4.0g SEG4.0v T2.1v T2.0v PF32.0v SL.4v FL.1a BC.0a SUF.1a SCL.1v
+D11.0a AT.0s UT.2a UT.3a SCL.0v KCOL.1v TI.0v MSG1.1v J32.0g MSG1.0v LS2.0v TK.0v LS2.1v BAR.1a PKC.0a J16.0g UT.0a FL.0a
+KCOL.0a TR.0g KCOL.2a XI.0g oMSG1.0g _LM1.0x SEG16.0v TB.2a UT.1a IDT.0g PKC.1a KA.0a BC.2a BC.3a BAR.2a TB.1a TB.4a TB.3a
+ZB.0a GD.0a KV.0v SK.0v LS1.0v QO0.0v PK.0v UQ.0v ST2.1v ST2.2v ST2.0v MASK.0v TB.5a KB.0a KA.3a AQ.0v TB.0a KA.14a KA.15a
+KB.1a LU1.3v PS0.0t PS4.0t TB.6a ST2.4s W2.0g ST2.5s KA.1a KA.13a S0.0a W1.0g KV.1v LU1.1v LU1.2v LU1.0v KA.8a KA.4a KA.6a
+LCN1.0v KA.11v KA.7v ST2.3s G1.0v KA.12a SEGT.0v AT.1s oST2.0g _LC2.0x KA.5a KA.9v KA.10a OL1.3a XM.0v SG1.0v KW.0v BAR.3a
+ZB.2a Z1.0a TU.0v KR.0v U1.0v SEG8.0a SEGT.1a AQ.1v KE1.0v KD1.0v AO1.0v oU1.0g _U1.0x KB.6a OL1.2a KB.4a E1.0s SEG8.1a D11.2a
+SUF.0v ZB.1v KK1.0v PS5.0t FL.2v AQ.2v D11.1a VA1.0v AQ.3v ZB.4v M161.0v PS6.0t PS7.0t NI1.0v SUF.2a OL1.0a MM1.0v BT1.0v KB.2a RT1.0v
+OG1.0a EQ1.0v AA1.0v XB.0a OL1.1a IC1.0a Z1.1a VR1.0a Z1.2a SFX1.0v KW.1v KEY1.0v OF1.0v KB.12v LU2.3s LU2.0v KM1.0v KB.13a
+KB.11a KB.15a LU2.2s W1.1v ZB.5v ZB.7v ZB.6v WD1.0v IC1.1v KB.14a KB.5a KB.7a KB.8a KB.9a KB.10a D12.0a ZB.3a WD1.1a TW1.2v
+TW1.0v NW1.0a TW1.1v RC1.0v NP1.0v TA1.0v PF1.1v LU2.1s PF1.0v SFC1.0v NQ1.0v PO1.1v PO1.0v SR1.0v KR1.0v SQ1.0v
+SV1.0v KP1.0v POW.0v A21.0v oSQ1.0g _QW0.0x LCN2.0v ZB.8v ZB.10v TA1.2v TA1.1v TA1.3v LB.1v SS1.0a Z1.3a MULT.0a LB.0v ZB.9v
+XT1.0v oSS1.0g _QP0.0x PS0.1t OL2.0a OL2.3a OG2.0a OL2.2a AO2.0v PS1.0t PS2.0t PS3.0t KI.0v XS1.0v XT1.1v IC2.0a GI.0a GT.1v
+CH1.0v GT.0v GT.3v GT.2v KE2.0v XO1.0v XO1.1v PS6.1t LA.0v OL2.1a Z1.4a Z1.6a LA.1v Z1.5v HT1.0v
+""" + ORDER[ORDER.index("HT1.0v") + 6:]
+
+
+ORDER = """
+PI.0g RA.0s RA.1a PJ.3v PJ.2v RA.2s RA.3a ZERO.0g RAW.2s PJ.0v RAW.1a PJ.1v PJ.4v RAW.0s J4.0g RAW.3a SL.0v SL.2v SL.1v J32.0g
+PJ.5v BAR.0a FL.0a SUF.1a BAR.2a KB.1a UC.0s E0.1a E0.0s SL.3v SL.4v AT.0s PJ.6v RB.0v RB.1v RL.0v RL.1v SEG4.0v RC.0v PF32.0v
+T2.1v T2.0v FOUR.0g DUPF.0g TR.0g RD.0v RD.1v TI.0v MSG1.0v MSG1.1v SCL.0v BC.1a UT.3a XI.0g oMSG1.0g _LM1.0x D11.0a UT.2a
+TK.0v SCL.1v PKC.0a LS1.0v BAR.1a TB.4a KCOL.0a POW.0v SK.0v LS1.1v LS2.1v KCOL.2a PKC.1a FL.1a UT.1a KCOL.1a LS2.0v UT.0a
+PK.0v TB.1a KB.0a TB.0a TB.3a BC.3a UQ.0v SEGT.0v MSG2.0v QO0.0v LCN1.0v ZB.0a GD.0a BC.0a TB.5a KW.0v IDT.0g oMSG2.0g _LM2.0x
+AQ.0v TB.6a TB.2a PS0.0t BC.2a KB.2a KB.3a KB.6a TU.0v LU2.0v LA1.3v KB.4a KB.5a XM.0v AQ.1v SUF.0v LCN2.0v LA1.2v MULT.0a
+S0.0a PS4.0t LA1.0v LA1.1v Z1.0a ST2.1s G1.0v KW.1v KB.10v W1.0g ST2.2s KB.12v KB.11v ST2.0s G1.1a AT.1s KB.7a KB.8a
+KB.9a KB.15a SG1.1v SG1.3v KB.13a PS5.0t SG1.0v SG1.2v oSG1.0g _U1.0x KB.14a GI1.0a oST2.0g _LC2.0x W2.0g SEGT.1v KI1.0v ZB.2v
+D11.2v KE1.0v KD1.0v ZB.1a GT1.0v BAR.3v GT1.2v FL.2v KK1.0v D11.1a U1.0a GT1.3v GT1.1v VA1.0v IC1.0v E1.0s OL1.2a LU1.0v
+ZB.4v M161.0v NI1.0v MM1.0v BT1.0v RT1.0v EQ1.0v OL1.0a AA1.0v SUF.2a IC2.0a OL1.3a SEG8.0a Z1.1a SFX1.0v KEY1.0v OF1.0v
+AO1.0v OL2.1a SEG8.1a XB.0a KM1.0v LU2.3s LU2.2s OL1.1a D12.0a ZB.3a OL2.2a OG2.0a OL2.0a OG1.0a OL2.3a VR1.0a W1.1v ZB.7v
+ZB.5v ZB.6v WD1.0v WD1.1a IC1.1v TW1.2v NW1.0a TW1.1v TW1.0v NP1.0v RC1.0v LU2.1s PF1.1v PF1.0v SFC1.0v NQ1.0v PO1.0v PO1.1v
+SR1.0v KR1.0v SQ1.0v A21.0v oSQ1.0g _QW0.0x LB.0v LB.1v AQ.2v PS6.0t KP1.0v SS1.0a TA1.2v TA1.3v SV1.0v TA1.0v oSS1.0g _QP0.0x
+TA1.1v AQ.3v ZB.10v PS7.0t GI2.0a GT2.2v GT2.3v ZB.8v KI2.0v GT2.1v XT1.0v GT2.0v Z1.2a XT1.1v ZB.9v PS0.1t PS2.0t PS1.0t
+KE2.0v Z1.3a Z1.4a AO2.0v LA2.0v XO1.0v XO1.1v LA2.1v KD2.0v PS3.0t XS1.0v Z1.6v PS6.1t HT1.0v Z1.5a Z1.7a HT1.2v HT1.3v
+HT1.1v HT1.4v QO1.0v S0.1a QO1.1v PS4.1t VR2.0a PB1.0a TA2.0v CH1.0v S1.0v PS5.1t PS7.1t PS6.2t PS4.2t S1.1v G2.0v SG2.1v
+SG2.0v PS5.2t G2.1a SG2.3v SG2.2v oSG2.0g FL.3v U2.0v _U2.0x D12.2v E2.0s KK2.0v oCH1.0s WT.0s Z2.0a D12.1a Z2.1a Z2.2a VA2.0v
+ZB.11v M162.0v NI2.0v MM2.0v BT2.0v RT2.0v EQ2.0v AA2.0v SFX2.0v KEY2.0v OF2.0v KM2.0v W2.1v ZB.12v ZB.14v ZB.13v WD2.0v
+IC2.1v Z2.3a WD2.1a TW2.0v TW2.2v NW2.0a TW2.1v RC2.0v NP2.0v PF2.1v PF2.0v SFC2.0v NQ2.0v PO2.0v PO2.1v SR2.0v KR2.0v SQ2.0v
+KP2.0v SV2.0v A22.0v oSQ2.0g _QW1.0x ZB.16v ZB.15v ZB.17v TA2.3v TA2.1v TA2.2v XS2.0v WQ.0v XT2.0v KQ2.0v XT2.1v PP2.0v CH2.0v
+SS2.0a oSS2.0g _QP1.0x PS0.2t PS3.1t PS2.1t PS1.1t XO2.0v XO2.1v PA2.0v Z2.7a Z2.4v Z2.6a PR2.0s oCH2.0s HT2.0v Z2.5a HT2.4v
+HT2.1v HT2.2v HT2.3v QO2.1v PS7.2t oQO2.1s QO2.0v YB.1a PS5.3t oQS2.1a PS6.3t YB.0a S2.1v oQO2.0s PS4.3t oQS2.2a oQS2.0s S2.0v
+oQS2.3a oYB.1s oYB.0s oS2.0a
+"""
+
+
+ORDER = """
+PI.0g RA.0s RA.1a RA.2s RA.3a J4.0g ZERO.0g RAW.2s RAW.1a RAW.0s RAW.3a UC.0s E0.1a E0.0s AT.0s PJ.3v PJ.1v PJ.0v PJ.2v SL.0v
+SL.1v SL.5v SL.6v SL.7v SL.4v SEG4.0v PJ.4v FOUR.0g DUPF.0g J32.0g TR.0g BAR.0a FL.0a SUF.1a KB.1a RB.0v RB.1v TI.0v PJ.5v
+PJ.6v RC.0v TK.0v TK.1v PF32.0v D11.0a PKC.0a BAR.2a RD.0v RD.1v SK.0v SK.1v MSG1.0v MSG1.1v oMSG1.0g XI.0g _LM1.0x BC.1a
+BAR.1a FL.1a PKC.1a UT.3a UT.2a SL.2v PK.0v SL.3v POW.0v SEGT.0v RL.0v MSG2.0v RL.1v oMSG2.0g _LM2.0x IDT.0g TB.4a
+UT.1a UT.0a KCOL.0a KCOL.2a KCOL.1a QO0.0v T2.0v T2.1v UQ.0v KW.0v SCL.0v SCL.1v LS1.0v LS2.1v TB.1a KB.0a TB.0a TB.3a BC.3a LS1.1v
+LS2.0v ZB.0a GD.0a BC.0a TB.5a TB.6a TB.2a PS0.0t BC.2a KB.2a KB.3a KB.6a TU.0v LA1.3v AQ.0v KB.4a KB.5a
+LA1.2v S0.0a MULT.0a PS4.0t LA1.0v LA1.1v KW.1v LCN1.0v LCN2.0v ST2.1s G1.0v KB.10v W1.0g ST2.2s KB.12v KB.11v
+ST2.0s G1.1a AT.1s KB.7a KB.8a KB.9a KB.15a SG1.1v SG1.3v KB.13a SG1.0v SG1.2v oSG1.0g _U1.0x KB.14a GI1.0a oST2.0g
+_LC2.0x W2.0g SEGT.1v SUF.0v KI1.0v ZB.2v D11.2v KE1.0v KD1.0v ZB.1a GT1.0v BAR.3v GT1.2v FL.2v KK1.0v D11.1a U1.0a Z1.0a GT1.3v GT1.1v
+VA1.0v XM.0v E1.0s OL1.2a LU1.0v ZB.4v M161.0v IC1.0v NI1.0v MM1.0v BT1.0v RT1.0v EQ1.0v OL1.0a AA1.0v SUF.2a IC2.0a OL1.3a SEG8.0a
+SFX1.0v LU2.0v KEY1.0v OF1.0v AO1.0v OL2.1a SEG8.1a XB.0a KM1.0v LU2.3s LU2.2s OL1.1a VR1.0a D12.0a ZB.3a OL2.2a OG2.0a OL2.0a OG1.0a
+OL2.3a W1.1v ZB.7v ZB.5v ZB.6v WD1.0v WD1.1a IC1.1v TW1.2v NW1.0a TW1.1v TW1.0v NP1.0v RC1.0v LU2.1s PF1.1v PF1.0v
+SFC1.0v NQ1.0v PO1.0v PO1.1v SR1.0v KR1.0v SQ1.0v A21.0v oSQ1.0g _QW0.0x AQ.1v PS5.0t LB.0v LB.1v AQ.2v PS6.0t SS1.0a TA1.2v TA1.3v
+TA1.0v oSS1.0g _QP0.0x TA1.1v AQ.3v KP1.0v SV1.0v PS7.0t GI2.0a Z1.1a XT1.0v XT1.1v ZB.10v ZB.8v ZB.9v GT2.2v GT2.3v XO1.0v XO1.1v GT2.1v GT2.0v Z1.2a
+PS0.1t PS2.0t PS1.0t Z1.3a Z1.4a KI2.0v AO2.0v LA2.0v LA2.1v XS1.0v KE2.0v KD2.0v PS3.0t Z1.6v PS6.1t HT1.0v
+""" + ORDER[ORDER.index("HT1.0v") + 6:]
+
+
+ORDER = """
+PI.0g RA.0s RA.1a RAW.0s RAW.1a RAW.2s RAW.3a J4.0g ZERO.0g UC.0a E0.0s E0.1a AT.0s PJ.3v PJ.1v PJ.0v PJ.2v SL.0v SL.1v
+SL.2v SL.3v SL.5v SL.4v SL.7v SL.6v SEG4.0v RB.0v RB.1v RB.2v RB.3v TI.0v PJ.4v PJ.5v RC.0v TK.0v TK.1v PJ.6v FOUR.0g DUPF.0g
+J32.0g TR.0g PKC.0a RD.0v RD.1v SK.0v SK.1v MSG1.0v MSG1.1v PF32.0v BAR.0a FL.0a SUF.1a PKC.1a PK.0v KB.1a D11.0a BAR.2a
+oMSG1.0g XI.0g _LM1.0x BC.1a BAR.1a FL.1a UT.3a UT.2a POW.0v SEGT.0v RL.0v MSG2.0v RL.1v oMSG2.0g _LM2.0x IDT.0g UT.1a UT.0a
+KCOL.0a TB.4a KCOL.1a KCOL.2a QO0.0v T2.0v T2.1v UQ.0v SCL.0v SCL.1v KW.0v TB.0v LS1.0v LS2.1v TB.1a KB.0a TB.3a BC.3a LS1.1v
+LS2.0v ZB.0a GD.0a BC.0a TB.5a TB.6a TB.2a PS0.0t BC.2a KB.2a KB.3a KB.6a TU.0v LA1.3v AQ.0v KB.4a KB.5a LA1.2v S0.0a MULT.0a
+PS4.0t LA1.0v LA1.1v KW.1v LCN1.0v LCN2.0v ST2.1s G1.0v KB.10v W1.0g ST2.2s KB.12v KB.11v ST2.0s G1.1a AT.1s KB.7a KB.8a KB.9a
+KB.15a SG1.1v SG1.3v KB.13a SG1.0v SG1.2v oSG1.0g _U1.0x KB.14a GI1.0a oST2.0g _LC2.0x W2.0g SEGT.1v SUF.0v KI1.0v ZB.2v
+D11.2v KE1.0v KD1.0v ZB.1a GT1.0v BAR.3v GT1.2v FL.2v KK1.0v D11.1a U1.0a Z1.0a GT1.3v GT1.1v VA1.0v XM.0v E1.0s OL1.2a LU1.0v
+""" + ORDER[ORDER.index("ZB.4v"):ORDER.index("PS0.2t")] + """
+PS0.2t PS3.1t PS2.1t PS1.1t XO2.0v XO2.1v PA2.0v PR2.0s oCH2.0s Z2.4v HT2.0v Z2.7a Z2.6a HT2.4v Z2.5a HT2.2v HT2.1v HT2.3v QO2.1v
+PS7.2t QO2.0v YB.1v oQS2.0a PS5.3t PS6.3t S2.1v oQS2.2a PS4.3t oQO2.1s oQS2.1s S2.0v YB.0a oQO2.0s oQS2.3s oYB.1s oYB.0a
+oS2.0s
+"""
+
+
+ORDER = _moved(ORDER, """
+U1.0 SUF.1a
+KR1.0 SQ1.0v SQ1.1v SS1.0a SS1.1a oSQ1.0g _QW0.0x oSQ1.1g _QW0.1x oSS1.0g _QP0.0x
+KR2.0 SQ2.0v SQ2.1v SS2.0a SS2.1a oSQ2.0g _QW1.0x oSQ2.1g _QW1.1x oSS2.0g _QP1.0x
+""")
 
 
 def rank_program(g, core, T, topo):
@@ -129,6 +325,9 @@ def rank_program(g, core, T, topo):
             sem, val = "q" + q, cnt.get(q, 0) + 1
             cnt[q] = val
             call().then_inc(T.sem[sem], 1)
+        elif kind == "dma" and not node["wr"]:
+            sem, val = "out", total.get("out", 0) + 16
+            call().then_inc(T.sem[sem], 16)
         elif kind == "dma":
             sem, val = "d%d" % cnt.get("dma", 0), 16
             cnt["dma"] = cnt.get("dma", 0) + 1
@@ -143,8 +342,17 @@ def rank_program(g, core, T, topo):
             hist.setdefault(r[0], []).append((r, w, node["ev"]))
 
     def lay():
+        seen, named = {}, {}
+        for nd in nodes:
+            if nd["wr"]:
+                v = nd["wr"][0]
+                b = ("_" if "x" in nd["opts"] else "") + v[0] + (str(v[3] // 512) if v[0] == "PS" else "")
+            else:
+                b = "o" + nd["rd"][0][0]
+            named["%s.%d" % (b, seen.get(b, 0))] = nd
+            seen[b] = seen.get(b, 0) + 1
         for w in ORDER.split():
-            issue(nodes[int(w[:-1])], w[-1])
+            issue(named[w[:-1]], w[-1])
         assert all("done" in nd for nd in nodes)
 
     def op(q, call, reads, writes):
@@ -244,8 +452,8 @@ def rank_program(g, core, T, topo):
         hist.setdefault(landing[0], []).append((landing, True, (sem, arrivals, {sem: arrivals})))
         return i
 
-    def spread(src, land, sem, lsem, landing):
-        e = topo.engines(core, T.cores[others[0]])[:16]
+    def spread(src, land, sem, lsem, landing, first=0, step=1):
+        e = topo.engines(core, T.cores[others[0]])[first:16:step]
         return remote([RemoteDMATransfer(
             dst_ids=[dst(d) for d in others], dma_engine_mask=mask_of(e), remote_sem=T.sem[sem], srcs=[ap(src)],
             dsts=[ap(land(s)) for s in slot_at])], src, lsem, len(e), sem, 3 * len(e), landing)
@@ -266,8 +474,22 @@ def rank_program(g, core, T, topo):
                 srcs=[ap(a).bitcast(dt.uint8) if code else ap(a)], dsts=[ap(z).bitcast(dt.uint8) if code else ap(z)]))
         return remote(trs, V(src), lsem, 16, sem, sum(len(deal(s, turn)[me]) for s in others), V(land))
 
+    def turn_of(s):
+        return sorted([d for d in range(4) if d != s], key=lambda d: (topo.die(T.cores[d]) != topo.die(T.cores[s]), (d - s) % 4 == 2))
+    turn = turn_of(me)
+
+    def columns(src, land, engines, sem, arrivals, lsem, count):
+        trs, code = [], SCRATCH[src][2] == C
+        for i in engines:
+            at = slot_at[others.index(turn[i])]
+            a, z = V(src, 64 * i, 64 * i + 64), V(land, 64 * at, 64 * at + 64)
+            trs.append(RemoteDMATransfer(
+                dst_ids=[dst(turn[i])], dma_engine_mask=mask_of(engines[i]), remote_sem=T.sem[sem],
+                srcs=[ap(a).bitcast(dt.uint8) if code else ap(a)], dsts=[ap(z).bitcast(dt.uint8) if code else ap(z)]))
+        return remote(trs, V(src, 64 * min(engines), 64 * max(engines) + 64), lsem, count, sem, arrivals, V(land))
+
     def zb(t, o, n):
-        o = o if t == 0 else 16 + 264 * (t - 1) + o
+        o = 136 * (t - 1) + o
         return V("ZB", o, o + n)
 
     def sub(v, a, b, k=None, st=1):
@@ -276,27 +498,29 @@ def rank_program(g, core, T, topo):
     def bufs(t):
         return lambda name, *a: V(name + str(t), *a)
 
+    for i in range(2):
+        load("sa", blk(i, "RA"), T.p1[:])
     for i in range(4):
         load("sa", V("RAW", p0=16 * i, p1=16 * i + 16), (T.p1, T.p2)[i % 2][:])
     load("sa", V("E0", 0, 512), T.e0[:, 0:512])
     load("sa", V("UC"), T.u[:, 0:4])
     load("sa", V("E0", 512, 1024), T.e0[:, 512:1024])
-    load("sa", V("AT", 0, 1024), T.a[:, 0:1024])
     op("g", lambda: g.iota(ap(V("PI")), [[0, 1]], 0, 1), [], [V("PI")])
     fill(V("J4"), 0, pattern=[[0, 16], [1, 4]])
     fill(V("ZERO"), 0)
-    fill(V("J16"), 0, pattern=[[0, 8], [1, 16]])
     for j, m in enumerate((15, 3, 1, 96, 31, 7)):
         ts(V("PJ", j, j + 1), V("PI"), m, A.bitwise_and)
     ts(V("PJ", 6, 7), V("PI"), 2, A.logical_shift_right, 3, A.bitwise_and)
-    ts(V("PJ", 7, 8), V("PI"), 3, A.logical_shift_right, 1, A.bitwise_and)
     tc(V("PF32"), V("PJ"))
-    p15, kcol, odd, p96, p31, p7, p4, p8 = [V("PF32", j, j + 1) for j in range(8)]
+    p15, kcol, odd, p96, p31, p7, p4 = [V("PF32", j, j + 1) for j in range(7)]
     ts(V("SL", 0, 1), V("PJ", 3, 4), 8.0, A.mult, -0.5, A.add)
     ts(V("SL", 1, 2), V("PJ", 3, 4), 8.0, A.mult, P - 0.5, A.add)
     ts(V("SL", 4, 5), V("PJ", 3, 4), 8.0, A.mult, 2 * P - 0.5, A.add)
     ts(V("SL", 5, 6), V("PJ", 3, 4), 8.0, A.mult, 3 * P - 0.5, A.add)
     ts(V("SL", 2, 3), V("PJ", 3, 4), 24.0, A.mult, 3 * (P - 0.5), A.add)
+    ts(V("SL", 3, 4), V("PJ", 1, 2), -1.0, A.mult, 3.0, A.add)
+    ts(V("SL", 6, 7), V("PJ", 3, 4), 8.0, A.mult)
+    ts(V("SL", 7, 8), V("PJ", 3, 4), 8.0, A.mult, 2.0 * P, A.add)
     ts(V("SEG4"), V("J4"), 1.0, A.min)
     lin(V("PKC"), V("SEG4"), -3.0, 4.0)
     lin(V("PKC", 0, 64, 32), V("ZERO", 0, 2))
@@ -311,45 +535,42 @@ def rank_program(g, core, T, topo):
     ms(V("BAR", 1, 32, 4), 1.5)
     ms(V("BAR", 3, 32, 4), BIG)
     lin(V("GD", 0, 1), p96, 8.0, float(-P * me))
-    lin(V("GD", 1, 2), V("BC", 0, 1), -1.0, V("GD", 0, 1))
 
     def more_fills():
         fill(V("W1", 0, 256), 0)
         fill(V("XI"), 0, pattern=[[0, 2], [1, 2], [0, 8]])
         ts(V("XM"), V("XI"), odd, A.is_equal)
+        lin(V("XB"), V("XM"), -1000.0, 1000.0)
+        ms(V("SEG8"), 1.0)
+        ms(V("SEG8", 0, 128, 8), 0.0)
         fill(V("W2", 0, 256), 0)
 
     def constants():
-        for c in range(0, 544, 109):
-            ms(V("ZB", c, min(544, c + 109)), 0.0)
+        for c in range(0, 272, 68):
+            ms(V("ZB", c, c + 68), 0.0)
         ms(V("FL", 0, 192, 3), 0.0)
         ms(V("FL", 1, 192, 3), -1.0)
         for t in (1, 2):
             ms(V("D1%d" % t, 1, 96, 3), -TINY)
         for d in range(4):
-            ms(sub(zb(0, 0, 8), (d - me) % 4, 8, d, 4), 65535.0)
+            ms(blk(d, "KB", (d - me) % 4, 8, 4), 65535.0)
         ts(V("SEGT"), V("J4", 0, 40), 1.5, A.is_gt)
         lin(V("SEGT", 4, 33, 4), V("TR"))
-        ts(V("MASK"), V("J16"), p15, A.is_equal)
-        ts(V("SEG16"), V("J16"), 1.0, A.min)
-        ts(V("SUF", 0, 31), V("J32", 0, 31), p31, A.is_ge)
-        ms(V("SUF", 31, 32), -1.0)
-        ms(V("SUF", 32, 64), 1.0)
+        ts(V("SUF", 0, 31), V("J32", 1, 32), p31, A.is_equal, 1.0 / FAINT - 1, A.mult)
+        lin(V("SUF", 0, 31), V("SUF", 0, 31), 1.0, 1.0)
+        ms(V("SUF", 31, 32), FAINT)
         kc = [V("KCOL", j, j + 1) for j in range(4)]
         lin(kc[0], kcol, 8.0, p4)
         lin(kc[1], p15, 4.0)
         lin(kc[2], p4, 4.0)
-        lin(kc[3], p7, 4.0, p8)
         tb = lambda name: tab(name, buf="TB")
         lin(tb("DUP"), V("DUPF"), 1.0, kc[1])
         lin(tb("PERM"), V("J32", 0, 2), 4.0, kc[0])
         lin(tb("PV"), V("J32", 0, 2), 4.0, p4)
         lin(tb("P8"), V("ZERO", 0, 2), 1.0, p7)
-        lin(tb("XA"), tb("P8"), 4.0, 3.0)
-        lin(tb("KO"), V("J32", 0, 2), 2.0, kc[3])
-        lin(tb("KX"), V("J4", 0, 8, 2), 2.0, kcol)
+        lin(tb("KX"), V("J32", 0, 2), 4.0, kcol)
         lin(tb("MX"), V("DUPF", 0, 4), 1.0 / 16, p4)
-        lin(tb("FX"), V("J32", 0, 4), 16.0, kc[2])
+        lin(tb("FX"), V("J32", 0, 2), 16.0, kc[2])
         tc(V("TU"), V("TB"))
         scan(V("POW"), V("FOUR"), V("ZERO", 0, 8), A.mult, A.add, 0.25)
         gata(V("MULT"), V("POW"), tab("MX"))
@@ -368,82 +589,119 @@ def rank_program(g, core, T, topo):
             o = 32 * h + 16 * (t - 1)
             ts(V(out, 4 * h, 4 * h + 4), V("SCL", o + 3, o + 16, 4), V("SL", 2, 3), A.subtract)
 
+    def first_lists():
+        for z in (0, 64):
+            for h in range(2):
+                ts(V("RB", 16 * h, 16 * h + 16, 1, z, z + 64), V("RA", h, 32, 2, 0, 64), V("SL", z // 16, z // 16 + 1, 1, 0, 64), A.max,
+                   V("SL", z // 16 + 1, z // 16 + 2, 1, 0, 64), A.min)
+        tr(V("RC"), V("RB"))
+        for h in range(2):
+            scan(V("RD", 16 * h, 16 * h + 16), V("SEG4", 0, 16), V("RC", h, 32, 2), A.mult, A.add)
+        for h in range(2):
+            ts(V("MSG1", h, 8, 2), V("RD", 16 * h + 3, 16 * h + 16, 4), V("SL", 2, 3), A.subtract)
+
     def prep_ties():
-        tc(V("TI"), V("T2"))
-        tt(V("TK"), V("TI"), V("T2"), A.is_equal)
-        scan(V("SK"), V("SEG4"), V("TK"), A.mult, A.add)
+        ts(V("TI", p1=64), V("RAW", p1=64), 3 * P, A.bitwise_and)
+        for z in (0, 64):
+            ts(V("TK", p0=z, p1=z + 64), V("TI", p1=64), V("SL", 6 + z // 64, 7 + z // 64, 1, 0, 64), A.is_equal,
+               V("SL", 3, 4, 1, 0, 64), A.mult)
+        for h in range(2):
+            tr(V("SK", 32 * h, 32 * h + 32), V("TK", h, 64, 2))
         scan(V("PK"), V("PKC"), V("SK"), A.mult, A.add)
-        ts(V("MSG2"), V("PK", 31, 64, 32), float(0x5555), A.subtract)
+        tc(V("MSG2"), V("PK", 31, 64, 32))
 
     def own_columns(t):
         b = bufs(t)
-        tc(b("LCN"), V("MSG1") if t == 1 else V("LS2"))
+        tc(b("LCN"), b("LS"))
         for k in [me] + others:
             lin(blk(k, "OL%d" % t), blk(me, "LCN%d" % t))
-        lin(sub(zb(t, 104, 32), 3, 32, me, 4), blk(me, "LCN%d" % t))
-        lin(sub(zb(t, 72, 32), 3, 32, me, 4), blk(me, "LCN%d" % t), 1.0, float(P * me))
-        for h in range(2):
-            lin(b("OB", 8 * h, 8 * h + 8), b("OL"), -1.0, V("BC", 0, 1))
-        lin(b("IC", 0, 8), b("LCN"), 1.0, V("GD", 1, 2))
+        lin(blk(me, "OG%d" % t), blk(me, "LCN%d" % t), 1.0, float(P * me))
+        lin(b("IC", 0, 8), b("LCN"), 1.0, V("GD", 0, 1))
+        tt(b("SV"), b("IC", 0, 8), b("OL"), A.subtract)
+        tti(b("AO"), b("LCN"), tab("P8"), V("XM"), A.mult)
+        tr(blk(me, "TA%d" % t, 0, 128, 4), blk(me, "AO%d" % t))
 
     def decode_ties():
-        ka = zb(0, 0, 8)
+        ka = V("KB")
         tc(V("KW", 6, 8), V("MSG2"))
         for s in others:
             lin(sub(ka, (s - me) % 4, 8, me, 4), blk(s, "KW", 6, 8))
-        tc(V("KW", 0, 2), V("LM2", 0, 2))
+        tc(V("KW", 0, 6), V("LM2"))
         for j, d in enumerate(others):
             for s in range(4):
                 if s != d:
-                    (tc if j else lin)(sub(ka, (s - me) % 4, 8, d, 4), blk(s, "LM2" if j else "KW", 2 * j, 2 * j + 2))
-        tti(V("KI"), ka, tab("KX"), V("MULT"), A.mult)
+                    (tc if j == 1 else lin)(sub(ka, (s - me) % 4, 8, d, 4), blk(s, "LM2" if j == 1 else "KW", 2 * j, 2 * j + 2))
+
+    def lower(t):
+        b = bufs(t)
+        tti(b("KI"), V("KB"), tab("KX"), V("MULT", 32 * t - 32, 32 * t), A.mult)
         for name in ("KD", "KE"):
-            ts(V(name), V("KI"), 0xC000, A.bitwise_and)
-        tti(V("FL", 2, 192, 3), V("KD"), tab("FX"), V("KE"), A.is_lt)
+            ts(b(name), b("KI"), 0xC000, A.bitwise_and)
+        tti(V("FL", 96 * t - 94, 96 * t, 3), b("KD"), tab("FX"), b("KE"), A.is_lt)
 
     def own_keys(t):
-        o, w, off = V("KK%d" % t), V("KD", 32 * t - 32, 32 * t), tab("KO")
-        op("v", lambda: g.vector.tensor_scalar(ap(o), ap(w).indirect(ap(off)), 2.0 ** -14, 1.0, A.mult, A.add), [w, off], [o])
+        ts(V("KK%d" % t), V("KD%d" % t), 2.0 ** -14, A.mult, 1.0, A.add)
 
     def value_rows(t):
         b = bufs(t)
-        gata(b("D1", 0, 96, 3), b("U", 0, 8), tab("PV"), AF.Abs, scale=STEP)
-        gatx(b("D1", 2, 96, 3), b("U", 0, 8), tab("PV"))
+        own = b("SG", 64, 72)
+        gata(b("D1", 0, 96, 3), own, tab("PV"), AF.Abs, scale=STEP)
+        gatx(b("D1", 2, 96, 3), own, tab("PV"))
         gata(b("VR"), V("IDT"), b("LU"))
 
     def thresholds(t):
         b = bufs(t)
+        lower(t)
         scan(b("VA"), V("FL", 96 * t - 96, 96 * t), b("D1"), A.mult, A.add)
 
     def scores_out(t):
         b = bufs(t)
-        tti(b("G"), V("S%d" % (t - 1), 0, P), b("LU"), V("MASK"), A.mult)
-        scan(b("SG"), V("SEG16"), b("G"), A.mult, A.add)
-        lin(b("U", 0, 8), b("SG", 15, 128, 16))
-        return spread(b("U", 0, 8), lambda s: b("U", 8 + 8 * s, 16 + 8 * s), "v%d" % t, "lv%d" % t, b("U", 8, 32))
+        for h in range(2):
+            gatx(b("G", 64 * h, 64 * h + 64), V("S%d" % (t - 1), 0, P), b("LA", 4 * h, 4 * h + 4))
+        for j in range(4):
+            tr(b("SG", 4 + j, 132, 4), b("G", 32 * j, 32 * j + 32))
+        lin(b("U", 0, 8), b("SG", 64, 72))
+        return spread(b("SG", 64, 72), lambda s: b("U", 8 + 8 * s, 16 + 8 * s), "v%d" % t, "lv%d" % t, b("U", 8, 32))
+
+    def turn_lists(t):
+        b = bufs(t)
+        if t == 2:
+            for h in range(2):
+                tc(V("LB", h, 8, 2), V("LU2", 4 * h, 4 * h + 4))
+        gata(b("GI"), V("IDT"), V("LA1" if t == 1 else "LB"))
+        for j in range(4):
+            tr(b("GT", j, 128, 4), b("GI", 32 * j, 32 * j + 32))
+        if t == 1:
+            tc(V("LU1"), b("GT", 60, 68))
+        else:
+            for h in range(2):
+                tc(V("LA2", h, 8, 2), b("GT", 60 + 4 * h, 64 + 4 * h))
 
     def choose_and_send(t):
         b = bufs(t)
-        worse = zb(t, 136, 96)
+        worse = zb(t, 72, 64)
         tti(sub(worse, 0, 32), b("U"), tab("PERM"), b("VA", 2, 96, 3), A.is_gt)
         scan(b("NI"), worse, V("BAR"))
         scan(b("BT", 0, 33), V("SEGT", 0, 33), sub(worse, 0, 33), A.mult, A.max)
-        tr(b("RT"), b("NI", 32, 96))
+        tr(b("RT"), b("NI", 32, 64))
         tt(b("AA"), b("BT", 4, 33, 4), b("NI", 4, 33, 4), A.subtract)
         scan(b("SFX"), b("RT"), V("SUF"), A.add, A.mult)
-        ts(b("OF"), b("AA"), b("SFX", 63, 64), A.subtract, 4.0, A.subtract)
+        ts(b("OF"), b("AA"), b("SFX", 31, 32), A.subtract, 4.0, A.subtract)
         op("v", lambda: g.vector.tensor_copy(ap(b("W")).indirect(ap(b("OF"))), ap(b("VR"))), [b("VR"), b("OF")], [b("W")])
-        gat(b("WD", 0, 96), b("W", 0, 256), tab("DUP", 0, 6))
-        gata(b("WD", 96, 128), b("W", 0, 256), tab("DUP", 6, 8))
-        for i, d in enumerate(others):
+        gat(b("WD", 0, 64), b("W", 0, 256), tab("DUP", 0, 4))
+        gata(b("WD", 64, 128), b("W", 0, 256), tab("DUP", 4, 8))
+        for i, d in enumerate(turn):
             tr(blk(me, "TW%d" % t, 128 * i, 128 * i + 128), blk(d, "WD%d" % t))
         for k in range(2):
             tt(blk(k, "PF%d" % t, 0, 12), blk(me, "TW%d" % t, 0, 384, 32), blk(me, "TW%d" % t, 16, 384, 32), A.add)
         for h in range(2):
             tc(b("PO", 0, 12, 1, 64 * h, 64 * h + 64), b("PF", 0, 12, 1, 0, 64))
-        pick(b("SQ"), b("SS"), V("QO%d" % (t - 1)), V("QS%d" % (t - 1)), b("PO"))
-        each("SQ%d" % t, 64, "QW%d" % (t - 1), "c%d" % t, "lc%d" % t)
-        return each("SS%d" % t, 64, "QP%d" % (t - 1), "s%d" % t, "ls%d" % t, 1)
+        for lo, hi in ((0, 2), (2, 3)):
+            pick(b("SQ", 64 * lo, 64 * hi), b("SS", 64 * lo, 64 * hi), V("QO%d" % (t - 1)), V("QS%d" % (t - 1)), b("PO", 4 * lo, 4 * hi))
+        e = topo.engines(core, T.cores[turn[0]])[:16]
+        columns("SQ%d" % t, "QW%d" % (t - 1), {0: e[1::2], 1: e[0::2]}, "c%d" % t, 24, "lc%d" % t, 16)
+        columns("SQ%d" % t, "QW%d" % (t - 1), {2: e[0::2]}, "c%d" % t, 24, "lc%d" % t, 24)
+        columns("SS%d" % t, "QP%d" % (t - 1), {0: e[0::2], 1: e[1::4], 2: e[3::4]}, "s%d" % t, 16, "ls%d" % t, 16)
 
     def own_list(t):
         b = bufs(t)
@@ -451,42 +709,45 @@ def rank_program(g, core, T, topo):
         tt(b("M16"), b("U", 0, 16), b("U", 16, 32), A.max)
         tt(b("MM"), b("M16", 0, 8), b("M16", 8, 16), A.max)
         tti(b("EQ"), b("MM"), tab("P8"), b("U"), A.is_equal)
-        tt(mk("KEY"), mk("EQ"), mk("KK"), A.mult)
-        tt(mk("K16"), mk("KEY", 0, 16), mk("KEY", 16, 32), A.max)
-        tt(mk("KM"), mk("K16", 0, 8), mk("K16", 8, 16), A.max)
-        wb, ic, bk = zb(t, 0, 72), b("IC", 8, 80), zb(t, 72, 64)
+        tti(b("KEY"), b("EQ"), tab("PERM"), b("KK"), A.mult)
+        scan(b("KM"), V("SEG4", 0, 32), b("KEY"), A.mult, A.max)
+        wb, ic = zb(t, 0, 40), b("IC", 8, 48)
         for i, s in enumerate(others):
-            tt(sub(wb, 0, 8, s), mk("KEY", 8 * i + 8, 8 * i + 16), mk("KM"), A.is_equal)
-        scan(ic, wb, V("ZERO", 0, 72))
-        tr(b("RC"), sub(ic, 8, 72))
+            tt(sub(wb, 0, 8, s), mk("KEY", i + 1, 32, 4), mk("KM", 3, 32, 4), A.is_equal)
+        scan(ic, wb, V("ZERO", 0, 40))
+        tr(b("RC"), sub(ic, 8, 40))
         scan(b("SFC"), b("RC"), V("SUF"), A.add, A.mult)
         lin(b("NW"), sub(wb, 0, 8), -1000.0, 1000.0)
         tt(b("NP"), sub(ic, 0, 8), b("NW"), A.add)
-        tt(b("SV"), b("IC", 0, 16), b("OB"), A.add)
-        for h in range(2):
-            ts(b("KP", 8 * h, 8 * h + 8), b("NP"), b("SFC", 63, 64), A.add, float(CAPP), A.is_le)
-        lin(b("SV", 8, 16), b("SV", 8, 16), 1.0, b("SFC", 63, 64))
+        tti(b("NQ"), b("NP"), tab("P8"), V("XB"), A.add)
+        ts(b("KR"), b("NQ"), b("SFC", 31, 32), A.add, CAPP + 0.5, A.is_le)
+        o, w, off, s1, s2 = b("SR"), sub(ic, 0, 8), tab("P8"), b("SFC", 31, 32), V("BC", 0, 1)
+        op("v", lambda: g.vector.tensor_scalar(ap(o), ap(w).indirect(ap(off)), ap(s1), ap(s2), A.add, A.add), [w, off, s1, s2], [o])
+        tt(b("A2"), b("KR"), b("SR"), A.mult)
         for i, s in enumerate(others):
-            tt(sub(bk, i, 64, me, 4), blk(s, "KP%d" % t), blk(s, "SV%d" % t), A.mult)
-        scan(b("XS"), V("SEG4"), bk, A.mult, A.add)
-        tti(b("A2"), b("XS", 32, 64), tab("XA"), V("XM"), A.mult)
-        tr(mk("TA"), mk("A2"))
+            tr(mk("TA", i + 1, 128, 4), blk(s, "A2%d" % t))
         half = me // 2
         for k in (2 * half, 2 * half + 1):
-            tt(blk(k, "XT%d" % t), mk("TA", 0, 32, 2), mk("TA", 1, 32, 2), A.add)
+            scan(blk(k, "XT%d" % t), blk(me, "SEG8"), mk("TA"), A.mult, A.max)
         for h in range(2):
-            tc(V("XO%d" % t, p0=64 * h, p1=64 * h + 64), V("XT%d" % t, p0=64 * half, p1=64 * half + 64))
+            tc(V("XO%d" % t, p0=64 * h, p1=64 * h + 64), V("XT%d" % t, 7, 128, 8, 64 * half, 64 * half + 64))
+
+    def own_choice(t):
+        b = bufs(t)
+        mk = lambda name, *a: blk(me, name + str(t), *a)
+        bk = zb(t, 40, 32)
+        ts(b("KP"), b("NP"), b("SFC", 31, 32), A.add, CAPP + 0.5, A.is_le)
+        for i, s in enumerate(others):
+            tt(sub(bk, i, 32, me, 4), blk(s, "KP%d" % t), blk(s, "SV%d" % t), A.mult)
+        scan(b("XS"), V("SEG4", 0, 32), bk, A.mult, A.add)
+        tt(mk("CH"), mk("XS", 3, 32, 4), mk("OG"), A.add)
+        dma("sa", T.ch[t - 1:t, :], ap(mk("CH")), [mk("CH")], [])
         if t == 2:
-            ts(mk("KQ"), mk("XS", 35, 64, 4), P - 0.5, A.is_lt, HUGE, A.mult)
+            ts(mk("KQ"), mk("XS", 3, 32, 4), 0.0, A.is_equal, HUGE, A.mult)
             tt(mk("PP"), mk("MM"), mk("KQ"), A.subtract)
             tt(mk("PA"), mk("PP"), mk("U", 0, 8), A.max)
             pr = V("PR2", 0, 256, 1, 0, 1)
             dma("sa", ap(pr), ap(mk("PA")), [mk("PA")], [pr])
-
-    def own_choice(t):
-        mk = lambda name, *a: blk(me, name + str(t), *a)
-        lin(mk("CH"), mk("XS", 3, 32, 4))
-        dma("sa", T.ch[t - 1:t, :], ap(mk("CH")), [mk("CH")], [])
 
     def products(t, i, arrived):
         q, s, n, o = ("QW", "QP", 192, 256) if arrived else ("QO", "QS", 256, 0)
@@ -534,9 +795,12 @@ def rank_program(g, core, T, topo):
         qz(V("AQ", 128 * i, 128 * i + 128), V("AP", 128 * i, 128 * i + 128), V("AT", 512 * i, 512 * i + 512))
         products(1, i, False)
 
+    first_lists()
     prep_lists()
-    list_of(1, "MSG1")
-    spread(V("MSG1"), lambda s: V("LM1", 8 * s, 8 * s + 8), "m1", "lm1", V("LM1"))
+    list_of(1, "LS1")
+    lists = spread(V("MSG1"), lambda s: V("LM1", 8 * s, 8 * s + 8), "m1", "lm1", V("LM1"), 0, 2)
+    load("sa", V("AT", 0, 1024), T.a[:, 0:1024])
+    load("sa", V("AT", 1024, 2048), T.a[:, 1024:2048], [lists])
     for i in range(4):
         lin(V("UT", i, 512, 4), V("ZERO"), 1.0, V("UC", i, i + 1))
     qz(V("UQ"), V("UP"), V("UT"))
@@ -544,21 +808,21 @@ def rank_program(g, core, T, topo):
     lin(V("S0", 0, P), mm(0, 256, V("UQ"), V("UP"), V("QO0"), V("QS0")))
     list_of(2, "LS2")
     prep_ties()
-    ties = spread(V("MSG2"), lambda s: V("LM2", 2 * s, 2 * s + 2), "m2", "lm2", V("LM2"))
+    spread(V("MSG2"), lambda s: V("LM2", 2 * s, 2 * s + 2), "m2", "lm2", V("LM2"), 1, 2)
     fill(V("IDT"), 0, 1)
     constants()
     for i in range(2):
         quantise_a(i)
     for d in others + [me]:
-        tc(blk(d, "LU1"), blk(me, "MSG1") if d == me else blk(me, "LM1", 8 * others.index(d), 8 * others.index(d) + 8))
+        tc(blk(d, "LA1"), blk(me, "MSG1") if d == me else blk(me, "LM1", 8 * others.index(d), 8 * others.index(d) + 8))
     tc(blk(me, "LU2"), blk(me, "LS2"))
     scores = scores_out(1)
+    turn_lists(1)
     more_fills()
-    load("sa", V("AT", 1024, 2048), T.a[:, 1024:2048], [scores])
     load("sa", V("E1"), T.e1[:], [scores])
     own_columns(1)
     for i, d in enumerate(others):
-        dma("sa", ap(V("ST2", 2 * i, 2 * i + 2)), ap(blk(d, "LS2")), [blk(d, "LS2")], [V("ST2", 2 * i, 2 * i + 2)], [ties])
+        dma("sa", ap(V("ST2", 2 * i, 2 * i + 2)), ap(blk(d, "LS2")), [blk(d, "LS2")], [V("ST2", 2 * i, 2 * i + 2)], [lists])
     value_rows(1)
     decode_ties()
     thresholds(1)
@@ -570,6 +834,7 @@ def rank_program(g, core, T, topo):
     for i in range(2, 4):
         quantise_a(i)
     own_list(1)
+    turn_lists(2)
     new_columns(1)
     scores = scores_out(2)
     load("sa", V("WT"), T.w[:], [scores])
@@ -588,4 +853,5 @@ def rank_program(g, core, T, topo):
     new_columns(2)
     lay()
     for sem in sorted(total):
-        wait("s", [(sem, total[sem], {})])
+        if all(know[q].get(sem, 0) < total[sem] for q in qs):
+            wait("s" if sem == "out" else "g", [(sem, total[sem], {})])

from concourse.bass import DstId, RemoteDMATransfer
from concourse.mybir import dt, AluOpType as A, ActivationFunctionType as AF

P, CAPP = 256, 64
TINY = 2.0 ** -100
STEP = 2.0 ** -24 * (1 + 2.0 ** -10)
BIG = 1.5 * 2.0 ** 25
FAINT = 2.0 ** -13
HUGE = 1e29
F, B, I, H, C, S8 = "float32", "bfloat16", "int32", "uint16", "float8_e4m3fn_x4", "uint8"
SCRATCH = {"PS": ("psum", [128, 4096], F)}
PLACE = {"PS": ("PS", 0, 4096)}


def _buf(dtype, **names):
    for k, n in names.items():
        SCRATCH[k] = ("sbuf", [128, n], dtype)
        PLACE[k] = (k, 0, n)


def _area(dtype, **names):
    k = "W" + dtype
    for name, n in names.items():
        at = SCRATCH[k][1][1] if k in SCRATCH else 0
        PLACE[name] = (k, at, n)
        SCRATCH[k] = ("sbuf", [128, at + (n + 15) // 16 * 16], dtype)


def _each(**names):
    return {n + str(t): w for t in (1, 2) for n, w in names.items()}


_buf(B, UC=4, UT=512, E0=1024, AT=2048, WT=512, E1=1024, E2=1024, HT1=1024, HT2=1024)
_buf(C, UQ=128, AQ=512, WQ=128, QO0=256, QO1=256, QO2=256, QW0=192, QW1=192, SQ1=192, SQ2=192)
_buf(S8, UP=128, AP=512, WP=128, QS0=256, QS1=256, QS2=256, QP0=192, QP1=192, SS1=192, SS2=192)
_buf(H, MSG1=8, MSG2=2, LM1=24, LM2=6, LS2=8, ST2=6, LC2=6, LU1=8, LU2=8)
_buf(F, ZERO=128, U1=32, U2=32, Z1=1792, Z2=1792, YB=256, S0=448, S1=256, S2=256, PR2=256, PB1=256)
_buf(I, RAW=64, RA=32)
_area(H, TU=22, LS1=8, LA1=8, LA2=8, LB=8)
_area(I, PI=1, PJ=7, TI=64, KI1=32, KI2=32, KD1=32, KE1=32, KD2=32, KE2=32)
_area(F, BAR=64, SEGT=40, KCOL=8, SL=8, XM=32, XI=32, GD=4, BC=4, TR=8, ZB=272, PF32=7, J4=64, SEG4=64,
      SUF=32, FOUR=8, J32=32, IDT=256, PKC=64, KW=8, FL=192, RL=64, T2=64, SCL=64, TK=64, SK=64, PK=64,
      TB=22, DUPF=8, POW=8, MULT=64, KB=8, XB=32, SEG8=128, RB=32, RC=32, RD=32)
_area(F, **_each(GI=128, GT=128, LCN=8, OL=8, OG=8, AO=32, KK=32, G=128, SG=132, D1=96, VA=96, BT=40, NI=64, RT=32,
                 SFX=32, AA=8, PF=16, M16=16, MM=8, EQ=32, KEY=32, KM=32,
                 IC=48, RC=32, SFC=32, KP=8, SV=8, NQ=32, KR=32, SR=32,
                 NW=8, NP=8, CH=8, XS=32, A2=32, TA=128, XT=128, KQ=8, PP=8, PA=8))
_area(B, **_each(VR=128, W=6208, WD=128, TW=384))
_area(H, **_each(OF=8, PO=12, XO=16))
TAB = dict(DUP=(0, 8), PERM=(8, 10), PV=(10, 12), P8=(12, 14), KX=(14, 16), MX=(16, 20), FX=(20, 22))
WIDE = (3, 3)
NDMA = 60
SEMAPHORES = ["out", "qv", "qa", "qt", "qg", "m1", "lm1", "m2", "lm2", "m3", "lm3"] + ["d%d" % i for i in range(NDMA)] + [
    x + str(t) for t in (1, 2) for x in ("v", "lv", "c", "lc", "s", "ls")]
ORDER = """
RAW.2s RAW.1a PI.0g J4.0g RAW.0s RAW.3a PJ.3v PJ.7v PJ.1v ZERO.0g PJ.5v UC.0s E0.1a PJ.4v SL.3v SL.1v SL.2v SL.0v E0.0s AT.0s
PJ.2v J16.0g PJ.6v PJ.0v FL.0a D11.0a D12.0a FOUR.0g BC.2a BC.3a TR.0g BC.0a ZB.0a J32.0g RL.1v DUPF.0g RL.0v SEG4.0v PF32.0v
T2.1v T2.0v PKC.0a SL.4v BC.1a SCL.1v SCL.0v TI.0v PKC.1a MSG1.1v TB.3a MSG1.0v ZB.6v KCOL.1a TK.0v ZB.7a oMSG1.0g _LM1.0x
UT.3v TB.6a UT.0a SK.0v LS2.0v LCN1.0v KCOL.0a TB.0v UT.1a TB.4a TB.1v PK.0v KCOL.2a TB.2v LS2.1v TB.7a MSG2.0v UT.2a TB.8a
QO0.0v ZB.4a SUF.1a OL1.3a GD.0v KW.0v OL1.1a UQ.0v BAR.0a SUF.0v KCOL.3a PS0.0t BAR.2v LCN2.0v TB.5a oMSG2.0g _LM2.0x
SEG16.0v BAR.1a POW.0v ZB.13a MASK.0v GD.1a AQ.0v ZB.3a AQ.1v XI.0g ZB.8a ZB.11v IC2.0a TU.0v OL2.2v ZB.1a IDT.0g PS5.0t
LU1.3v S0.0a OL1.0a PS4.0t FL.1a ZB.12a LU1.1v MULT.0a LU1.2v LU1.0v OL2.1v ZB.30a ZB.5v OL2.0a G1.0v ST2.1s ST2.2s KW.1v
ZB.18v ZB.20v ZB.22v ST2.0s ZB.15a SG1.0v ZB.14a ZB.21v ZB.19v ZB.16a ZB.17v U1.0v ZB.9a XM.0v Z1.0a KI.0v oU1.0g _U1.0x
D11.2v ZB.2a KD.0v KE.0v IC1.0a BAR.3a FL.2v D11.1a SEGT.0v OL1.2a SUF.2v ZB.10a VA1.0v OB1.0a KK1.0v OB1.1a VR1.0a
oST2.0g _LC2.0x SEGT.1a E1.0s W1.0g AT.1s
ZB.23v M161.0v NI1.0v BT1.0v MM1.0v RT1.0v W2.0g AA1.0v EQ1.0v SFX1.0v KEY1.0v OF1.0v K161.0v W1.1v LU2.3s KM1.0v LU2.2s
LU2.0v WD1.0v WD1.1a ZB.26v LU2.1s ZB.25v ZB.24v TW1.1v TW1.2v TW1.0v NW1.0a IC1.1v PF1.0v PF1.1v RC1.0v SV1.0v PO1.1v
PO1.0v NP1.0v SFC1.0v SQ1.0v SV1.1a KP1.0v SS1.0a KP1.1v AQ.2v oSQ1.0g _QW0.0x ZB.28v Z1.1a ZB.27v ZB.29v PS6.0t AQ.3v
XS1.0v oSS1.0g _QP0.0x A21.0v PS7.0t TA1.0v XT1.0v XT1.1v Z1.3a XO1.1v XO1.0v Z1.2a
PS0.1t PS1.0t Z1.4v PS2.0t Z1.5a HT1.0v PS3.0t Z1.6a HT1.1v PS6.1t Z1.7a HT1.2v CH1.0a S0.1a HT1.3v HT1.4v PB1.0a
QO1.0v QO1.1v PS4.1t PS5.1t S1.0v PS7.1t S1.1v PS6.2t G2.0v KK2.0v SG2.0v PS4.2t U2.0v D12.2v PS5.2t D12.1a oU2.0g _U2.0x
VR2.0a VA2.0v OL2.3v Z2.1v OB2.1a Z2.0a ZB.31v OB2.0a Z2.3a E2.0s oCH1.0s
ZB.32v M162.0v WT.0s NI2.0v BT2.0v MM2.0v RT2.0v AA2.0v EQ2.0v SFX2.0v KEY2.0v OF2.0v K162.0v W2.1v KM2.0v WD2.0v WD2.1a
ZB.34v ZB.33v ZB.35v TW2.1v TW2.2v TW2.0v NW2.0a IC2.1v Z2.2a PF2.0v PF2.1v RC2.0v NP2.0v PO2.0v PO2.1v SFC2.0v SV2.0v
SQ2.0v SS2.0a KP2.1v SV2.1a KP2.0v oSQ2.0g _QW1.0x ZB.38v ZB.37v ZB.36v WQ.0v XS2.0v oSS2.0g _QP1.0x A22.0v CH2.0a KQ2.0v
TA2.0v PP2.0v XT2.0v XT2.1v XO2.1v XO2.0v
PS3.1t PS1.1t Z2.7v PS0.2t PA2.0v Z2.5a HT2.3v PR2.0s PS2.1t HT2.5v Z2.4a oCH2.0s HT2.1v Z2.6a HT2.0v HT2.4v HT2.2v
QO2.1v QO2.0v oQO2.1s PS7.2t oQS2.1a PS6.3t oQO2.0s YB.1v oQS2.2a PS4.3t oQS2.0s YB.0a PS5.3t oQS2.3a S2.0v oYB.1s S2.1v
oYB.0s oS2.0a
"""


ORDER = """
PI.0g RAW.2s PV.0v RAW.1a RAW.0s ZERO.0g RAW.3a UC.0s PJ.1v J4.0g PJ.2v PJ.0v SL.3v E0.1a SL.2v SL.1v SL.0v BC.2a KA.2a E0.0s
BC.1a BC.0a KA.0a PJ.5v PJ.3v RL.1v RL.0v AT.0s SEG4.0v FL.0a BAR.0a TR.0g SL.4v UT.3a J32.0g UT.0a PJ.4v UT.1a PKC.0a T2.1v
DUPF.0g T2.0v FOUR.0g ZB.0a PJ.6v SCL.1v SCL.0v TI.0v J16.0g PF32.0v UT.2a MSG1.1v MSG1.0v oMSG1.0g _LM1.0x KA.3a TK.0v QO0.0v
SK.0v PKC.1a IDT.0g D11.0a UQ.0v TB.4a KCOL.2a LU1.3v KV.0v KA.1a TB.3a TB.2a FL.1a TB.5a PS0.0t PK.0v LS2.0v LS1.0v KCOL.0a
XI.0g KCOL.1a KA.14a KA.13a SUF.1a GD.0a SEG16.0v W1.0g MASK.0v LS2.1v S0.0a ST2.2v TB.6a ST2.1v ST2.0v KB.3a LU1.2v LU1.1v
LU1.0v KV.1v W2.0g KA.15a ST2.4s TB.0a TB.1a KA.6a ST2.5s LCN1.0v G1.0v KA.7a KA.4a KA.11a KA.12a KA.5v KA.10v KA.8a ST2.3s
KA.9v BC.3a KB.0a BAR.1a SG1.0v KB.2a U1.0a oST2.0g _LC2.0x oU1.0g _U1.0x SEGT.0v KR.0v SUF.2v BAR.2v TU.0v SUF.0v KE1.0v
KD1.0v AQ.1v BAR.3a D11.2v FL.2v AQ.0v E1.0s OL1.3a SEGT.1a KB.1a D11.1a OL1.1a XM.0v VA1.0v AT.1s KK1.0v KW.0v ZB.1a OL1.2v
ZB.4v KB.4v M161.0v PS5.0t PS4.0t SEG8.0a NI1.0v BT1.0v SEG8.1a MM1.0v KW.1v RT1.0v VR1.0a OG1.0a AA1.0v EQ1.0v SFX1.0v AO1.0v
LU2.3s KEY1.0v KB.6a LU2.2s KB.9a Z1.0a OF1.0v XB.0a KM1.0v W1.1v ZB.6v KB.7a ZB.5v KB.12a WD1.1a ZB.7v WD1.0v TA1.0v IC1.1v
TW1.2v KB.13a TW1.0v TW1.1v LU2.1s RC1.0v NW1.0a KB.15a NP1.0v PF1.1v PF1.0v IC1.0a SFC1.0v NQ1.0v D12.0a PO1.0v PO1.1v SR1.0v
OL1.0a KR1.0v KB.11a SQ1.0v A21.0v AQ.2v ZB.3a PS6.0t Z1.1a KB.5a AQ.3v TA1.2v SV1.0v KP1.0v TA1.1v KB.8a TA1.3v ZB.8v ZB.9v
ZB.2a oSQ1.0g _QW0.0x SS1.0a ZB.10v oSS1.0g _QP0.0x PS7.0t Z1.3a POW.0v XT1.1v PS0.1t LCN2.0v PS3.0t XT1.0v KB.10v OL2.0v
MULT.0a XO1.0v XO1.1v KB.14a PS2.0t Z1.4a Z1.2a Z1.7a LU2.0v XS1.0v KI.0v PS1.0t Z1.6a CH1.0v HT1.0v HT1.3v Z1.5a PS6.1t
HT1.2v HT1.1v HT1.4v S0.1a QO1.0v QO1.1v AO2.0v PS4.1t KD2.0v PB1.0a PS5.1t VR2.0a KE2.0v S1.0v S1.1v OG2.0v G2.0v SG2.0v
OL2.3a oSG2.0g U2.0v _U2.0x D12.1a KK2.0v D12.2v FL.3v E2.0s VA2.0v OL2.2a ZB.11v M162.0v IC2.0a PS4.2t NI2.0v PS6.2t oCH1.0s
WT.0s BT2.0v MM2.0v RT2.0v Z2.0a AA2.0v EQ2.0v PS5.2t PS7.1t SFX2.0v TA2.0v KEY2.0v OF2.0v KM2.0v W2.1v WD2.1a ZB.12v ZB.13v
ZB.14v WD2.0v IC2.1v NW2.0v TW2.0v Z2.2a TW2.1v TW2.2v NP2.0v RC2.0v Z2.3a Z2.1a PF2.1v OL2.1a PF2.0v SFC2.0v NQ2.0v PO2.0v
PO2.1v SR2.0v KR2.0v SQ2.0v SS2.0a SV2.0v A22.0v oSQ2.0g _QW1.0x KP2.0v TA2.2v ZB.17v ZB.16v TA2.1v WQ.0v ZB.15v oSS2.0g
_QP1.0x TA2.3v XS2.0v XT2.0v PS3.1t XT2.1v PS0.2t KQ2.0v CH2.0v PP2.0v XO2.0v XO2.1v Z2.7a PS1.1t PA2.0v Z2.5a PR2.0s
oCH2.0s PS2.1t HT2.3v Z2.6a HT2.4v HT2.1v Z2.4a HT2.0v HT2.2v QO2.1v QO2.0v oQO2.1s oQS2.1a PS7.2t PS5.3t oQO2.0s PS6.3t
oQS2.2a YB.1v PS4.3t S2.1v S2.0v YB.0a oQS2.0s oQS2.3a oYB.1s oYB.0s oS2.0a
"""


def _moved(order, moves):
    o = order.split()
    for line in moves.strip().split("\n"):
        after, *ws = line.split()
        o = [w for w in o if w[:-1] not in [x[:-1] for x in ws]]
        i = [w[:-1] for w in o].index(after) + 1
        o[i:i] = ws
    return " ".join(o)


ORDER = _moved(ORDER, """
ST2.3 AT.0s
A21.0 AQ.0v PS4.0t AQ.1v PS5.0t
SS1.0 Z1.0a Z1.1a
KK1.0 AO1.0v
Z1.1 Z1.2a
IC1.1 LU2.0v
A21.0 LB.0v LB.1v
Z1.0 GI.0a
XT1.0 GT.0v GT.1v GT.2v GT.3v
XO1.1 LA.0v LA.1v
S1.1 G2.1a G2.0v OG2.0v SG2.0v SG2.1v SG2.2v SG2.3v
W1.1 KM1.0v
W2.1 KM2.0v
PA2.0 PS0.2t PS1.1t PS2.1t PS3.1t Z2.4v Z2.5a Z2.6a Z2.7a PR2.0s oCH2.0s HT2.0v HT2.1v HT2.2v HT2.4v HT2.3v QO2.1v QO2.0v
""")


ORDER = """
PI.0g RAW.2s PV.0v PJ.2v PJ.1v ZERO.0g RAW.1a PJ.0v SL.0v RAW.0s SL.2v SL.3v RAW.3a SL.1v PJ.5v UC.0s KB.3a E0.1a PJ.6v PJ.3v
RL.1v RL.0v KA.2a BC.1a BAR.0a PJ.4v DUPF.0g E0.0s FOUR.0g J4.0g SEG4.0v T2.1v T2.0v PF32.0v SL.4v FL.1a BC.0a SUF.1a SCL.1v
D11.0a AT.0s UT.2a UT.3a SCL.0v KCOL.1v TI.0v MSG1.1v J32.0g MSG1.0v BAR.1a PKC.0a J16.0g UT.0a FL.0a KCOL.0a TR.0g KCOL.2a
XI.0g oMSG1.0g _LM1.0x SEG16.0v TB.2a LS2.0v UT.1a TK.0v IDT.0g PKC.1a KA.0a BC.2a BC.3a BAR.2a TB.1a TB.4a TB.3a LS2.1v ZB.0a
GD.0a KV.0v QO0.0v SK.0v LS1.0v UQ.0v TB.5a KA.3a AQ.0v TB.0a KA.14a PK.0v KB.0v MASK.0v KA.15a KB.1a LU1.3v ST2.1v ST2.2v
PS0.0t PS4.0t ST2.0v AQ.1v TB.6a ST2.4s W2.0g ST2.5s KA.1a KA.13a S0.0a Z1.0a W1.0g KV.1v LU1.0v LU1.2v LU1.1v KA.8a KA.4a
KA.6a LCN1.0v KA.11v KA.7v ST2.3s G1.0v KA.9a KA.12a SEGT.0v AT.1s oST2.0g _LC2.0x KA.5a KW.0v KA.10a OL1.3a XM.0v SG1.0v
ZB.2a TU.0v KR.0v SEGT.1v PS5.0t U1.0v SEG8.0a AO1.0v KE1.0v KD1.0v BAR.3v Z1.1a oU1.0g _U1.0x KB.6a OL1.2a KB.4a E1.0s
SEG8.1a ZB.1a AQ.2v D11.2v FL.2v KK1.0v SUF.0v D11.1a AQ.3v KW.1v VA1.0v ZB.4v M161.0v PS6.0t NI1.0v OL1.0a MM1.0v BT1.0v
KB.2a RT1.0v SUF.2a OG1.0a PS7.0t EQ1.0v AA1.0v XB.0a OL1.1a VR1.0a Z1.2a SFX1.0v KB.12a KEY1.0v OF1.0v LU2.3s LU2.0v KM1.0v
KB.13a KB.11a KB.15a LU2.2s W1.1v ZB.5v ZB.7v ZB.6v IC1.0a WD1.0v IC1.1v KB.14a KB.5a KB.7a KB.8a KB.9a KB.10a D12.0a ZB.3a
Z1.3a WD1.1a TW1.2v TW1.0v NW1.0a TW1.1v RC1.0v NP1.0v TA1.0v PF1.1v LU2.1s PF1.0v SFC1.0v NQ1.0v PO1.1v PO1.0v SR1.0v KR1.0v
SQ1.0v KP1.0v SV1.0v POW.0v A21.0v oSQ1.0g _QW0.0x LCN2.0v ZB.8v ZB.10v TA1.2v TA1.1v TA1.3v LB.1v SS1.0a MULT.0a LB.0v ZB.9v
XT1.0v oSS1.0g _QP0.0x PS0.1t OL2.0a OL2.3a OG2.0a OL2.2a AO2.0v PS1.0t PS2.0t PS3.0t KI.0v XS1.0v XT1.1v IC2.0a GI.0a GT.1v
CH1.0v GT.0v GT.3v GT.2v KE2.0v XO1.0v XO1.1v PS6.1t LA.0v OL2.1a Z1.4a Z1.6a LA.1v Z1.5v HT1.0v Z1.7a HT1.2v HT1.3v HT1.1v
HT1.4v QO1.0v S0.1a QO1.1v PS4.1t KD2.0v VR2.0a PB1.0a TA2.0v S1.0v PS5.1t PS7.1t PS6.2t PS4.2t S1.1v G2.0v SG2.1v SG2.0v
PS5.2t G2.1a SG2.3v SG2.2v oSG2.0g FL.3v U2.0v _U2.0x D12.2v E2.0s KK2.0v oCH1.0s WT.0s Z2.0a D12.1a Z2.1a Z2.2a VA2.0v ZB.11v
M162.0v NI2.0v MM2.0v BT2.0v RT2.0v EQ2.0v AA2.0v SFX2.0v KEY2.0v OF2.0v KM2.0v W2.1v ZB.12v ZB.14v ZB.13v WD2.0v IC2.1v Z2.3a
WD2.1a TW2.0v TW2.2v NW2.0a TW2.1v RC2.0v NP2.0v PF2.1v PF2.0v SFC2.0v NQ2.0v PO2.0v PO2.1v SR2.0v KR2.0v SQ2.0v KP2.0v SV2.0v
A22.0v oSQ2.0g _QW1.0x ZB.16v ZB.15v ZB.17v TA2.3v TA2.1v TA2.2v XS2.0v WQ.0v XT2.0v KQ2.0v XT2.1v PP2.0v CH2.0v SS2.0a
oSS2.0g _QP1.0x PS0.2t PS3.1t PS2.1t PS1.1t XO2.0v XO2.1v PA2.0v Z2.7a Z2.4v Z2.6a PR2.0s oCH2.0s HT2.0v Z2.5a HT2.4v HT2.1v
HT2.2v HT2.3v QO2.1v PS7.2t oQO2.1s QO2.0v YB.1a PS5.3t oQS2.1a PS6.3t YB.0a S2.1v oQO2.0s PS4.3t oQS2.2a oQS2.0s S2.0v
oQS2.3a oYB.1s oYB.0s oS2.0a
"""


ORDER = """
PI.0g RAW.2s PV.0v PJ.2v PJ.1v ZERO.0g RAW.1a PJ.0v SL.0v RAW.0s SL.2v SL.3v RAW.3a SL.1v PJ.5v UC.0s KB.3a E0.1a PJ.6v PJ.3v
RL.1v RL.0v KA.2a BC.1a BAR.0a PJ.4v DUPF.0g E0.0s FOUR.0g J4.0g SEG4.0v T2.1v T2.0v PF32.0v SL.4v FL.1a BC.0a SUF.1a SCL.1v
D11.0a AT.0s UT.2a UT.3a SCL.0v KCOL.1v TI.0v MSG1.1v J32.0g MSG1.0v LS2.0v TK.0v LS2.1v BAR.1a PKC.0a J16.0g UT.0a FL.0a
KCOL.0a TR.0g KCOL.2a XI.0g oMSG1.0g _LM1.0x SEG16.0v TB.2a UT.1a IDT.0g PKC.1a KA.0a BC.2a BC.3a BAR.2a TB.1a TB.4a TB.3a
ZB.0a GD.0a KV.0v SK.0v LS1.0v QO0.0v PK.0v UQ.0v ST2.1v ST2.2v ST2.0v MASK.0v TB.5a KB.0a KA.3a AQ.0v TB.0a KA.14a KA.15a
KB.1a LU1.3v PS0.0t PS4.0t TB.6a ST2.4s W2.0g ST2.5s KA.1a KA.13a S0.0a W1.0g KV.1v LU1.1v LU1.2v LU1.0v KA.8a KA.4a KA.6a
LCN1.0v KA.11v KA.7v ST2.3s G1.0v KA.12a SEGT.0v AT.1s oST2.0g _LC2.0x KA.5a KA.9v KA.10a OL1.3a XM.0v SG1.0v KW.0v BAR.3a
ZB.2a Z1.0a TU.0v KR.0v U1.0v SEG8.0a SEGT.1a AQ.1v KE1.0v KD1.0v AO1.0v oU1.0g _U1.0x KB.6a OL1.2a KB.4a E1.0s SEG8.1a D11.2a
SUF.0v ZB.1v KK1.0v PS5.0t FL.2v AQ.2v D11.1a VA1.0v AQ.3v ZB.4v M161.0v PS6.0t PS7.0t NI1.0v SUF.2a OL1.0a MM1.0v BT1.0v KB.2a RT1.0v
OG1.0a EQ1.0v AA1.0v XB.0a OL1.1a IC1.0a Z1.1a VR1.0a Z1.2a SFX1.0v KW.1v KEY1.0v OF1.0v KB.12v LU2.3s LU2.0v KM1.0v KB.13a
KB.11a KB.15a LU2.2s W1.1v ZB.5v ZB.7v ZB.6v WD1.0v IC1.1v KB.14a KB.5a KB.7a KB.8a KB.9a KB.10a D12.0a ZB.3a WD1.1a TW1.2v
TW1.0v NW1.0a TW1.1v RC1.0v NP1.0v TA1.0v PF1.1v LU2.1s PF1.0v SFC1.0v NQ1.0v PO1.1v PO1.0v SR1.0v KR1.0v SQ1.0v
SV1.0v KP1.0v POW.0v A21.0v oSQ1.0g _QW0.0x LCN2.0v ZB.8v ZB.10v TA1.2v TA1.1v TA1.3v LB.1v SS1.0a Z1.3a MULT.0a LB.0v ZB.9v
XT1.0v oSS1.0g _QP0.0x PS0.1t OL2.0a OL2.3a OG2.0a OL2.2a AO2.0v PS1.0t PS2.0t PS3.0t KI.0v XS1.0v XT1.1v IC2.0a GI.0a GT.1v
CH1.0v GT.0v GT.3v GT.2v KE2.0v XO1.0v XO1.1v PS6.1t LA.0v OL2.1a Z1.4a Z1.6a LA.1v Z1.5v HT1.0v
""" + ORDER[ORDER.index("HT1.0v") + 6:]


ORDER = """
PI.0g RA.0s RA.1a PJ.3v PJ.2v RA.2s RA.3a ZERO.0g RAW.2s PJ.0v RAW.1a PJ.1v PJ.4v RAW.0s J4.0g RAW.3a SL.0v SL.2v SL.1v J32.0g
PJ.5v BAR.0a FL.0a SUF.1a BAR.2a KB.1a UC.0s E0.1a E0.0s SL.3v SL.4v AT.0s PJ.6v RB.0v RB.1v RL.0v RL.1v SEG4.0v RC.0v PF32.0v
T2.1v T2.0v FOUR.0g DUPF.0g TR.0g RD.0v RD.1v TI.0v MSG1.0v MSG1.1v SCL.0v BC.1a UT.3a XI.0g oMSG1.0g _LM1.0x D11.0a UT.2a
TK.0v SCL.1v PKC.0a LS1.0v BAR.1a TB.4a KCOL.0a POW.0v SK.0v LS1.1v LS2.1v KCOL.2a PKC.1a FL.1a UT.1a KCOL.1a LS2.0v UT.0a
PK.0v TB.1a KB.0a TB.0a TB.3a BC.3a UQ.0v SEGT.0v MSG2.0v QO0.0v LCN1.0v ZB.0a GD.0a BC.0a TB.5a KW.0v IDT.0g oMSG2.0g _LM2.0x
AQ.0v TB.6a TB.2a PS0.0t BC.2a KB.2a KB.3a KB.6a TU.0v LU2.0v LA1.3v KB.4a KB.5a XM.0v AQ.1v SUF.0v LCN2.0v LA1.2v MULT.0a
S0.0a PS4.0t LA1.0v LA1.1v Z1.0a ST2.1s G1.0v KW.1v KB.10v W1.0g ST2.2s KB.12v KB.11v ST2.0s G1.1a AT.1s KB.7a KB.8a
KB.9a KB.15a SG1.1v SG1.3v KB.13a PS5.0t SG1.0v SG1.2v oSG1.0g _U1.0x KB.14a GI1.0a oST2.0g _LC2.0x W2.0g SEGT.1v KI1.0v ZB.2v
D11.2v KE1.0v KD1.0v ZB.1a GT1.0v BAR.3v GT1.2v FL.2v KK1.0v D11.1a U1.0a GT1.3v GT1.1v VA1.0v IC1.0v E1.0s OL1.2a LU1.0v
ZB.4v M161.0v NI1.0v MM1.0v BT1.0v RT1.0v EQ1.0v OL1.0a AA1.0v SUF.2a IC2.0a OL1.3a SEG8.0a Z1.1a SFX1.0v KEY1.0v OF1.0v
AO1.0v OL2.1a SEG8.1a XB.0a KM1.0v LU2.3s LU2.2s OL1.1a D12.0a ZB.3a OL2.2a OG2.0a OL2.0a OG1.0a OL2.3a VR1.0a W1.1v ZB.7v
ZB.5v ZB.6v WD1.0v WD1.1a IC1.1v TW1.2v NW1.0a TW1.1v TW1.0v NP1.0v RC1.0v LU2.1s PF1.1v PF1.0v SFC1.0v NQ1.0v PO1.0v PO1.1v
SR1.0v KR1.0v SQ1.0v A21.0v oSQ1.0g _QW0.0x LB.0v LB.1v AQ.2v PS6.0t KP1.0v SS1.0a TA1.2v TA1.3v SV1.0v TA1.0v oSS1.0g _QP0.0x
TA1.1v AQ.3v ZB.10v PS7.0t GI2.0a GT2.2v GT2.3v ZB.8v KI2.0v GT2.1v XT1.0v GT2.0v Z1.2a XT1.1v ZB.9v PS0.1t PS2.0t PS1.0t
KE2.0v Z1.3a Z1.4a AO2.0v LA2.0v XO1.0v XO1.1v LA2.1v KD2.0v PS3.0t XS1.0v Z1.6v PS6.1t HT1.0v Z1.5a Z1.7a HT1.2v HT1.3v
HT1.1v HT1.4v QO1.0v S0.1a QO1.1v PS4.1t VR2.0a PB1.0a TA2.0v CH1.0v S1.0v PS5.1t PS7.1t PS6.2t PS4.2t S1.1v G2.0v SG2.1v
SG2.0v PS5.2t G2.1a SG2.3v SG2.2v oSG2.0g FL.3v U2.0v _U2.0x D12.2v E2.0s KK2.0v oCH1.0s WT.0s Z2.0a D12.1a Z2.1a Z2.2a VA2.0v
ZB.11v M162.0v NI2.0v MM2.0v BT2.0v RT2.0v EQ2.0v AA2.0v SFX2.0v KEY2.0v OF2.0v KM2.0v W2.1v ZB.12v ZB.14v ZB.13v WD2.0v
IC2.1v Z2.3a WD2.1a TW2.0v TW2.2v NW2.0a TW2.1v RC2.0v NP2.0v PF2.1v PF2.0v SFC2.0v NQ2.0v PO2.0v PO2.1v SR2.0v KR2.0v SQ2.0v
KP2.0v SV2.0v A22.0v oSQ2.0g _QW1.0x ZB.16v ZB.15v ZB.17v TA2.3v TA2.1v TA2.2v XS2.0v WQ.0v XT2.0v KQ2.0v XT2.1v PP2.0v CH2.0v
SS2.0a oSS2.0g _QP1.0x PS0.2t PS3.1t PS2.1t PS1.1t XO2.0v XO2.1v PA2.0v Z2.7a Z2.4v Z2.6a PR2.0s oCH2.0s HT2.0v Z2.5a HT2.4v
HT2.1v HT2.2v HT2.3v QO2.1v PS7.2t oQO2.1s QO2.0v YB.1a PS5.3t oQS2.1a PS6.3t YB.0a S2.1v oQO2.0s PS4.3t oQS2.2a oQS2.0s S2.0v
oQS2.3a oYB.1s oYB.0s oS2.0a
"""


ORDER = """
PI.0g RA.0s RA.1a RA.2s RA.3a J4.0g ZERO.0g RAW.2s RAW.1a RAW.0s RAW.3a UC.0s E0.1a E0.0s AT.0s PJ.3v PJ.1v PJ.0v PJ.2v SL.0v
SL.1v SL.5v SL.6v SL.7v SL.4v SEG4.0v PJ.4v FOUR.0g DUPF.0g J32.0g TR.0g BAR.0a FL.0a SUF.1a KB.1a RB.0v RB.1v TI.0v PJ.5v
PJ.6v RC.0v TK.0v TK.1v PF32.0v D11.0a PKC.0a BAR.2a RD.0v RD.1v SK.0v SK.1v MSG1.0v MSG1.1v oMSG1.0g XI.0g _LM1.0x BC.1a
BAR.1a FL.1a PKC.1a UT.3a UT.2a SL.2v PK.0v SL.3v POW.0v SEGT.0v RL.0v MSG2.0v RL.1v oMSG2.0g _LM2.0x IDT.0g TB.4a
UT.1a UT.0a KCOL.0a KCOL.2a KCOL.1a QO0.0v T2.0v T2.1v UQ.0v KW.0v SCL.0v SCL.1v LS1.0v LS2.1v TB.1a KB.0a TB.0a TB.3a BC.3a LS1.1v
LS2.0v ZB.0a GD.0a BC.0a TB.5a TB.6a TB.2a PS0.0t BC.2a KB.2a KB.3a KB.6a TU.0v LA1.3v AQ.0v KB.4a KB.5a
LA1.2v S0.0a MULT.0a PS4.0t LA1.0v LA1.1v KW.1v LCN1.0v LCN2.0v ST2.1s G1.0v KB.10v W1.0g ST2.2s KB.12v KB.11v
ST2.0s G1.1a AT.1s KB.7a KB.8a KB.9a KB.15a SG1.1v SG1.3v KB.13a SG1.0v SG1.2v oSG1.0g _U1.0x KB.14a GI1.0a oST2.0g
_LC2.0x W2.0g SEGT.1v SUF.0v KI1.0v ZB.2v D11.2v KE1.0v KD1.0v ZB.1a GT1.0v BAR.3v GT1.2v FL.2v KK1.0v D11.1a U1.0a Z1.0a GT1.3v GT1.1v
VA1.0v XM.0v E1.0s OL1.2a LU1.0v ZB.4v M161.0v IC1.0v NI1.0v MM1.0v BT1.0v RT1.0v EQ1.0v OL1.0a AA1.0v SUF.2a IC2.0a OL1.3a SEG8.0a
SFX1.0v LU2.0v KEY1.0v OF1.0v AO1.0v OL2.1a SEG8.1a XB.0a KM1.0v LU2.3s LU2.2s OL1.1a VR1.0a D12.0a ZB.3a OL2.2a OG2.0a OL2.0a OG1.0a
OL2.3a W1.1v ZB.7v ZB.5v ZB.6v WD1.0v WD1.1a IC1.1v TW1.2v NW1.0a TW1.1v TW1.0v NP1.0v RC1.0v LU2.1s PF1.1v PF1.0v
SFC1.0v NQ1.0v PO1.0v PO1.1v SR1.0v KR1.0v SQ1.0v A21.0v oSQ1.0g _QW0.0x AQ.1v PS5.0t LB.0v LB.1v AQ.2v PS6.0t SS1.0a TA1.2v TA1.3v
TA1.0v oSS1.0g _QP0.0x TA1.1v AQ.3v KP1.0v SV1.0v PS7.0t GI2.0a Z1.1a XT1.0v XT1.1v ZB.10v ZB.8v ZB.9v GT2.2v GT2.3v XO1.0v XO1.1v GT2.1v GT2.0v Z1.2a
PS0.1t PS2.0t PS1.0t Z1.3a Z1.4a KI2.0v AO2.0v LA2.0v LA2.1v XS1.0v KE2.0v KD2.0v PS3.0t Z1.6v PS6.1t HT1.0v
""" + ORDER[ORDER.index("HT1.0v") + 6:]


ORDER = """
PI.0g RA.0s RA.1a RAW.0s RAW.1a RAW.2s RAW.3a J4.0g ZERO.0g UC.0a E0.0s E0.1a AT.0s PJ.3v PJ.1v PJ.0v PJ.2v SL.0v SL.1v
SL.2v SL.3v SL.5v SL.4v SL.7v SL.6v SEG4.0v RB.0v RB.1v RB.2v RB.3v TI.0v PJ.4v PJ.5v RC.0v TK.0v TK.1v PJ.6v FOUR.0g DUPF.0g
J32.0g TR.0g PKC.0a RD.0v RD.1v SK.0v SK.1v MSG1.0v MSG1.1v PF32.0v BAR.0a FL.0a SUF.1a PKC.1a PK.0v KB.1a D11.0a BAR.2a
oMSG1.0g XI.0g _LM1.0x BC.1a BAR.1a FL.1a UT.3a UT.2a POW.0v SEGT.0v RL.0v MSG2.0v RL.1v oMSG2.0g _LM2.0x IDT.0g UT.1a UT.0a
KCOL.0a TB.4a KCOL.1a KCOL.2a QO0.0v T2.0v T2.1v UQ.0v SCL.0v SCL.1v KW.0v TB.0v LS1.0v LS2.1v TB.1a KB.0a TB.3a BC.3a LS1.1v
LS2.0v ZB.0a GD.0a BC.0a TB.5a TB.6a TB.2a PS0.0t BC.2a KB.2a KB.3a KB.6a TU.0v LA1.3v AQ.0v KB.4a KB.5a LA1.2v S0.0a MULT.0a
PS4.0t LA1.0v LA1.1v KW.1v LCN1.0v LCN2.0v ST2.1s G1.0v KB.10v W1.0g ST2.2s KB.12v KB.11v ST2.0s G1.1a AT.1s KB.7a KB.8a KB.9a
KB.15a SG1.1v SG1.3v KB.13a SG1.0v SG1.2v oSG1.0g _U1.0x KB.14a GI1.0a oST2.0g _LC2.0x W2.0g SEGT.1v SUF.0v KI1.0v ZB.2v
D11.2v KE1.0v KD1.0v ZB.1a GT1.0v BAR.3v GT1.2v FL.2v KK1.0v D11.1a U1.0a Z1.0a GT1.3v GT1.1v VA1.0v XM.0v E1.0s OL1.2a LU1.0v
""" + ORDER[ORDER.index("ZB.4v"):ORDER.index("PS0.2t")] + """
PS0.2t PS3.1t PS2.1t PS1.1t XO2.0v XO2.1v PA2.0v PR2.0s oCH2.0s Z2.4v HT2.0v Z2.7a Z2.6a HT2.4v Z2.5a HT2.2v HT2.1v HT2.3v QO2.1v
PS7.2t QO2.0v YB.1v oQS2.0a PS5.3t PS6.3t S2.1v oQS2.2a PS4.3t oQO2.1s oQS2.1s S2.0v YB.0a oQO2.0s oQS2.3s oYB.1s oYB.0a
oS2.0s
"""


ORDER = _moved(ORDER, """
U1.0 SUF.1a
KR1.0 SQ1.0v SQ1.1v SS1.0a SS1.1a oSQ1.0g _QW0.0x oSQ1.1g _QW0.1x oSS1.0g _QP0.0x
KR2.0 SQ2.0v SQ2.1v SS2.0a SS2.1a oSQ2.0g _QW1.0x oSQ2.1g _QW1.1x oSS2.0g _QP1.0x
""")


def rank_program(g, core, T, topo):
    me = T.rank_of(core)
    if me is None:
        return
    others = [(me + 1 + i) % 4 for i in range(3)]
    slot_at = [(me - d) % 4 - 1 for d in others]
    qs = {"v": g.vector, "a": g.scalar, "t": g.tensor, "g": g, "s": g.sync}
    hist, know, cnt, total = {}, {q: {} for q in qs}, {}, {}
    nodes, past = [], {}

    def V(name, c0=0, c1=None, st=1, p0=0, p1=128):
        return (name, p0, p1, c0, PLACE[name][2] if c1 is None else c1, st)

    def tab(name, c0=0, c1=None, buf="TU"):
        a, z = TAB[name]
        return V(buf, a + c0, z if c1 is None else a + c1)

    def blk(k, name, c0=0, c1=None, st=1):
        return V(name, c0, c1, st, 32 * k, 32 * k + 32)

    def ap(v):
        name, o, _ = PLACE[v[0]]
        return T[name][v[1]:v[2], o + v[3]:o + v[4]] if v[5] == 1 else T[name][v[1]:v[2], o + v[3]:o + v[4]:v[5]]

    def width(v):
        return (v[4] - v[3] + v[5] - 1) // v[5]

    def clash(a, b):
        if a[2] <= b[1] or b[2] <= a[1] or a[4] <= b[3] or b[4] <= a[3]:
            return False
        return not (a[5] == b[5] and a[5] > 1 and (a[3] - b[3]) % a[5])

    def bank(v):
        return (v[0], 0, 128, v[3] // 512 * 512, v[3] // 512 * 512 + 512, 1) if v[0] == "PS" else v

    def regions(reads, writes):
        return [(bank(v), False) for v in reads] + [(bank(v), True) for v in writes]

    def push(opts, reads, writes, after=()):
        i, deps = len(nodes), set(after)
        for r, w in regions(reads, writes):
            deps |= {j for (o, ow, j) in past.get(r[0], []) if (w or ow) and clash(r, o)}
        for r, w in regions(reads, writes):
            past.setdefault(r[0], []).append((r, w, i))
        nodes.append({"opts": opts, "rd": reads, "wr": writes, "deps": deps - {i}, "gate": list(after)})
        return i

    def wait(q, evs):
        need = {}
        for sem, val, clock in evs:
            if know[q].get(sem, 0) < val and need.get(sem, (0, 0))[0] < val:
                need[sem] = (val, clock)
        for sem in sorted(need):
            val, clock = need[sem]
            if know[q].get(sem, 0) >= val or any(o != sem and need[o][1].get(sem, 0) >= val for o in need):
                continue
            qs[q].wait_ge(T.sem[sem], val)
        for sem in need:
            for k, n in list(need[sem][1].items()) + [(sem, need[sem][0])]:
                know[q][k] = max(know[q].get(k, 0), n)

    def issue(node, q):
        node["done"] = True
        if q == "x":
            return
        assert all("done" in nodes[j] for j in node["deps"])
        evs = [nodes[j]["ev"] for j in node["gate"]]
        for r, w in regions(node["rd"], node["wr"]):
            evs += [ev for (o, ow, ev) in hist.get(r[0], []) if (w or ow) and clash(r, o)]
        wait(q, evs)
        kind, call = node["opts"][q]
        if kind == "op":
            sem, val = "q" + q, cnt.get(q, 0) + 1
            cnt[q] = val
            call().then_inc(T.sem[sem], 1)
        elif kind == "dma" and not node["wr"]:
            sem, val = "out", total.get("out", 0) + 16
            call().then_inc(T.sem[sem], 16)
        elif kind == "dma":
            sem, val = "d%d" % cnt.get("dma", 0), 16
            cnt["dma"] = cnt.get("dma", 0) + 1
            call().then_inc(T.sem[sem], 16)
        else:
            sem, val = call()
        clock = dict(know[q])
        clock[sem] = val
        total[sem] = max(total.get(sem, 0), val)
        node["ev"] = (sem, val, clock)
        for r, w in regions(node["rd"], node["wr"]):
            hist.setdefault(r[0], []).append((r, w, node["ev"]))

    def lay():
        seen, named = {}, {}
        for nd in nodes:
            if nd["wr"]:
                v = nd["wr"][0]
                b = ("_" if "x" in nd["opts"] else "") + v[0] + (str(v[3] // 512) if v[0] == "PS" else "")
            else:
                b = "o" + nd["rd"][0][0]
            named["%s.%d" % (b, seen.get(b, 0))] = nd
            seen[b] = seen.get(b, 0) + 1
        for w in ORDER.split():
            issue(named[w[:-1]], w[-1])
        assert all("done" in nd for nd in nodes)

    def op(q, call, reads, writes):
        return push({q: ("op", call)}, reads, writes)

    def sv(s):
        return ap(s) if isinstance(s, tuple) else s

    def cols_of(*ss):
        return [s for s in ss if isinstance(s, tuple)]

    def tc(o, a):
        op("v", lambda: g.vector.tensor_copy(ap(o), ap(a)), [a], [o])

    def tt(o, a, b, f):
        op("v", lambda: g.vector.tensor_tensor(ap(o), ap(a), ap(b), f), [a, b], [o])

    def tti(o, w, off, b, f):
        op("v", lambda: g.vector.tensor_tensor(ap(o), ap(w).indirect(ap(off)), ap(b), f), [w, off, b], [o])

    def ts(o, a, s1, f1, s2=None, f2=None):
        if f2 is None:
            op("v", lambda: g.vector.tensor_scalar(ap(o), ap(a), sv(s1), None, f1), [a] + cols_of(s1), [o])
        else:
            op("v", lambda: g.vector.tensor_scalar(ap(o), ap(a), sv(s1), sv(s2), f1, f2), [a] + cols_of(s1, s2), [o])

    def lin(o, a, scale=1.0, bias=0.0):
        def on_v():
            if scale == 1.0 and bias == 0.0:
                return g.vector.tensor_copy(ap(o), ap(a))
            if bias == 0.0:
                return g.vector.tensor_scalar(ap(o), ap(a), sv(scale), None, A.mult)
            if scale == 1.0:
                return g.vector.tensor_scalar(ap(o), ap(a), sv(bias), None, A.add)
            return g.vector.tensor_scalar(ap(o), ap(a), sv(scale), sv(bias), A.mult, A.add)

        def on_a():
            if bias == 0.0:
                return g.scalar.activation(ap(o), ap(a), AF.Copy, scale=sv(scale))
            return g.scalar.activation(ap(o), ap(a), AF.Identity, scale=sv(scale), bias=sv(bias))
        push({"v": ("op", on_v), "a": ("op", on_a)}, [a] + cols_of(scale, bias), [o])

    def scan(o, a, b, f0=A.add, f1=A.add, first=0.0):
        op("v", lambda: g.vector.tensor_tensor_scan(ap(o), ap(a), ap(b), first, f0, f1), [a, b], [o])

    def tr(o, a):
        op("v", lambda: g.vector.transpose(ap(o), ap(a)), [a], [o])

    def ms(o, c):
        lin(o, ("ZERO",) + o[1:3] + (0, width(o), 1), 1.0, c)

    def fill(o, base, step=0, rise=0, pattern=None):
        op("g", lambda: g.iota(ap(o), pattern or [[step, width(o)]], base, rise, allow_small_or_imprecise_dtypes=True), [], [o])

    def gat(o, w, off):
        op("v", lambda: g.vector.tensor_copy(ap(o), ap(w).indirect(ap(off))), [w, off], [o])

    def gata(o, w, off, func=AF.Copy, **k):
        op("a", lambda: g.scalar.activation(ap(o), ap(w).indirect(ap(off)), func, **k), [w, off], [o])

    def gatx(o, w, off):
        push({"v": ("op", lambda: g.vector.tensor_copy(ap(o), ap(w).indirect(ap(off)))),
              "a": ("op", lambda: g.scalar.activation(ap(o), ap(w).indirect(ap(off)), AF.Copy))}, [w, off], [o])

    def pick(qo, so, qw, sw, off):
        op("v", lambda: g.vector.tensor_copy(ap(qo).bitcast(dt.uint32), ap(qw).bitcast(dt.uint32).indirect(ap(off))), [qw, off], [qo])
        gata(so, sw, off)

    def qz(q, s, a):
        return op("v", lambda: g.vector.quantize_mx(ap(q), ap(s), ap(a)), [a], [q, s])

    def mm(b, n, wq, ws, xq, xs):
        o = V("PS", 512 * b, 512 * b + n)
        op("t", lambda: g.tensor.matmul_mx(ap(o), ap(wq), ap(ws), ap(xq), ap(xs), True, True), [wq, ws, xq, xs], [o])
        return o

    def dma(q, out, in_, reads, writes, after=()):
        return push({k: ("dma", lambda k=k: qs[k].dma_start(out, in_)) for k in q}, reads, writes, after)

    def load(q, v, src, after=()):
        return dma(q, ap(v), src, [], [v], after)

    def mask_of(engines):
        return sum(1 << e for e in engines)

    def dst(d):
        rid, pid, _ = topo.addr(T.cores[d])
        return DstId(rid=rid, pnc=pid)

    def remote(transfers, src, lsem, count, sem, arrivals, landing):
        def call():
            g.remote_dma_fused(transfers, local_sem=T.sem[lsem])
            return lsem, count
        i = push({"g": ("remote", call)}, [src], [])
        push({"x": None}, [], [landing], [i])
        total[sem] = arrivals
        hist.setdefault(landing[0], []).append((landing, True, (sem, arrivals, {sem: arrivals})))
        return i

    def spread(src, land, sem, lsem, landing, first=0, step=1):
        e = topo.engines(core, T.cores[others[0]])[first:16:step]
        return remote([RemoteDMATransfer(
            dst_ids=[dst(d) for d in others], dma_engine_mask=mask_of(e), remote_sem=T.sem[sem], srcs=[ap(src)],
            dsts=[ap(land(s)) for s in slot_at])], src, lsem, len(e), sem, 3 * len(e), landing)

    def deal(s, turn):
        order = sorted([d for d in range(4) if d != s], key=lambda d: (topo.die(T.cores[d]) != topo.die(T.cores[s]), (d - s) % 4 == 2))
        e = topo.engines(T.cores[s], T.cores[order[0]])
        a, z = (e[8:16], e[0:8]) if turn else (e[0:8], e[8:16])
        return {order[0]: a[1::2], order[1]: a[0::2], order[2]: z}

    def each(src, w, land, sem, lsem, turn=0):
        trs = []
        for i, d in enumerate(others):
            a, z = V(src, w * i, w * i + w), V(land, w * slot_at[i], w * slot_at[i] + w)
            code = SCRATCH[src][2] == C
            trs.append(RemoteDMATransfer(
                dst_ids=[dst(d)], dma_engine_mask=mask_of(deal(me, turn)[d]), remote_sem=T.sem[sem],
                srcs=[ap(a).bitcast(dt.uint8) if code else ap(a)], dsts=[ap(z).bitcast(dt.uint8) if code else ap(z)]))
        return remote(trs, V(src), lsem, 16, sem, sum(len(deal(s, turn)[me]) for s in others), V(land))

    def turn_of(s):
        return sorted([d for d in range(4) if d != s], key=lambda d: (topo.die(T.cores[d]) != topo.die(T.cores[s]), (d - s) % 4 == 2))
    turn = turn_of(me)

    def columns(src, land, engines, sem, arrivals, lsem, count):
        trs, code = [], SCRATCH[src][2] == C
        for i in engines:
            at = slot_at[others.index(turn[i])]
            a, z = V(src, 64 * i, 64 * i + 64), V(land, 64 * at, 64 * at + 64)
            trs.append(RemoteDMATransfer(
                dst_ids=[dst(turn[i])], dma_engine_mask=mask_of(engines[i]), remote_sem=T.sem[sem],
                srcs=[ap(a).bitcast(dt.uint8) if code else ap(a)], dsts=[ap(z).bitcast(dt.uint8) if code else ap(z)]))
        return remote(trs, V(src, 64 * min(engines), 64 * max(engines) + 64), lsem, count, sem, arrivals, V(land))

    def zb(t, o, n):
        o = 136 * (t - 1) + o
        return V("ZB", o, o + n)

    def sub(v, a, b, k=None, st=1):
        return (v[0], v[1] if k is None else 32 * k, v[2] if k is None else 32 * k + 32, v[3] + a, v[3] + b, st)

    def bufs(t):
        return lambda name, *a: V(name + str(t), *a)

    for i in range(2):
        load("sa", blk(i, "RA"), T.p1[:])
    for i in range(4):
        load("sa", V("RAW", p0=16 * i, p1=16 * i + 16), (T.p1, T.p2)[i % 2][:])
    load("sa", V("E0", 0, 512), T.e0[:, 0:512])
    load("sa", V("UC"), T.u[:, 0:4])
    load("sa", V("E0", 512, 1024), T.e0[:, 512:1024])
    op("g", lambda: g.iota(ap(V("PI")), [[0, 1]], 0, 1), [], [V("PI")])
    fill(V("J4"), 0, pattern=[[0, 16], [1, 4]])
    fill(V("ZERO"), 0)
    for j, m in enumerate((15, 3, 1, 96, 31, 7)):
        ts(V("PJ", j, j + 1), V("PI"), m, A.bitwise_and)
    ts(V("PJ", 6, 7), V("PI"), 2, A.logical_shift_right, 3, A.bitwise_and)
    tc(V("PF32"), V("PJ"))
    p15, kcol, odd, p96, p31, p7, p4 = [V("PF32", j, j + 1) for j in range(7)]
    ts(V("SL", 0, 1), V("PJ", 3, 4), 8.0, A.mult, -0.5, A.add)
    ts(V("SL", 1, 2), V("PJ", 3, 4), 8.0, A.mult, P - 0.5, A.add)
    ts(V("SL", 4, 5), V("PJ", 3, 4), 8.0, A.mult, 2 * P - 0.5, A.add)
    ts(V("SL", 5, 6), V("PJ", 3, 4), 8.0, A.mult, 3 * P - 0.5, A.add)
    ts(V("SL", 2, 3), V("PJ", 3, 4), 24.0, A.mult, 3 * (P - 0.5), A.add)
    ts(V("SL", 3, 4), V("PJ", 1, 2), -1.0, A.mult, 3.0, A.add)
    ts(V("SL", 6, 7), V("PJ", 3, 4), 8.0, A.mult)
    ts(V("SL", 7, 8), V("PJ", 3, 4), 8.0, A.mult, 2.0 * P, A.add)
    ts(V("SEG4"), V("J4"), 1.0, A.min)
    lin(V("PKC"), V("SEG4"), -3.0, 4.0)
    lin(V("PKC", 0, 64, 32), V("ZERO", 0, 2))
    fill(V("DUPF"), 0, pattern=[[64, 4], [0, 2]])
    fill(V("FOUR"), 4)
    fill(V("J32"), 0, 1)
    fill(V("TR"), 1028, 4, 32)
    for k in range(4):
        ms(blk(k, "BC", 0, 1), float(255 + 64 * others.index(k)) if k != me else 0.0)
    ms(V("BAR"), 0.0)
    ms(V("BAR", 4, 33, 4), -BIG - 4.0)
    ms(V("BAR", 1, 32, 4), 1.5)
    ms(V("BAR", 3, 32, 4), BIG)
    lin(V("GD", 0, 1), p96, 8.0, float(-P * me))

    def more_fills():
        fill(V("W1", 0, 256), 0)
        fill(V("XI"), 0, pattern=[[0, 2], [1, 2], [0, 8]])
        ts(V("XM"), V("XI"), odd, A.is_equal)
        lin(V("XB"), V("XM"), -1000.0, 1000.0)
        ms(V("SEG8"), 1.0)
        ms(V("SEG8", 0, 128, 8), 0.0)
        fill(V("W2", 0, 256), 0)

    def constants():
        for c in range(0, 272, 68):
            ms(V("ZB", c, c + 68), 0.0)
        ms(V("FL", 0, 192, 3), 0.0)
        ms(V("FL", 1, 192, 3), -1.0)
        for t in (1, 2):
            ms(V("D1%d" % t, 1, 96, 3), -TINY)
        for d in range(4):
            ms(blk(d, "KB", (d - me) % 4, 8, 4), 65535.0)
        ts(V("SEGT"), V("J4", 0, 40), 1.5, A.is_gt)
        lin(V("SEGT", 4, 33, 4), V("TR"))
        ts(V("SUF", 0, 31), V("J32", 1, 32), p31, A.is_equal, 1.0 / FAINT - 1, A.mult)
        lin(V("SUF", 0, 31), V("SUF", 0, 31), 1.0, 1.0)
        ms(V("SUF", 31, 32), FAINT)
        kc = [V("KCOL", j, j + 1) for j in range(4)]
        lin(kc[0], kcol, 8.0, p4)
        lin(kc[1], p15, 4.0)
        lin(kc[2], p4, 4.0)
        tb = lambda name: tab(name, buf="TB")
        lin(tb("DUP"), V("DUPF"), 1.0, kc[1])
        lin(tb("PERM"), V("J32", 0, 2), 4.0, kc[0])
        lin(tb("PV"), V("J32", 0, 2), 4.0, p4)
        lin(tb("P8"), V("ZERO", 0, 2), 1.0, p7)
        lin(tb("KX"), V("J32", 0, 2), 4.0, kcol)
        lin(tb("MX"), V("DUPF", 0, 4), 1.0 / 16, p4)
        lin(tb("FX"), V("J32", 0, 2), 16.0, kc[2])
        tc(V("TU"), V("TB"))
        scan(V("POW"), V("FOUR"), V("ZERO", 0, 8), A.mult, A.add, 0.25)
        gata(V("MULT"), V("POW"), tab("MX"))

    def prep_lists():
        for z in (0, 64):
            ts(V("RL", 0, 64, 1, z, z + 64), V("RAW", 0, 64, 1, 0, 64), V("SL", z // 16, z // 16 + 1, 1, 0, 64), A.max,
               V("SL", z // 16 + 1, z // 16 + 2, 1, 0, 64), A.min)
        for h in range(2):
            tr(V("T2", 32 * h, 32 * h + 32), V("RL", h, 64, 2))
        for h in range(2):
            scan(V("SCL", 32 * h, 32 * h + 32), V("SEG4", 0, 32), V("T2", 32 * h, 32 * h + 32), A.mult, A.add)

    def list_of(t, out):
        for h in range(2):
            o = 32 * h + 16 * (t - 1)
            ts(V(out, 4 * h, 4 * h + 4), V("SCL", o + 3, o + 16, 4), V("SL", 2, 3), A.subtract)

    def first_lists():
        for z in (0, 64):
            for h in range(2):
                ts(V("RB", 16 * h, 16 * h + 16, 1, z, z + 64), V("RA", h, 32, 2, 0, 64), V("SL", z // 16, z // 16 + 1, 1, 0, 64), A.max,
                   V("SL", z // 16 + 1, z // 16 + 2, 1, 0, 64), A.min)
        tr(V("RC"), V("RB"))
        for h in range(2):
            scan(V("RD", 16 * h, 16 * h + 16), V("SEG4", 0, 16), V("RC", h, 32, 2), A.mult, A.add)
        for h in range(2):
            ts(V("MSG1", h, 8, 2), V("RD", 16 * h + 3, 16 * h + 16, 4), V("SL", 2, 3), A.subtract)

    def prep_ties():
        ts(V("TI", p1=64), V("RAW", p1=64), 3 * P, A.bitwise_and)
        for z in (0, 64):
            ts(V("TK", p0=z, p1=z + 64), V("TI", p1=64), V("SL", 6 + z // 64, 7 + z // 64, 1, 0, 64), A.is_equal,
               V("SL", 3, 4, 1, 0, 64), A.mult)
        for h in range(2):
            tr(V("SK", 32 * h, 32 * h + 32), V("TK", h, 64, 2))
        scan(V("PK"), V("PKC"), V("SK"), A.mult, A.add)
        tc(V("MSG2"), V("PK", 31, 64, 32))

    def own_columns(t):
        b = bufs(t)
        tc(b("LCN"), b("LS"))
        for k in [me] + others:
            lin(blk(k, "OL%d" % t), blk(me, "LCN%d" % t))
        lin(blk(me, "OG%d" % t), blk(me, "LCN%d" % t), 1.0, float(P * me))
        lin(b("IC", 0, 8), b("LCN"), 1.0, V("GD", 0, 1))
        tt(b("SV"), b("IC", 0, 8), b("OL"), A.subtract)
        tti(b("AO"), b("LCN"), tab("P8"), V("XM"), A.mult)
        tr(blk(me, "TA%d" % t, 0, 128, 4), blk(me, "AO%d" % t))

    def decode_ties():
        ka = V("KB")
        tc(V("KW", 6, 8), V("MSG2"))
        for s in others:
            lin(sub(ka, (s - me) % 4, 8, me, 4), blk(s, "KW", 6, 8))
        tc(V("KW", 0, 6), V("LM2"))
        for j, d in enumerate(others):
            for s in range(4):
                if s != d:
                    (tc if j == 1 else lin)(sub(ka, (s - me) % 4, 8, d, 4), blk(s, "LM2" if j == 1 else "KW", 2 * j, 2 * j + 2))

    def lower(t):
        b = bufs(t)
        tti(b("KI"), V("KB"), tab("KX"), V("MULT", 32 * t - 32, 32 * t), A.mult)
        for name in ("KD", "KE"):
            ts(b(name), b("KI"), 0xC000, A.bitwise_and)
        tti(V("FL", 96 * t - 94, 96 * t, 3), b("KD"), tab("FX"), b("KE"), A.is_lt)

    def own_keys(t):
        ts(V("KK%d" % t), V("KD%d" % t), 2.0 ** -14, A.mult, 1.0, A.add)

    def value_rows(t):
        b = bufs(t)
        own = b("SG", 64, 72)
        gata(b("D1", 0, 96, 3), own, tab("PV"), AF.Abs, scale=STEP)
        gatx(b("D1", 2, 96, 3), own, tab("PV"))
        gata(b("VR"), V("IDT"), b("LU"))

    def thresholds(t):
        b = bufs(t)
        lower(t)
        scan(b("VA"), V("FL", 96 * t - 96, 96 * t), b("D1"), A.mult, A.add)

    def scores_out(t):
        b = bufs(t)
        for h in range(2):
            gatx(b("G", 64 * h, 64 * h + 64), V("S%d" % (t - 1), 0, P), b("LA", 4 * h, 4 * h + 4))
        for j in range(4):
            tr(b("SG", 4 + j, 132, 4), b("G", 32 * j, 32 * j + 32))
        lin(b("U", 0, 8), b("SG", 64, 72))
        return spread(b("SG", 64, 72), lambda s: b("U", 8 + 8 * s, 16 + 8 * s), "v%d" % t, "lv%d" % t, b("U", 8, 32))

    def turn_lists(t):
        b = bufs(t)
        if t == 2:
            for h in range(2):
                tc(V("LB", h, 8, 2), V("LU2", 4 * h, 4 * h + 4))
        gata(b("GI"), V("IDT"), V("LA1" if t == 1 else "LB"))
        for j in range(4):
            tr(b("GT", j, 128, 4), b("GI", 32 * j, 32 * j + 32))
        if t == 1:
            tc(V("LU1"), b("GT", 60, 68))
        else:
            for h in range(2):
                tc(V("LA2", h, 8, 2), b("GT", 60 + 4 * h, 64 + 4 * h))

    def choose_and_send(t):
        b = bufs(t)
        worse = zb(t, 72, 64)
        tti(sub(worse, 0, 32), b("U"), tab("PERM"), b("VA", 2, 96, 3), A.is_gt)
        scan(b("NI"), worse, V("BAR"))
        scan(b("BT", 0, 33), V("SEGT", 0, 33), sub(worse, 0, 33), A.mult, A.max)
        tr(b("RT"), b("NI", 32, 64))
        tt(b("AA"), b("BT", 4, 33, 4), b("NI", 4, 33, 4), A.subtract)
        scan(b("SFX"), b("RT"), V("SUF"), A.add, A.mult)
        ts(b("OF"), b("AA"), b("SFX", 31, 32), A.subtract, 4.0, A.subtract)
        op("v", lambda: g.vector.tensor_copy(ap(b("W")).indirect(ap(b("OF"))), ap(b("VR"))), [b("VR"), b("OF")], [b("W")])
        gat(b("WD", 0, 64), b("W", 0, 256), tab("DUP", 0, 4))
        gata(b("WD", 64, 128), b("W", 0, 256), tab("DUP", 4, 8))
        for i, d in enumerate(turn):
            tr(blk(me, "TW%d" % t, 128 * i, 128 * i + 128), blk(d, "WD%d" % t))
        for k in range(2):
            tt(blk(k, "PF%d" % t, 0, 12), blk(me, "TW%d" % t, 0, 384, 32), blk(me, "TW%d" % t, 16, 384, 32), A.add)
        for h in range(2):
            tc(b("PO", 0, 12, 1, 64 * h, 64 * h + 64), b("PF", 0, 12, 1, 0, 64))
        for lo, hi in ((0, 2), (2, 3)):
            pick(b("SQ", 64 * lo, 64 * hi), b("SS", 64 * lo, 64 * hi), V("QO%d" % (t - 1)), V("QS%d" % (t - 1)), b("PO", 4 * lo, 4 * hi))
        e = topo.engines(core, T.cores[turn[0]])[:16]
        columns("SQ%d" % t, "QW%d" % (t - 1), {0: e[1::2], 1: e[0::2]}, "c%d" % t, 24, "lc%d" % t, 16)
        columns("SQ%d" % t, "QW%d" % (t - 1), {2: e[0::2]}, "c%d" % t, 24, "lc%d" % t, 24)
        columns("SS%d" % t, "QP%d" % (t - 1), {0: e[0::2], 1: e[1::4], 2: e[3::4]}, "s%d" % t, 16, "ls%d" % t, 16)

    def own_list(t):
        b = bufs(t)
        mk = lambda name, *a: blk(me, name + str(t), *a)
        tt(b("M16"), b("U", 0, 16), b("U", 16, 32), A.max)
        tt(b("MM"), b("M16", 0, 8), b("M16", 8, 16), A.max)
        tti(b("EQ"), b("MM"), tab("P8"), b("U"), A.is_equal)
        tti(b("KEY"), b("EQ"), tab("PERM"), b("KK"), A.mult)
        scan(b("KM"), V("SEG4", 0, 32), b("KEY"), A.mult, A.max)
        wb, ic = zb(t, 0, 40), b("IC", 8, 48)
        for i, s in enumerate(others):
            tt(sub(wb, 0, 8, s), mk("KEY", i + 1, 32, 4), mk("KM", 3, 32, 4), A.is_equal)
        scan(ic, wb, V("ZERO", 0, 40))
        tr(b("RC"), sub(ic, 8, 40))
        scan(b("SFC"), b("RC"), V("SUF"), A.add, A.mult)
        lin(b("NW"), sub(wb, 0, 8), -1000.0, 1000.0)
        tt(b("NP"), sub(ic, 0, 8), b("NW"), A.add)
        tti(b("NQ"), b("NP"), tab("P8"), V("XB"), A.add)
        ts(b("KR"), b("NQ"), b("SFC", 31, 32), A.add, CAPP + 0.5, A.is_le)
        o, w, off, s1, s2 = b("SR"), sub(ic, 0, 8), tab("P8"), b("SFC", 31, 32), V("BC", 0, 1)
        op("v", lambda: g.vector.tensor_scalar(ap(o), ap(w).indirect(ap(off)), ap(s1), ap(s2), A.add, A.add), [w, off, s1, s2], [o])
        tt(b("A2"), b("KR"), b("SR"), A.mult)
        for i, s in enumerate(others):
            tr(mk("TA", i + 1, 128, 4), blk(s, "A2%d" % t))
        half = me // 2
        for k in (2 * half, 2 * half + 1):
            scan(blk(k, "XT%d" % t), blk(me, "SEG8"), mk("TA"), A.mult, A.max)
        for h in range(2):
            tc(V("XO%d" % t, p0=64 * h, p1=64 * h + 64), V("XT%d" % t, 7, 128, 8, 64 * half, 64 * half + 64))

    def own_choice(t):
        b = bufs(t)
        mk = lambda name, *a: blk(me, name + str(t), *a)
        bk = zb(t, 40, 32)
        ts(b("KP"), b("NP"), b("SFC", 31, 32), A.add, CAPP + 0.5, A.is_le)
        for i, s in enumerate(others):
            tt(sub(bk, i, 32, me, 4), blk(s, "KP%d" % t), blk(s, "SV%d" % t), A.mult)
        scan(b("XS"), V("SEG4", 0, 32), bk, A.mult, A.add)
        tt(mk("CH"), mk("XS", 3, 32, 4), mk("OG"), A.add)
        dma("sa", T.ch[t - 1:t, :], ap(mk("CH")), [mk("CH")], [])
        if t == 2:
            ts(mk("KQ"), mk("XS", 3, 32, 4), 0.0, A.is_equal, HUGE, A.mult)
            tt(mk("PP"), mk("MM"), mk("KQ"), A.subtract)
            tt(mk("PA"), mk("PP"), mk("U", 0, 8), A.max)
            pr = V("PR2", 0, 256, 1, 0, 1)
            dma("sa", ap(pr), ap(mk("PA")), [mk("PA")], [pr])

    def products(t, i, arrived):
        q, s, n, o = ("QW", "QP", 192, 256) if arrived else ("QO", "QS", 256, 0)
        q, s, z = q + str(t - 1), s + str(t - 1), "Z%d" % t
        a = (V("AQ", 128 * i, 128 * i + 128), V("AP", 128 * i, 128 * i + 128))
        lin(V(z, 448 * i + o, 448 * i + o + n), mm(i if arrived else 4 + i, n, *a, V(q), V(s)), 0.05)

    def new_columns(t):
        b = bufs(t)
        for i in range(4):
            products(t, i, True)
        if t == 1:
            lin(V("S0", P, 448), mm(6, 192, V("UQ"), V("UP"), V("QW0"), V("QP0")))
            gata(V("PB1"), V("S0"), b("XO"))

        def choose(i, lo, hi):
            tti(b("HT", 4 * lo + i, 4 * hi, 4), b("Z", 448 * i, 448 * i + 448), b("XO", lo // 16, hi // 16),
                V("E%d" % t, 4 * lo + i, 4 * hi, 4), A.add)
        wide = WIDE[t - 1]
        for i in range(wide):
            choose(i, 0, P)
        for f in range(2):
            lo, hi = 128 * f, 128 * f + 128
            for i in range(wide, 4):
                choose(i, lo, hi)
            q, s = V("QO%d" % t, lo, hi), V("QS%d" % t, lo, hi)
            qz(q, s, b("HT", 512 * f, 512 * f + 512))
            if t == 2:
                dma("sa", T.oc[:, 4 * lo:4 * hi], ap(q).bitcast(dt.uint8), [q], [])
                lin(V("YB", lo, hi), mm(6 + f, 128, V("WQ"), V("WP"), q, s))
                dma("sa", T.y[:, lo:hi], ap(V("YB", lo, hi)), [V("YB", lo, hi)], [])
            r = mm(4 + f, 128, V("UQ"), V("UP"), q, s)
            if t == 1:
                tt(V("S1", lo, hi), r, V("PB1", lo, hi), A.add)
            else:
                tt(V("S2", lo, hi, 1, 0, 1), r[:2] + (1,) + r[3:], V("PR2", lo, hi, 1, 0, 1), A.add)
        if t == 2:
            for k in range(4):
                sc = V("QS2", 0, P, 1, 32 * k, 32 * k + 4)
                dma("sa", T.osc[4 * k:4 * k + 4, :], ap(sc), [sc], [])
            row = V("S2", 0, 256, 1, 0, 1)
            dma("sa", T.g[:], ap(row), [row], [])

    def quantise_a(i):
        qz(V("AQ", 128 * i, 128 * i + 128), V("AP", 128 * i, 128 * i + 128), V("AT", 512 * i, 512 * i + 512))
        products(1, i, False)

    first_lists()
    prep_lists()
    list_of(1, "LS1")
    lists = spread(V("MSG1"), lambda s: V("LM1", 8 * s, 8 * s + 8), "m1", "lm1", V("LM1"), 0, 2)
    load("sa", V("AT", 0, 1024), T.a[:, 0:1024])
    load("sa", V("AT", 1024, 2048), T.a[:, 1024:2048], [lists])
    for i in range(4):
        lin(V("UT", i, 512, 4), V("ZERO"), 1.0, V("UC", i, i + 1))
    qz(V("UQ"), V("UP"), V("UT"))
    qz(V("QO0"), V("QS0"), V("E0"))
    lin(V("S0", 0, P), mm(0, 256, V("UQ"), V("UP"), V("QO0"), V("QS0")))
    list_of(2, "LS2")
    prep_ties()
    spread(V("MSG2"), lambda s: V("LM2", 2 * s, 2 * s + 2), "m2", "lm2", V("LM2"), 1, 2)
    fill(V("IDT"), 0, 1)
    constants()
    for i in range(2):
        quantise_a(i)
    for d in others + [me]:
        tc(blk(d, "LA1"), blk(me, "MSG1") if d == me else blk(me, "LM1", 8 * others.index(d), 8 * others.index(d) + 8))
    tc(blk(me, "LU2"), blk(me, "LS2"))
    scores = scores_out(1)
    turn_lists(1)
    more_fills()
    load("sa", V("E1"), T.e1[:], [scores])
    own_columns(1)
    for i, d in enumerate(others):
        dma("sa", ap(V("ST2", 2 * i, 2 * i + 2)), ap(blk(d, "LS2")), [blk(d, "LS2")], [V("ST2", 2 * i, 2 * i + 2)], [lists])
    value_rows(1)
    decode_ties()
    thresholds(1)
    own_keys(1)
    choose_and_send(1)
    each("ST2", 2, "LC2", "m3", "lm3")
    for i, d in enumerate(others):
        dma("sa", ap(blk(d, "LU2")), ap(V("LC2", 2 * i, 2 * i + 2)), [V("LC2", 2 * i, 2 * i + 2)], [blk(d, "LU2")])
    for i in range(2, 4):
        quantise_a(i)
    own_list(1)
    turn_lists(2)
    new_columns(1)
    scores = scores_out(2)
    load("sa", V("WT"), T.w[:], [scores])
    load("sa", V("E2"), T.e2[:], [scores])
    value_rows(2)
    thresholds(2)
    own_keys(2)
    for i in range(4):
        products(2, i, False)
    own_columns(2)
    own_choice(1)
    choose_and_send(2)
    qz(V("WQ"), V("WP"), V("WT"))
    own_list(2)
    own_choice(2)
    new_columns(2)
    lay()
    for sem in sorted(total):
        if all(know[q].get(sem, 0) < total[sem] for q in qs):
            wait("s" if sem == "out" else "g", [(sem, total[sem], {})])
